import numpy as np
import ml_dtypes


def mxq(x, axis, fmt="e4m3"):
    dtype, down = {"e4m3": (ml_dtypes.float8_e4m3fn, 7), "e5m2": (ml_dtypes.float8_e5m2, 14)}[fmt]
    v = np.moveaxis(np.asarray(x, np.float32).astype(ml_dtypes.bfloat16).astype(np.float64), axis, -1)
    blocks = v.reshape(v.shape[:-1] + (-1, 32))
    amax = np.abs(blocks).max(-1, keepdims=True)
    byte = np.maximum(np.where(amax > 0, np.frexp(amax)[1] - 1 + 127, 0) - down, 1)
    scale = np.exp2(byte - 127.0)
    codes = (blocks / scale).astype(np.float32).astype(dtype).astype(np.float64)
    return np.moveaxis((codes * scale).reshape(v.shape), -1, axis)


WIDE = False


def mx_kscale(k):
    if not WIDE:
        return np.ones(k)
    levels = np.array([10, -10, 5, -5, 0])
    if k % 512:
        return np.exp2(np.random.permutation(np.resize(levels, k // 32))).repeat(32)
    a = np.empty((k // 512, 16))
    for p in range(k // 512):
        a[p, :8] = np.random.permutation(np.resize(levels, 8))
        for g in range(8):
            far = levels[np.abs(levels - a[p, g]) >= 10]
            a[p, g + 8] = far[np.random.randint(len(far))]
    return np.exp2(a.ravel()).repeat(32)


BF16 = ml_dtypes.bfloat16


def bf(x):
    return np.asarray(x, np.float32).astype(BF16)


def f64(x):
    return np.asarray(x).astype(np.float64)


E2M1 = np.array([0.0, 0.5, 1.0, 1.5, 2.0, 3.0, 4.0, 6.0, -0.0, -0.5, -1.0, -1.5, -2.0, -3.0, -4.0, -6.0])


def pack_weight(w, fmt):
    k, n = w.shape
    w = f64(bf(w)).reshape(k // 32, 32, n)
    amax = np.abs(w).max(1)
    if fmt == "e4m3":
        byte = np.frexp(amax)[1] - 1 + 127 - 7
    else:
        mant, ex = np.frexp(amax / 6.0)
        byte = np.where(mant > 0.5, ex, ex - 1) + 127
    byte = np.clip(np.where(amax > 0, byte, 1), 1, 254)
    scaled = (w * np.exp2(127.0 - byte)[:, None, :]).reshape(k, n).astype(np.float32)
    by_word = np.ascontiguousarray(scaled.reshape(k // 512, 128, 4, n).transpose(0, 1, 3, 2))
    if fmt == "e4m3":
        words = by_word.astype(ml_dtypes.float8_e4m3fn).view(np.uint8)
    else:
        c = by_word.astype(ml_dtypes.float4_e2m1fn).view(np.uint8) & 0xF
        words = c[..., 0::2] | (c[..., 1::2] << 4)
    return np.ascontiguousarray(words), np.ascontiguousarray(byte.astype(np.uint8).reshape(k // 512, 16, n))


def unpack_weight(words, scales, fmt):
    g, p, n, _ = words.shape
    if fmt == "e4m3":
        vals = np.ascontiguousarray(words).view(ml_dtypes.float8_e4m3fn).astype(np.float64)
    else:
        nib = np.empty((g, p, n, 4), np.uint8)
        nib[..., 0::2] = words & 0xF
        nib[..., 1::2] = words >> 4
        vals = E2M1[nib]
    vals = vals * np.repeat(np.exp2(scales.astype(np.float64) - 127.0), 8, axis=1)[..., None]
    return vals.transpose(0, 1, 3, 2).reshape(g * 512, n)
def pack4(w):
    words, scales = pack_weight(w, "e2m1")
    return words.reshape(words.shape[0], 128, -1), scales


def unpack4(words, scales):
    return unpack_weight(words.reshape(words.shape[0], 128, -1, 2), scales, "e2m1")


T, F, D, E = 2048, 1024, 1024, 512


def setup_inputs():
    s = mx_kscale(F)
    r = mx_kscale(D)
    t = mx_kscale(T)
    a = np.random.standard_normal((F, T)) * s[:, None] * t
    w = np.random.standard_normal((F, D)) / np.sqrt(F) / T ** 0.25 / s[:, None]
    a_words, a_scales = pack4(a)
    w_words, w_scales = pack4(w)
    return {"a_words": a_words, "a_scales": a_scales,
            "w_words": w_words, "w_scales": w_scales,
            "grad": bf(np.random.standard_normal((T, D)) * r),
            "values": bf(np.random.standard_normal((D, E)) / np.sqrt(D) / r[:, None]),
            "prob": bf(np.exp(0.5 * np.random.standard_normal((T, E))) / T ** 0.25 / t[:, None]),
            "balance": bf(0.5 * np.random.standard_normal(E)),
            "base": bf(0.5 * np.random.standard_normal(T))}


def reference(a_words, a_scales, w_words, w_scales, grad, values, prob, balance, base):
    x = unpack4(a_words, a_scales).T @ unpack4(w_words, w_scales)
    u = mxq(f64(grad), 1, "e4m3") @ mxq(f64(values), 0, "e4m3")
    dl = f64(prob) * (u + f64(balance) - f64(base)[:, None])
    return mxq(x, 0, "e4m3").T @ mxq(dl, 0, "e4m3")

@@ -1,0 +1,308 @@
+from contextlib import ExitStack
+
+import concourse.mybir as mybir
+from concourse.masks import make_identity
+
+T, F, D, E = 2048, 1024, 1024, 512
+FLOPS = 2 * (T * F * D + T * D * E + T * D * E)
+
+F32 = mybir.dt.float32
+BF16 = mybir.dt.bfloat16
+I32 = mybir.dt.int32
+U32 = mybir.dt.uint32
+U8 = mybir.dt.uint8
+FP8X4 = mybir.dt.float8_e4m3fn_x4
+FP4X4 = mybir.dt.float4_e2m1fn_x4
+ALU = mybir.AluOpType
+
+P = 128
+PACK = 4
+GROUP = P * PACK
+GROUPS = T // GROUP
+PASSES = 2
+BANK = 512
+BANKS = 8
+ALIGN = 64
+
+
+def tile_router_weight_gradient_s12_kernel(
+    tc, a_words, a_scales, w_words, w_scales, grad, values, prob, balance, base, out
+):
+    nc = tc.nc
+    with ExitStack() as ctx:
+        sb = ctx.enter_context(tc.tile_pool(name="sb", bufs=1))
+        psum = ctx.enter_context(tc.psum_pool(name="psum", bufs=1))
+        ctx.enter_context(tc.manual_schedule())
+
+        def keep(name, shape, dtype):
+            return sb.tile(shape, dtype, name=name, align_bytes=ALIGN)
+
+        taken = []
+
+        def next_bank():
+            n = len(taken)
+            bank = psum.tile([P, BANK], F32, name="bank%d" % n, tag="bank%d" % (n % BANKS))
+            taken.append(bank)
+            return bank
+
+        ident = keep("ident", [P, P], F32)
+        bal_col = keep("bal_col", [P, PACK], BF16)
+        bal_wide = keep("bal_wide", [P, PACK, P], F32)
+        bal_row = keep("bal_row", [P, E], F32)
+        base_sb = keep("base_sb", [P, GROUPS, 16], BF16)
+
+        a_raw = [keep("a_raw%d" % g, [P, PASSES, 256], I32) for g in range(GROUPS)]
+        a_codes = [keep("a_codes%d" % g, [P, PACK, PASSES, 256], U8) for g in range(GROUPS)]
+        a_sc_first = keep("a_sc_first", [P, PASSES, 128], I32)
+        a_sc_rest = keep("a_sc_rest", [P, PASSES, 384], I32)
+        a_planes = [keep("a_plane%d" % g, [P, PACK, PASSES, P], U8) for g in range(GROUPS)]
+        w_codes = [keep("w_codes%d" % n, [P, PASSES, 1024], U8) for n in range(2)]
+        w_plane = keep("w_plane", [P, PASSES, D], U8)
+
+        g_raw = [keep("g_raw%d" % g, [P, PACK, D], BF16) for g in range(GROUPS)]
+        g_t = [[keep("g_t%d_%d" % (g, h), [P, GROUP * PACK], BF16) for h in range(PASSES)] for g in range(2)] * 2
+        g_codes = [[keep("g_codes%d_%d" % (g, h), [P, GROUP], U32) for h in range(PASSES)] for g in range(2)] * 2
+        g_planes = [[keep("g_plane%d_%d" % (g, h), [P, GROUP], U8) for h in range(PASSES)] for g in range(2)] * 2
+        v_raw = [keep("v_raw%d" % h, [P, PACK, E], BF16) for h in range(PASSES)]
+        v_t = [keep("v_t%d" % h, [P, E * PACK], BF16) for h in range(PASSES)]
+        v_codes = [keep("v_codes%d" % h, [P, E], U32) for h in range(PASSES)]
+        v_planes = [keep("v_plane%d" % h, [P, E], U8) for h in range(PASSES)]
+        p_sb = [keep("p_sb%d" % g, [P, PACK, E], BF16) for g in range(GROUPS)]
+        shifted = [keep("shifted%d" % n, [P, E * PACK], F32) for n in range(2)]
+        l_bf = [keep("l_bf%d" % n, [P, E * PACK], BF16) for n in range(2)]
+        l_codes = [keep("l_codes%d" % g, [P, E], U32) for g in range(GROUPS)]
+        l_planes = [keep("l_plane%d" % g, [P, E], U8) for g in range(GROUPS)]
+        x_bf = [[keep("x_bf%d_%d" % (g, n), [P, 512 * PACK], BF16) for n in range(2)] for g in range(2)] * 2
+        x_codes = [[keep("x_codes%d_%d" % (g, n), [P, 512], U32) for n in range(2)] for g in range(GROUPS)]
+        x_planes = [[keep("x_plane%d_%d" % (g, n), [P, 512], U8) for n in range(2)] for g in range(GROUPS)]
+        result = [keep("result%d" % j, [P, E], F32) for j in range(D // P)]
+
+        def load_a(g):
+            src = a_words.rearrange("h p n -> p h n")[:, :, 1024 * g : 1024 * (g + 1)]
+            nc.sync.dma_start(out=a_raw[g][:], in_=src.bitcast(I32))
+
+        def load_scales(dst, scales, lo, hi):
+            for q in range(4):
+                src = scales.rearrange("h r n -> r h n")[4 * q : 4 * q + 4, :, lo:hi]
+                nc.sync.dma_start(out=dst[32 * q : 32 * q + 4], in_=src.bitcast(I32))
+
+        def load_w(n):
+            src = w_words.rearrange("h p n -> p h n")[:, :, 1024 * n : 1024 * (n + 1)]
+            nc.sync.dma_start(out=w_codes[n][:].bitcast(I32), in_=src.bitcast(I32))
+
+        def load_grad(g):
+            rows = grad[GROUP * g : GROUP * (g + 1), :].rearrange("(m s) d -> m s d", s=PACK)
+            for pair in range(2):
+                nc.sync.dma_start(out=g_raw[g][:, 2 * pair : 2 * pair + 2, :], in_=rows[:, 2 * pair : 2 * pair + 2, :])
+
+        def load_values(h):
+            rows = values[GROUP * h : GROUP * (h + 1), :].rearrange("(p j) e -> p j e", j=PACK)
+            nc.sync.dma_start(out=v_raw[h][:], in_=rows)
+
+        def load_prob(g):
+            rows = prob[GROUP * g : GROUP * (g + 1), :].rearrange("(c t s) e -> s c t e", t=PACK, s=PACK)
+            for s in range(PACK):
+                nc.sync.dma_start(out=p_sb[g][s:P:PACK, :, :], in_=rows[s])
+
+        def load_base():
+            rows = base.rearrange("(g c w) -> c g w", g=GROUPS, w=16)
+            for s in range(PACK):
+                nc.sync.dma_start(out=base_sb[s:P:PACK, :, 0:13], in_=rows[:, :, s : s + 13])
+
+        def order_a(g):
+            nc.vector.tensor_copy(
+                out=a_codes[g][:].bitcast(I32).rearrange("p t h (c w) -> p t (h c) w", w=2),
+                in_=a_raw[g][:].rearrange("p h (c t w) -> p t (h c) w", t=PACK, w=2),
+            )
+            if g == 0:
+                staged = a_sc_first[:]
+            else:
+                staged = a_sc_rest[:, :, 128 * (g - 1) : 128 * g]
+            nc.vector.tensor_copy(
+                out=a_planes[g][:].bitcast(I32),
+                in_=staged.rearrange("p h (c t) -> p t h c", t=PACK),
+            )
+
+        def quantize(codes, plane, src):
+            nc.vector.quantize_mx(out=codes[:].bitcast(FP8X4), scales=plane[:], in_=src[:])
+
+        def spread_balance():
+            nc.scalar.copy(out=bal_wide[:], in_=bal_col[:].unsqueeze(2).to_broadcast([P, PACK, P]))
+            bank = next_bank()
+            for j in range(PACK):
+                nc.tensor.transpose(bank[:, P * j : P * (j + 1)], bal_wide[:, j, :], ident[:])
+            nc.scalar.copy(
+                out=bal_row[:].rearrange("p (n j) -> p n j", j=PACK),
+                in_=bank[:].rearrange("p (j n) -> p n j", j=PACK),
+            )
+
+        def x_half(g, n):
+            for jj in range(4):
+                j = 4 * n + jj
+                bank = next_bank()
+                for t in range(PACK):
+                    for h in range(PASSES):
+                        nc.tensor.matmul_mx(
+                            out=bank[:, P * t : P * (t + 1)],
+                            lhsT=a_codes[g][:, t, h, :].bitcast(FP4X4),
+                            lhsT_scale=a_planes[g][:, t, h, :],
+                            rhs=w_codes[n][:, h, 256 * jj : 256 * (jj + 1)].bitcast(FP4X4),
+                            rhs_scale=w_plane[:, h, P * j : P * (j + 1)],
+                            start=(h == 0),
+                            stop=(h == PASSES - 1),
+                        )
+                nc.scalar.copy(
+                    out=x_bf[g][n][:, BANK * jj : BANK * (jj + 1)].rearrange("p (d t) -> p d t", t=PACK),
+                    in_=bank[:].rearrange("p (t d) -> p d t", t=PACK),
+                )
+
+        def turn_grad(g):
+            for h in range(PASSES):
+                for pair in range(2):
+                    bank = next_bank()
+                    for ss in range(2):
+                        words = g_raw[g][:, 2 * pair + ss, :].bitcast(F32)
+                        for u in range(2):
+                            q = 2 * ss + u
+                            nc.tensor.transpose(
+                                bank[:, P * q : P * (q + 1)], words[:, 256 * h + u : 256 * (h + 1) : 2], ident[:]
+                            )
+                    dst = g_t[g][h][:].bitcast(F32).rearrange("p (t c w) -> p t c w", t=PACK, w=8)
+                    nc.scalar.copy(
+                        out=dst[:, :, :, 4 * pair : 4 * pair + 4],
+                        in_=bank[:].rearrange("p (q c t) -> p t c q", q=4, t=PACK),
+                    )
+
+        def interleave_values(h):
+            nc.vector.tensor_copy(
+                out=v_t[h][:].rearrange("p (c i t) -> p c t i", i=4, t=PACK),
+                in_=v_raw[h][:].rearrange("p t (c i) -> p c t i", i=4),
+            )
+
+        def utilities(g):
+            dst = shifted[g % 2][:].rearrange("p (c t i) -> p c t i", t=PACK, i=4)
+            for t in range(PACK):
+                bank = next_bank()
+                for h in range(PASSES):
+                    nc.tensor.matmul_mx(
+                        out=bank[:],
+                        lhsT=g_codes[g][h][:, P * t : P * (t + 1)].bitcast(FP8X4),
+                        lhsT_scale=g_planes[g][h][:, P * t : P * (t + 1)],
+                        rhs=v_codes[h][:].bitcast(FP8X4),
+                        rhs_scale=v_planes[h][:],
+                        start=(h == 0),
+                        stop=(h == PASSES - 1),
+                    )
+                nc.vector.scalar_tensor_tensor(
+                    out=dst[:, :, t, :],
+                    in0=bank[:].rearrange("p (c i) -> p c i", i=4),
+                    scalar=base_sb[:, g, 4 * t : 4 * t + 1],
+                    in1=bal_row[:].rearrange("p (c i) -> p c i", i=4),
+                    op0=ALU.subtract,
+                    op1=ALU.add,
+                )
+
+        def weigh(g, n):
+            cs = slice(64 * n, 64 * (n + 1))
+            nc.vector.tensor_tensor(
+                out=l_bf[g % 2][:].rearrange("p (c i t) -> p c t i", i=4, t=PACK)[:, cs],
+                in0=shifted[g % 2][:].rearrange("p (c t i) -> p c t i", t=PACK, i=4)[:, cs],
+                in1=p_sb[g][:].rearrange("p t (c i) -> p c t i", i=4)[:, cs],
+                op=ALU.mult,
+            )
+
+        def quantize_x(g, n):
+            quantize(x_codes[g][n], x_planes[g][n], x_bf[g][n])
+
+        def quantize_grad(g, h):
+            quantize(g_codes[g][h], g_planes[g][h], g_t[g][h])
+
+        def quantize_l(g):
+            quantize(l_codes[g], l_planes[g], l_bf[g % 2])
+
+        def final(j, lo, hi, on_scalar):
+            bank = next_bank()
+            n, cols = j // 4, slice(P * (j % 4), P * (j % 4 + 1))
+            for g in range(GROUPS):
+                nc.tensor.matmul_mx(
+                    out=bank[:, 0 : hi - lo],
+                    lhsT=x_codes[g][n][:, cols].bitcast(FP8X4),
+                    lhsT_scale=x_planes[g][n][:, cols],
+                    rhs=l_codes[g][:, lo:hi].bitcast(FP8X4),
+                    rhs_scale=l_planes[g][:, lo:hi],
+                    start=(g == 0),
+                    stop=(g == GROUPS - 1),
+                )
+            if on_scalar:
+                nc.scalar.copy(out=result[j][:, lo:hi], in_=bank[:, 0 : hi - lo])
+            else:
+                nc.vector.tensor_copy(out=result[j][:, lo:hi], in_=bank[:, 0 : hi - lo])
+            nc.sync.dma_start(out=out[P * j : P * (j + 1), lo:hi], in_=result[j][:, lo:hi])
+
+        nc.gpsimd.dma_start(out=bal_col[:], in_=balance.rearrange("(p j) -> p j", j=PACK))
+        make_identity(nc, ident[:])
+        nc.vector.memset(a_sc_first[:], 0)
+        nc.vector.memset(w_plane[:].bitcast(I32), 0)
+        nc.vector.memset(a_sc_rest[:], 0)
+
+        load_a(0)
+        load_w(0)
+        load_scales(a_sc_first, a_scales, 0, GROUP)
+        load_scales(w_plane[:].bitcast(I32), w_scales, 0, D)
+        load_grad(0)
+        load_w(1)
+        load_values(0)
+        load_values(1)
+        load_scales(a_sc_rest, a_scales, GROUP, T)
+        load_base()
+        load_a(1)
+        load_prob(0)
+        for g in range(1, GROUPS):
+            load_grad(g)
+            if g + 1 < GROUPS:
+                load_a(g + 1)
+            load_prob(g)
+
+        spread_balance()
+        order_a(0)
+        x_half(0, 0)
+        turn_grad(0)
+        x_half(0, 1)
+        interleave_values(0)
+        interleave_values(1)
+        quantize(v_codes[0], v_planes[0], v_t[0])
+        quantize_grad(0, 0)
+        quantize(v_codes[1], v_planes[1], v_t[1])
+        quantize_grad(0, 1)
+        order_a(1)
+        quantize_x(0, 0)
+
+        halves = [(g, n) for g in range(GROUPS) for n in range(2)]
+        for g in range(GROUPS - 1):
+            utilities(g)
+            quantize_x(*halves[g + 1])
+            turn_grad(g + 1)
+            weigh(g, 0)
+            quantize_grad(g + 1, 0)
+            weigh(g, 1)
+            quantize_grad(g + 1, 1)
+            if g + 2 < GROUPS:
+                order_a(g + 2)
+            quantize_l(g)
+            x_half(*halves[g + 2])
+        last = GROUPS - 1
+        utilities(last)
+        quantize_x(*halves[4])
+        x_half(*halves[5])
+        weigh(last, 0)
+        weigh(last, 1)
+        quantize_x(*halves[5])
+        quantize_l(last)
+        x_half(*halves[6])
+        quantize_x(*halves[6])
+        x_half(*halves[7])
+        quantize_x(*halves[7])
+        for j in range(D // P - 1):
+            final(j, 0, E, j % 2 == 0)
+        final(D // P - 1, 0, E // 2, False)
+        final(D // P - 1, E // 2, E, True)

@@ -136,9 +136,10 @@ def tile_router_weight_gradient_s12_kernel(
                 in_=bank[:].rearrange("p (j n) -> p n j", j=PACK),
             )
 
-        def x_half(g, n):
-            for jj in range(4):
-                j = 4 * n + jj
+        def x_tiles(first, count):
+            for unit in range(first, first + count):
+                g, j = divmod(unit, 8)
+                n, jj = divmod(j, 4)
                 bank = next_bank()
                 for t in range(PACK):
                     for h in range(PASSES):
@@ -220,10 +221,9 @@ def tile_router_weight_gradient_s12_kernel(
         def quantize_l(g):
             quantize(l_codes[g], l_planes[g], l_bf[g % 2])
 
-        def final(j, lo, hi, on_scalar):
-            bank = next_bank()
+        def final_passes(bank, j, lo, hi, groups):
             n, cols = j // 4, slice(P * (j % 4), P * (j % 4 + 1))
-            for g in range(GROUPS):
+            for g in groups:
                 nc.tensor.matmul_mx(
                     out=bank[:, 0 : hi - lo],
                     lhsT=x_codes[g][n][:, cols].bitcast(FP8X4),
@@ -233,11 +233,24 @@ def tile_router_weight_gradient_s12_kernel(
                     start=(g == 0),
                     stop=(g == GROUPS - 1),
                 )
+
+        def store(bank, j, lo, hi, on_scalar):
             if on_scalar:
                 nc.scalar.copy(out=result[j][:, lo:hi], in_=bank[:, 0 : hi - lo])
             else:
                 nc.vector.tensor_copy(out=result[j][:, lo:hi], in_=bank[:, 0 : hi - lo])
             nc.sync.dma_start(out=out[P * j : P * (j + 1), lo:hi], in_=result[j][:, lo:hi])
+
+        def final(j, lo, hi, on_scalar):
+            bank = next_bank()
+            final_passes(bank, j, lo, hi, range(GROUPS))
+            store(bank, j, lo, hi, on_scalar)
+
+        def warm_up():
+            for n in range(2):
+                bank = next_bank()
+                for q in range(4):
+                    nc.tensor.transpose(bank[:, P * q : P * (q + 1)], ident[:], ident[:])
 
         nc.gpsimd.dma_start(out=bal_col[:], in_=balance.rearrange("(p j) -> p j", j=PACK))
         make_identity(nc, ident[:])
@@ -249,13 +262,13 @@ def tile_router_weight_gradient_s12_kernel(
         load_w(0)
         load_scales(a_sc_first, a_scales, 0, GROUP)
         load_scales(w_plane[:].bitcast(I32), w_scales, 0, D)
+        load_values(0)
         load_grad(0)
         load_w(1)
-        load_values(0)
         load_values(1)
         load_scales(a_sc_rest, a_scales, GROUP, T)
-        load_base()
         load_a(1)
+        load_base()
         load_prob(0)
         for g in range(1, GROUPS):
             load_grad(g)
@@ -263,46 +276,51 @@ def tile_router_weight_gradient_s12_kernel(
                 load_a(g + 1)
             load_prob(g)
 
+        warm_up()
         spread_balance()
         order_a(0)
-        x_half(0, 0)
-        turn_grad(0)
-        x_half(0, 1)
+        x_tiles(0, 4)
         interleave_values(0)
-        interleave_values(1)
+        turn_grad(0)
         quantize(v_codes[0], v_planes[0], v_t[0])
+        interleave_values(1)
+        x_tiles(4, 4)
         quantize_grad(0, 0)
         quantize(v_codes[1], v_planes[1], v_t[1])
         quantize_grad(0, 1)
         order_a(1)
         quantize_x(0, 0)
 
-        halves = [(g, n) for g in range(GROUPS) for n in range(2)]
         for g in range(GROUPS - 1):
             utilities(g)
-            quantize_x(*halves[g + 1])
+            if g + 2 < GROUPS:
+                order_a(g + 2)
+            else:
+                quantize_x(1, 1)
             turn_grad(g + 1)
             weigh(g, 0)
             quantize_grad(g + 1, 0)
-            weigh(g, 1)
             quantize_grad(g + 1, 1)
-            if g + 2 < GROUPS:
-                order_a(g + 2)
+            weigh(g, 1)
+            quantize_x(*[(0, 1), (1, 0), (2, 0)][g])
             quantize_l(g)
-            x_half(*halves[g + 2])
+            x_tiles(8 + 6 * g, 6)
         last = GROUPS - 1
         utilities(last)
-        quantize_x(*halves[4])
-        x_half(*halves[5])
+        quantize_x(2, 1)
+        x_tiles(26, 6)
         weigh(last, 0)
         weigh(last, 1)
-        quantize_x(*halves[5])
+        quantize_x(3, 0)
         quantize_l(last)
-        x_half(*halves[6])
-        quantize_x(*halves[6])
-        x_half(*halves[7])
-        quantize_x(*halves[7])
-        for j in range(D // P - 1):
+        quantize_x(3, 1)
+        early = [next_bank() for j in range(4)]
+        for j in range(4):
+            final_passes(early[j], j, 0, E, range(last))
+        for j in range(4):
+            final_passes(early[j], j, 0, E, [last])
+            store(early[j], j, 0, E, j % 2 == 0)
+        for j in range(4, D // P - 1):
             final(j, 0, E, j % 2 == 0)
         final(D // P - 1, 0, E // 2, False)
         final(D // P - 1, E // 2, E, True)

@@ -51,7 +51,7 @@ def tile_router_weight_gradient_s12_kernel(
         bal_row = keep("bal_row", [P, E], F32)
         base_sb = keep("base_sb", [P, GROUPS, 16], BF16)
 
-        a_raw = [keep("a_raw%d" % g, [P, PASSES, 256], I32) for g in range(GROUPS)]
+        a_raw = [keep("a_raw%d" % g, [P, PASSES, 256], I32) for g in range(2)] * 2
         a_codes = [keep("a_codes%d" % g, [P, PACK, PASSES, 256], U8) for g in range(GROUPS)]
         a_sc_first = keep("a_sc_first", [P, PASSES, 128], I32)
         a_sc_rest = keep("a_sc_rest", [P, PASSES, 384], I32)
@@ -59,7 +59,8 @@ def tile_router_weight_gradient_s12_kernel(
         w_codes = [keep("w_codes%d" % n, [P, PASSES, 1024], U8) for n in range(2)]
         w_plane = keep("w_plane", [P, PASSES, D], U8)
 
-        g_raw = [keep("g_raw%d" % g, [P, PACK, D], BF16) for g in range(GROUPS)]
+        g_raw = [keep("g_raw%d" % g, [P, PACK, D], BF16) for g in range(2)] * 2
+        g_split = [[keep("g_split%d_%d" % (h, pair), [P, 4, P], F32) for pair in range(2)] for h in range(PASSES)]
         g_t = [[keep("g_t%d_%d" % (g, h), [P, GROUP * PACK], BF16) for h in range(PASSES)] for g in range(2)] * 2
         g_codes = [[keep("g_codes%d_%d" % (g, h), [P, GROUP], U32) for h in range(PASSES)] for g in range(2)] * 2
         g_planes = [[keep("g_plane%d_%d" % (g, h), [P, GROUP], U8) for h in range(PASSES)] for g in range(2)] * 2
@@ -72,7 +73,7 @@ def tile_router_weight_gradient_s12_kernel(
         l_bf = [keep("l_bf%d" % n, [P, E * PACK], BF16) for n in range(2)]
         l_codes = [keep("l_codes%d" % g, [P, E], U32) for g in range(GROUPS)]
         l_planes = [keep("l_plane%d" % g, [P, E], U8) for g in range(GROUPS)]
-        x_bf = [[keep("x_bf%d_%d" % (g, n), [P, 512 * PACK], BF16) for n in range(2)] for g in range(2)] * 2
+        x_bf = [[keep("x_bf%d_%d" % (g, n), [P, 512 * PACK], BF16) for n in range(2)] for g in range(GROUPS)]
         x_codes = [[keep("x_codes%d_%d" % (g, n), [P, 512], U32) for n in range(2)] for g in range(GROUPS)]
         x_planes = [[keep("x_plane%d_%d" % (g, n), [P, 512], U8) for n in range(2)] for g in range(GROUPS)]
         result = [keep("result%d" % j, [P, E], F32) for j in range(D // P)]
@@ -157,17 +158,21 @@ def tile_router_weight_gradient_s12_kernel(
                     in_=bank[:].rearrange("p (t d) -> p d t", t=PACK),
                 )
 
+        def split_grad(g, copy):
+            for h in range(PASSES):
+                for pair in range(2):
+                    words = g_raw[g][:, 2 * pair : 2 * pair + 2, GROUP * h : GROUP * (h + 1)].bitcast(F32)
+                    copy(
+                        out=g_split[h][pair][:].rearrange("p (s u) w -> p s u w", u=2),
+                        in_=words.rearrange("p s (w u) -> p s u w", u=2),
+                    )
+
         def turn_grad(g):
             for h in range(PASSES):
                 for pair in range(2):
                     bank = next_bank()
-                    for ss in range(2):
-                        words = g_raw[g][:, 2 * pair + ss, :].bitcast(F32)
-                        for u in range(2):
-                            q = 2 * ss + u
-                            nc.tensor.transpose(
-                                bank[:, P * q : P * (q + 1)], words[:, 256 * h + u : 256 * (h + 1) : 2], ident[:]
-                            )
+                    for q in range(4):
+                        nc.tensor.transpose(bank[:, P * q : P * (q + 1)], g_split[h][pair][:, q, :], ident[:])
                     dst = g_t[g][h][:].bitcast(F32).rearrange("p (t c w) -> p t c w", t=PACK, w=8)
                     nc.scalar.copy(
                         out=dst[:, :, :, 4 * pair : 4 * pair + 4],
@@ -264,23 +269,20 @@ def tile_router_weight_gradient_s12_kernel(
         load_scales(w_plane[:].bitcast(I32), w_scales, 0, D)
         load_values(0)
         load_grad(0)
-        load_w(1)
         load_values(1)
+        load_w(1)
+        load_grad(1)
+        load_base()
         load_scales(a_sc_rest, a_scales, GROUP, T)
         load_a(1)
-        load_base()
         load_prob(0)
-        for g in range(1, GROUPS):
-            load_grad(g)
-            if g + 1 < GROUPS:
-                load_a(g + 1)
-            load_prob(g)
 
         warm_up()
         spread_balance()
         order_a(0)
         x_tiles(0, 4)
         interleave_values(0)
+        split_grad(0, nc.vector.tensor_copy)
         turn_grad(0)
         quantize(v_codes[0], v_planes[0], v_t[0])
         interleave_values(1)
@@ -288,15 +290,16 @@ def tile_router_weight_gradient_s12_kernel(
         quantize_grad(0, 0)
         quantize(v_codes[1], v_planes[1], v_t[1])
         quantize_grad(0, 1)
-        order_a(1)
         quantize_x(0, 0)
 
         for g in range(GROUPS - 1):
-            utilities(g)
+            split_grad(g + 1, nc.scalar.copy)
             if g + 2 < GROUPS:
-                order_a(g + 2)
-            else:
-                quantize_x(1, 1)
+                load_a(g + 2)
+                load_grad(g + 2)
+            load_prob(g + 1)
+            utilities(g)
+            order_a(g + 1)
             turn_grad(g + 1)
             weigh(g, 0)
             quantize_grad(g + 1, 0)
@@ -307,13 +310,13 @@ def tile_router_weight_gradient_s12_kernel(
             x_tiles(8 + 6 * g, 6)
         last = GROUPS - 1
         utilities(last)
-        quantize_x(2, 1)
         x_tiles(26, 6)
         weigh(last, 0)
         weigh(last, 1)
         quantize_x(3, 0)
         quantize_l(last)
-        quantize_x(3, 1)
+        for g in range(1, GROUPS):
+            quantize_x(g, 1)
         early = [next_bank() for j in range(4)]
         for j in range(4):
             final_passes(early[j], j, 0, E, range(last))

@@ -23,6 +23,8 @@ PASSES = 2
 BANK = 512
 BANKS = 8
 ALIGN = 64
+WARM_N = 256
+WARM_PASSES = 7
 
 
 def tile_router_weight_gradient_s12_kernel(
@@ -49,6 +51,8 @@ def tile_router_weight_gradient_s12_kernel(
         bal_col = keep("bal_col", [P, PACK], BF16)
         bal_wide = keep("bal_wide", [P, PACK, P], F32)
         bal_row = keep("bal_row", [P, E], F32)
+        warm_codes = keep("warm_codes", [P, WARM_N], U32)
+        warm_plane = keep("warm_plane", [P, WARM_N], U8)
         base_sb = keep("base_sb", [P, GROUPS, 16], BF16)
 
         a_raw = [keep("a_raw%d" % g, [P, PASSES, 256], I32) for g in range(2)] * 2
@@ -82,8 +86,8 @@ def tile_router_weight_gradient_s12_kernel(
             src = a_words.rearrange("h p n -> p h n")[:, :, 1024 * g : 1024 * (g + 1)]
             nc.sync.dma_start(out=a_raw[g][:], in_=src.bitcast(I32))
 
-        def load_scales(dst, scales, lo, hi):
-            for q in range(4):
+        def load_scales(dst, scales, lo, hi, quadrants=range(4)):
+            for q in quadrants:
                 src = scales.rearrange("h r n -> r h n")[4 * q : 4 * q + 4, :, lo:hi]
                 nc.sync.dma_start(out=dst[32 * q : 32 * q + 4], in_=src.bitcast(I32))
 
@@ -159,8 +163,8 @@ def tile_router_weight_gradient_s12_kernel(
                 )
 
         def split_grad(g, copy):
-            for h in range(PASSES):
-                for pair in range(2):
+            for pair in range(2):
+                for h in range(PASSES):
                     words = g_raw[g][:, 2 * pair : 2 * pair + 2, GROUP * h : GROUP * (h + 1)].bitcast(F32)
                     copy(
                         out=g_split[h][pair][:].rearrange("p (s u) w -> p s u w", u=2),
@@ -168,8 +172,8 @@ def tile_router_weight_gradient_s12_kernel(
                     )
 
         def turn_grad(g):
-            for h in range(PASSES):
-                for pair in range(2):
+            for pair in range(2):
+                for h in range(PASSES):
                     bank = next_bank()
                     for q in range(4):
                         nc.tensor.transpose(bank[:, P * q : P * (q + 1)], g_split[h][pair][:, q, :], ident[:])
@@ -252,45 +256,57 @@ def tile_router_weight_gradient_s12_kernel(
             store(bank, j, lo, hi, on_scalar)
 
         def warm_up():
-            for n in range(2):
-                bank = next_bank()
-                for q in range(4):
-                    nc.tensor.transpose(bank[:, P * q : P * (q + 1)], ident[:], ident[:])
+            bank = next_bank()
+            for n in range(WARM_PASSES):
+                nc.tensor.matmul_mx(
+                    out=bank[:, 0:WARM_N],
+                    lhsT=warm_codes[:, 0:P].bitcast(FP8X4),
+                    lhsT_scale=warm_plane[:, 0:P],
+                    rhs=warm_codes[:].bitcast(FP8X4),
+                    rhs_scale=warm_plane[:],
+                    start=(n == 0),
+                    stop=(n == WARM_PASSES - 1),
+                )
 
         nc.gpsimd.dma_start(out=bal_col[:], in_=balance.rearrange("(p j) -> p j", j=PACK))
         make_identity(nc, ident[:])
         nc.vector.memset(a_sc_first[:], 0)
-        nc.vector.memset(w_plane[:].bitcast(I32), 0)
         nc.vector.memset(a_sc_rest[:], 0)
+        nc.vector.memset(w_plane[:].bitcast(I32), 0)
+        zeros = a_sc_rest[:].rearrange("p h n -> p (h n)").bitcast(BF16)[:, 0 : WARM_N * PACK]
+        nc.vector.quantize_mx(out=warm_codes[:].bitcast(FP8X4), scales=warm_plane[:], in_=zeros)
 
         load_a(0)
+        load_scales(a_sc_first, a_scales, 0, GROUP, (0, 2, 1, 3))
         load_w(0)
-        load_scales(a_sc_first, a_scales, 0, GROUP)
-        load_scales(w_plane[:].bitcast(I32), w_scales, 0, D)
-        load_values(0)
+        load_scales(w_plane[:].bitcast(I32), w_scales, 0, D, (0, 2, 1, 3))
         load_grad(0)
-        load_values(1)
         load_w(1)
+        load_values(0)
+        load_a(1)
+        load_scales(a_sc_rest, a_scales, GROUP, T, (0, 2, 1, 3))
+        load_values(1)
         load_grad(1)
         load_base()
-        load_scales(a_sc_rest, a_scales, GROUP, T)
-        load_a(1)
         load_prob(0)
 
         warm_up()
         spread_balance()
         order_a(0)
         x_tiles(0, 4)
-        interleave_values(0)
         split_grad(0, nc.vector.tensor_copy)
         turn_grad(0)
+        quantize_x(0, 0)
+        interleave_values(0)
+        x_tiles(4, 4)
+        order_a(1)
+        quantize_grad(0, 0)
         quantize(v_codes[0], v_planes[0], v_t[0])
         interleave_values(1)
-        x_tiles(4, 4)
-        quantize_grad(0, 0)
-        quantize(v_codes[1], v_planes[1], v_t[1])
         quantize_grad(0, 1)
-        quantize_x(0, 0)
+        quantize(v_codes[1], v_planes[1], v_t[1])
+        quantize_x(0, 1)
+        x_tiles(8, 4)
 
         for g in range(GROUPS - 1):
             split_grad(g + 1, nc.scalar.copy)
@@ -299,23 +315,24 @@ def tile_router_weight_gradient_s12_kernel(
                 load_grad(g + 2)
             load_prob(g + 1)
             utilities(g)
-            order_a(g + 1)
+            if g + 2 < GROUPS:
+                order_a(g + 2)
             turn_grad(g + 1)
             weigh(g, 0)
             quantize_grad(g + 1, 0)
             quantize_grad(g + 1, 1)
             weigh(g, 1)
-            quantize_x(*[(0, 1), (1, 0), (2, 0)][g])
+            quantize_x(*[(1, 0), (1, 1), (2, 0)][g])
             quantize_l(g)
-            x_tiles(8 + 6 * g, 6)
+            x_tiles(12 + 6 * g, 6 if g < 2 else 5)
         last = GROUPS - 1
         utilities(last)
-        x_tiles(26, 6)
+        x_tiles(29, 3)
         weigh(last, 0)
         weigh(last, 1)
         quantize_x(3, 0)
         quantize_l(last)
-        for g in range(1, GROUPS):
+        for g in range(2, GROUPS):
             quantize_x(g, 1)
         early = [next_bank() for j in range(4)]
         for j in range(4):

@@ -21,10 +21,15 @@ GROUP = P * PACK
 GROUPS = T // GROUP
 PASSES = 2
 BANK = 512
+HALF = 256
 BANKS = 8
 ALIGN = 64
 WARM_N = 256
 WARM_PASSES = 7
+PORT_ORDER = (0, 2, 1, 3)
+ROUND = (7, 7, 6)
+WIDE = ()
+LATE = 1
 
 
 def tile_router_weight_gradient_s12_kernel(
@@ -49,7 +54,6 @@ def tile_router_weight_gradient_s12_kernel(
 
         ident = keep("ident", [P, P], F32)
         bal_col = keep("bal_col", [P, PACK], BF16)
-        bal_wide = keep("bal_wide", [P, PACK, P], F32)
         bal_row = keep("bal_row", [P, E], F32)
         warm_codes = keep("warm_codes", [P, WARM_N], U32)
         warm_plane = keep("warm_plane", [P, WARM_N], U8)
@@ -80,14 +84,19 @@ def tile_router_weight_gradient_s12_kernel(
         x_bf = [[keep("x_bf%d_%d" % (g, n), [P, 512 * PACK], BF16) for n in range(2)] for g in range(GROUPS)]
         x_codes = [[keep("x_codes%d_%d" % (g, n), [P, 512], U32) for n in range(2)] for g in range(GROUPS)]
         x_planes = [[keep("x_plane%d_%d" % (g, n), [P, 512], U8) for n in range(2)] for g in range(GROUPS)]
-        result = [keep("result%d" % j, [P, E], F32) for j in range(D // P)]
+        result = [keep("result%d" % j, [P, BANK], F32) for j in range(D // P)]
+
+        def as_words(tile):
+            return tile[:].bitcast(F32)[:, 0 : 4 * P].rearrange("p (q w) -> p q w", q=4)
+
+        parted = [[[g_split[h][pair][:] for pair in range(2)] for h in range(PASSES)] for g in range(GROUPS)]
 
         def load_a(g):
             src = a_words.rearrange("h p n -> p h n")[:, :, 1024 * g : 1024 * (g + 1)]
             nc.sync.dma_start(out=a_raw[g][:], in_=src.bitcast(I32))
 
-        def load_scales(dst, scales, lo, hi, quadrants=range(4)):
-            for q in quadrants:
+        def load_scales(dst, scales, lo, hi):
+            for q in PORT_ORDER:
                 src = scales.rearrange("h r n -> r h n")[4 * q : 4 * q + 4, :, lo:hi]
                 nc.sync.dma_start(out=dst[32 * q : 32 * q + 4], in_=src.bitcast(I32))
 
@@ -114,8 +123,11 @@ def tile_router_weight_gradient_s12_kernel(
             for s in range(PACK):
                 nc.sync.dma_start(out=base_sb[s:P:PACK, :, 0:13], in_=rows[:, :, s : s + 13])
 
-        def order_a(g):
-            nc.vector.tensor_copy(
+        def load_balance(queue):
+            queue.dma_start(out=bal_col[:], in_=balance.rearrange("(p j) -> p j", j=PACK))
+
+        def order_a(g, copy):
+            copy(
                 out=a_codes[g][:].bitcast(I32).rearrange("p t h (c w) -> p t (h c) w", w=2),
                 in_=a_raw[g][:].rearrange("p h (c t w) -> p t (h c) w", t=PACK, w=2),
             )
@@ -123,60 +135,105 @@ def tile_router_weight_gradient_s12_kernel(
                 staged = a_sc_first[:]
             else:
                 staged = a_sc_rest[:, :, 128 * (g - 1) : 128 * g]
-            nc.vector.tensor_copy(
+            copy(
                 out=a_planes[g][:].bitcast(I32),
                 in_=staged.rearrange("p h (c t) -> p t h c", t=PACK),
             )
 
         def quantize(codes, plane, src):
-            nc.vector.quantize_mx(out=codes[:].bitcast(FP8X4), scales=plane[:], in_=src[:])
+            nc.vector.quantize_mx(out=codes.bitcast(FP8X4), scales=plane, in_=src)
 
         def spread_balance():
-            nc.scalar.copy(out=bal_wide[:], in_=bal_col[:].unsqueeze(2).to_broadcast([P, PACK, P]))
             bank = next_bank()
-            for j in range(PACK):
-                nc.tensor.transpose(bank[:, P * j : P * (j + 1)], bal_wide[:, j, :], ident[:])
+            words = bal_col[:].bitcast(F32)
+            for u in range(2):
+                nc.tensor.transpose(bank[:, P * u : P * (u + 1)], words[:, u : u + 1].to_broadcast([P, P]), ident[:])
             nc.scalar.copy(
-                out=bal_row[:].rearrange("p (n j) -> p n j", j=PACK),
-                in_=bank[:].rearrange("p (j n) -> p n j", j=PACK),
+                out=bal_row[:].rearrange("p (n u e) -> p n u e", u=2, e=2),
+                in_=bank[:, 0 : 2 * P].bitcast(BF16).rearrange("p (u n e) -> p n u e", u=2, e=2),
             )
 
-        def x_tiles(first, count):
-            for unit in range(first, first + count):
-                g, j = divmod(unit, 8)
-                n, jj = divmod(j, 4)
-                bank = next_bank()
-                for t in range(PACK):
-                    for h in range(PASSES):
-                        nc.tensor.matmul_mx(
-                            out=bank[:, P * t : P * (t + 1)],
-                            lhsT=a_codes[g][:, t, h, :].bitcast(FP4X4),
-                            lhsT_scale=a_planes[g][:, t, h, :],
-                            rhs=w_codes[n][:, h, 256 * jj : 256 * (jj + 1)].bitcast(FP4X4),
-                            rhs_scale=w_plane[:, h, P * j : P * (j + 1)],
-                            start=(h == 0),
-                            stop=(h == PASSES - 1),
-                        )
-                nc.scalar.copy(
-                    out=x_bf[g][n][:, BANK * jj : BANK * (jj + 1)].rearrange("p (d t) -> p d t", t=PACK),
-                    in_=bank[:].rearrange("p (t d) -> p d t", t=PACK),
+        def x_narrow(unit):
+            g, j = divmod(unit, 8)
+            n, jj = divmod(j, 4)
+            bank = next_bank()
+            for t in range(PACK):
+                for h in range(PASSES):
+                    nc.tensor.matmul_mx(
+                        out=bank[:, P * t : P * (t + 1)],
+                        lhsT=a_codes[g][:, t, h, :].bitcast(FP4X4),
+                        lhsT_scale=a_planes[g][:, t, h, :],
+                        rhs=w_codes[n][:, h, 256 * jj : 256 * (jj + 1)].bitcast(FP4X4),
+                        rhs_scale=w_plane[:, h, P * j : P * (j + 1)],
+                        start=(h == 0),
+                        stop=(h == PASSES - 1),
+                    )
+            nc.scalar.copy(
+                out=x_bf[g][n][:, BANK * jj : BANK * (jj + 1)].rearrange("p (d t) -> p d t", t=PACK),
+                in_=bank[:].rearrange("p (t d) -> p d t", t=PACK),
+            )
+
+        def x_wide(unit):
+            g, rest = divmod(unit, 8)
+            jp, pair = divmod(rest, 2)
+            n, jj = divmod(jp, 2)
+            bank = next_bank()
+            for u in range(2):
+                for h in range(PASSES):
+                    nc.tensor.matmul_mx(
+                        out=bank[:, HALF * u : HALF * (u + 1)],
+                        lhsT=a_codes[g][:, 2 * pair + u, h, :].bitcast(FP4X4),
+                        lhsT_scale=a_planes[g][:, 2 * pair + u, h, :],
+                        rhs=w_codes[n][:, h, 512 * jj : 512 * (jj + 1)].bitcast(FP4X4),
+                        rhs_scale=w_plane[:, h, HALF * jp : HALF * (jp + 1)],
+                        start=(h == 0),
+                        stop=(h == PASSES - 1),
+                    )
+            dst = x_bf[g][n][:, 1024 * jj : 1024 * (jj + 1)].rearrange("p (d t) -> p d t", t=PACK)
+            nc.scalar.copy(
+                out=dst[:, :, 2 * pair : 2 * pair + 2],
+                in_=bank[:].rearrange("p (u d) -> p d u", u=2),
+            )
+
+        made = []
+
+        def x_tiles(count):
+            for n in range(count):
+                unit = len(made)
+                made.append(unit)
+                if unit // 2 in WIDE:
+                    x_wide(unit)
+                else:
+                    x_narrow(unit)
+
+        def split_grad(g, copies):
+            for n, copy in enumerate(copies):
+                h, pair = divmod(n, 2)
+                words = g_raw[g][:, 2 * pair : 2 * pair + 2, GROUP * h : GROUP * (h + 1)].bitcast(F32)
+                copy(
+                    out=parted[g][h][pair].rearrange("p (s u) w -> p s u w", u=2),
+                    in_=words.rearrange("p s (w u) -> p s u w", u=2),
                 )
 
-        def split_grad(g, copy):
-            for pair in range(2):
-                for h in range(PASSES):
-                    words = g_raw[g][:, 2 * pair : 2 * pair + 2, GROUP * h : GROUP * (h + 1)].bitcast(F32)
-                    copy(
-                        out=g_split[h][pair][:].rearrange("p (s u) w -> p s u w", u=2),
-                        in_=words.rearrange("p s (w u) -> p s u w", u=2),
-                    )
+        def split_pair(g, pair):
+            for h in range(PASSES):
+                words = g_raw[g][:, 2 * pair : 2 * pair + 2, GROUP * h : GROUP * (h + 1)].bitcast(F32)
+                nc.vector.tensor_copy(
+                    out=parted[g][h][pair].rearrange("p (s u) w -> p s u w", u=2),
+                    in_=words.rearrange("p s (w u) -> p s u w", u=2),
+                )
 
-        def turn_grad(g):
-            for pair in range(2):
-                for h in range(PASSES):
+        def turn_grad(g, direct=False):
+            for h in range(PASSES):
+                for pair in range(2):
                     bank = next_bank()
                     for q in range(4):
-                        nc.tensor.transpose(bank[:, P * q : P * (q + 1)], g_split[h][pair][:, q, :], ident[:])
+                        if direct:
+                            s, u = divmod(q, 2)
+                            words = g_raw[g][:, 2 * pair + s, GROUP * h : GROUP * (h + 1)].bitcast(F32)[:, u::2]
+                        else:
+                            words = parted[g][h][pair][:, q, :]
+                        nc.tensor.transpose(bank[:, P * q : P * (q + 1)], words, ident[:])
                     dst = g_t[g][h][:].bitcast(F32).rearrange("p (t c w) -> p t c w", t=PACK, w=8)
                     nc.scalar.copy(
                         out=dst[:, :, :, 4 * pair : 4 * pair + 4],
@@ -189,28 +246,44 @@ def tile_router_weight_gradient_s12_kernel(
                 in_=v_raw[h][:].rearrange("p t (c i) -> p c t i", i=4),
             )
 
-        def utilities(g):
+        def utility_passes(g, t, dst, lo, hi):
+            for h in range(PASSES):
+                nc.tensor.matmul_mx(
+                    out=dst,
+                    lhsT=g_codes[g][h][:, P * t : P * (t + 1)].bitcast(FP8X4),
+                    lhsT_scale=g_planes[g][h][:, P * t : P * (t + 1)],
+                    rhs=v_codes[h][:, lo:hi].bitcast(FP8X4),
+                    rhs_scale=v_planes[h][:, lo:hi],
+                    start=(h == 0),
+                    stop=(h == PASSES - 1),
+                )
+
+        def shift(g, t, src, lo, hi):
             dst = shifted[g % 2][:].rearrange("p (c t i) -> p c t i", t=PACK, i=4)
+            nc.vector.scalar_tensor_tensor(
+                out=dst[:, lo // 4 : hi // 4, t, :],
+                in0=src.rearrange("p (c i) -> p c i", i=4),
+                scalar=base_sb[:, g, 4 * t : 4 * t + 1],
+                in1=bal_row[:, lo:hi].rearrange("p (c i) -> p c i", i=4),
+                op0=ALU.subtract,
+                op1=ALU.add,
+            )
+
+        def utilities(g):
             for t in range(PACK):
                 bank = next_bank()
-                for h in range(PASSES):
-                    nc.tensor.matmul_mx(
-                        out=bank[:],
-                        lhsT=g_codes[g][h][:, P * t : P * (t + 1)].bitcast(FP8X4),
-                        lhsT_scale=g_planes[g][h][:, P * t : P * (t + 1)],
-                        rhs=v_codes[h][:].bitcast(FP8X4),
-                        rhs_scale=v_planes[h][:],
-                        start=(h == 0),
-                        stop=(h == PASSES - 1),
-                    )
-                nc.vector.scalar_tensor_tensor(
-                    out=dst[:, :, t, :],
-                    in0=bank[:].rearrange("p (c i) -> p c i", i=4),
-                    scalar=base_sb[:, g, 4 * t : 4 * t + 1],
-                    in1=bal_row[:].rearrange("p (c i) -> p c i", i=4),
-                    op0=ALU.subtract,
-                    op1=ALU.add,
-                )
+                utility_passes(g, t, bank[:], 0, E)
+                shift(g, t, bank[:], 0, E)
+
+        def half_utilities(g, n):
+            banks = [next_bank() for pair in range(2)]
+            for t in range(PACK):
+                utility_passes(g, t, banks[t // 2][:, HALF * (t % 2) : HALF * (t % 2 + 1)], HALF * n, HALF * (n + 1))
+            return banks
+
+        def half_shift(g, n, banks):
+            for t in range(PACK):
+                shift(g, t, banks[t // 2][:, HALF * (t % 2) : HALF * (t % 2 + 1)], HALF * n, HALF * (n + 1))
 
         def weigh(g, n):
             cs = slice(64 * n, 64 * (n + 1))
@@ -221,39 +294,43 @@ def tile_router_weight_gradient_s12_kernel(
                 op=ALU.mult,
             )
 
+        def quantize_values(h):
+            quantize(v_codes[h][:], v_planes[h][:], v_t[h][:])
+
         def quantize_x(g, n):
-            quantize(x_codes[g][n], x_planes[g][n], x_bf[g][n])
+            quantize(x_codes[g][n][:], x_planes[g][n][:], x_bf[g][n][:])
 
         def quantize_grad(g, h):
-            quantize(g_codes[g][h], g_planes[g][h], g_t[g][h])
+            quantize(g_codes[g][h][:], g_planes[g][h][:], g_t[g][h][:])
 
-        def quantize_l(g):
-            quantize(l_codes[g], l_planes[g], l_bf[g % 2])
+        def quantize_l(g, lo=0, hi=E):
+            quantize(l_codes[g][:, lo:hi], l_planes[g][:, lo:hi], l_bf[g % 2][:, PACK * lo : PACK * hi])
 
-        def final_passes(bank, j, lo, hi, groups):
+        def final_passes(dst, j, lo, hi, groups, stop=True):
             n, cols = j // 4, slice(P * (j % 4), P * (j % 4 + 1))
             for g in groups:
                 nc.tensor.matmul_mx(
-                    out=bank[:, 0 : hi - lo],
+                    out=dst,
                     lhsT=x_codes[g][n][:, cols].bitcast(FP8X4),
                     lhsT_scale=x_planes[g][n][:, cols],
                     rhs=l_codes[g][:, lo:hi].bitcast(FP8X4),
                     rhs_scale=l_planes[g][:, lo:hi],
                     start=(g == 0),
-                    stop=(g == GROUPS - 1),
+                    stop=(stop and g == GROUPS - 1),
                 )
 
-        def store(bank, j, lo, hi, on_scalar):
-            if on_scalar:
-                nc.scalar.copy(out=result[j][:, lo:hi], in_=bank[:, 0 : hi - lo])
-            else:
-                nc.vector.tensor_copy(out=result[j][:, lo:hi], in_=bank[:, 0 : hi - lo])
-            nc.sync.dma_start(out=out[P * j : P * (j + 1), lo:hi], in_=result[j][:, lo:hi])
+        stored = []
 
-        def final(j, lo, hi, on_scalar):
-            bank = next_bank()
-            final_passes(bank, j, lo, hi, range(GROUPS))
-            store(bank, j, lo, hi, on_scalar)
+        def store(src, dst, copy):
+            staged = result[len(stored) % len(result)][:, 0 : src.shape[1]]
+            stored.append(staged)
+            copy(out=staged, in_=src)
+            if len(dst.shape) == 3:
+                staged = staged.rearrange("p (j e) -> p j e", j=dst.shape[1])
+            nc.sync.dma_start(out=dst, in_=staged)
+
+        out_tiles = out.rearrange("(j p) e -> p j e", p=P)
+        on_vector, on_scalar, on_gpsimd = nc.vector.tensor_copy, nc.scalar.copy, nc.gpsimd.tensor_copy
 
         def warm_up():
             bank = next_bank()
@@ -268,79 +345,80 @@ def tile_router_weight_gradient_s12_kernel(
                     stop=(n == WARM_PASSES - 1),
                 )
 
-        nc.gpsimd.dma_start(out=bal_col[:], in_=balance.rearrange("(p j) -> p j", j=PACK))
-        make_identity(nc, ident[:])
+        last = GROUPS - 1
         nc.vector.memset(a_sc_first[:], 0)
         nc.vector.memset(a_sc_rest[:], 0)
         nc.vector.memset(w_plane[:].bitcast(I32), 0)
         zeros = a_sc_rest[:].rearrange("p h n -> p (h n)").bitcast(BF16)[:, 0 : WARM_N * PACK]
-        nc.vector.quantize_mx(out=warm_codes[:].bitcast(FP8X4), scales=warm_plane[:], in_=zeros)
+        quantize(warm_codes[:], warm_plane[:], zeros)
+        make_identity(nc, ident[:])
 
         load_a(0)
-        load_scales(a_sc_first, a_scales, 0, GROUP, (0, 2, 1, 3))
+        load_scales(a_sc_first, a_scales, 0, GROUP)
         load_w(0)
-        load_scales(w_plane[:].bitcast(I32), w_scales, 0, D, (0, 2, 1, 3))
-        load_grad(0)
+        load_scales(w_plane[:].bitcast(I32), w_scales, 0, D)
         load_w(1)
         load_values(0)
-        load_a(1)
-        load_scales(a_sc_rest, a_scales, GROUP, T, (0, 2, 1, 3))
+        load_balance(nc.sync)
+        load_grad(0)
         load_values(1)
-        load_grad(1)
         load_base()
+        load_a(1)
+        load_scales(a_sc_rest, a_scales, GROUP, T)
+        load_grad(1)
         load_prob(0)
 
         warm_up()
-        spread_balance()
-        order_a(0)
-        x_tiles(0, 4)
-        split_grad(0, nc.vector.tensor_copy)
-        turn_grad(0)
-        quantize_x(0, 0)
+        order_a(0, on_vector)
+        x_tiles(6)
         interleave_values(0)
-        x_tiles(4, 4)
-        order_a(1)
-        quantize_grad(0, 0)
-        quantize(v_codes[0], v_planes[0], v_t[0])
+        spread_balance()
+        turn_grad(0, direct=True)
+        quantize_values(0)
+        quantize_x(0, 0)
         interleave_values(1)
+        x_tiles(2)
+        quantize_grad(0, 0)
+        quantize_values(1)
         quantize_grad(0, 1)
-        quantize(v_codes[1], v_planes[1], v_t[1])
-        quantize_x(0, 1)
-        x_tiles(8, 4)
-
-        for g in range(GROUPS - 1):
-            split_grad(g + 1, nc.scalar.copy)
+        order_a(1, on_vector)
+        for g in range(last):
+            utilities(g)
+            split_grad(g + 1, [on_scalar] * 4)
             if g + 2 < GROUPS:
                 load_a(g + 2)
                 load_grad(g + 2)
             load_prob(g + 1)
-            utilities(g)
-            if g + 2 < GROUPS:
-                order_a(g + 2)
             turn_grad(g + 1)
+            quantize_x(g, 1 if g == 0 else 0)
             weigh(g, 0)
-            quantize_grad(g + 1, 0)
-            quantize_grad(g + 1, 1)
             weigh(g, 1)
-            quantize_x(*[(1, 0), (1, 1), (2, 0)][g])
+            quantize_grad(g + 1, 0)
+            if g + 2 < GROUPS:
+                order_a(g + 2, on_vector)
+            quantize_grad(g + 1, 1)
             quantize_l(g)
-            x_tiles(12 + 6 * g, 6 if g < 2 else 5)
-        last = GROUPS - 1
+            x_tiles(ROUND[g])
         utilities(last)
-        x_tiles(29, 3)
+        x_tiles(32 - len(made))
+        quantize_x(last, 0)
         weigh(last, 0)
         weigh(last, 1)
-        quantize_x(3, 0)
+        quantize_x(LATE, 1)
         quantize_l(last)
-        for g in range(2, GROUPS):
+        for g in range(LATE + 1, GROUPS):
             quantize_x(g, 1)
         early = [next_bank() for j in range(4)]
         for j in range(4):
-            final_passes(early[j], j, 0, E, range(last))
+            final_passes(early[j][:], j, 0, E, range(last))
         for j in range(4):
-            final_passes(early[j], j, 0, E, [last])
-            store(early[j], j, 0, E, j % 2 == 0)
-        for j in range(4, D // P - 1):
-            final(j, 0, E, j % 2 == 0)
-        final(D // P - 1, 0, E // 2, False)
-        final(D // P - 1, E // 2, E, True)
+            final_passes(early[j][:], j, 0, E, [last])
+            store(early[j][:], out_tiles[:, j, :], on_scalar if j % 2 == 0 else on_vector)
+        for j in range(4, 7):
+            bank = next_bank()
+            final_passes(bank[:], j, 0, E, range(GROUPS))
+            store(bank[:], out_tiles[:, j, :], on_scalar if j % 2 == 0 else on_vector)
+        for n in range(2):
+            bank = next_bank()
+            final_passes(bank[:, 0:HALF], 7, HALF * n, HALF * (n + 1), range(GROUPS))
+            store(bank[:, 0:HALF], out_tiles[:, 7, HALF * n : HALF * (n + 1)], on_vector if n == 0 else on_scalar)

@@ -25,11 +25,14 @@ HALF = 256
 BANKS = 8
 ALIGN = 64
 WARM_N = 256
-WARM_PASSES = 7
+WARM_PASSES = 6
 PORT_ORDER = (0, 2, 1, 3)
-ROUND = (7, 7, 6)
 WIDE = ()
-LATE = 1
+ORDER = ((0, 0), (1, 0), (0, 1), (1, 1), (2, 0), (2, 1), (3, 0), (3, 1))
+BATCHES = (((0, 0),), ((1, 0),), ((0, 1),), (("L", 0),), ((1, 1),), (("L", 1), (2, 0)), ((2, 1),), (("L", 2), (3, 0)), ((3, 1),), (("L", 3),))
+EARLY = 5
+NH = 3
+ROUND = (5, 6, 6)
 
 
 def tile_router_weight_gradient_s12_kernel(
@@ -61,35 +64,40 @@ def tile_router_weight_gradient_s12_kernel(
 
         a_raw = [keep("a_raw%d" % g, [P, PASSES, 256], I32) for g in range(2)] * 2
         a_codes = [keep("a_codes%d" % g, [P, PACK, PASSES, 256], U8) for g in range(GROUPS)]
-        a_sc_first = keep("a_sc_first", [P, PASSES, 128], I32)
-        a_sc_rest = keep("a_sc_rest", [P, PASSES, 384], I32)
-        a_planes = [keep("a_plane%d" % g, [P, PACK, PASSES, P], U8) for g in range(GROUPS)]
+        a_sc_first = keep("a_sc_first", [P, PASSES, 256], I32)
+        a_sc_rest = keep("a_sc_rest", [P, PASSES, 256], I32)
+        a_planes = [keep("a_plane%d" % half, [P, PACK, PASSES, 2, P], U8) for half in range(2)]
         w_codes = [keep("w_codes%d" % n, [P, PASSES, 1024], U8) for n in range(2)]
-        w_plane = keep("w_plane", [P, PASSES, D], U8)
+        w_planes = [keep("w_plane%d" % n, [P, PASSES, 512], U8) for n in range(2)]
 
         g_raw = [keep("g_raw%d" % g, [P, PACK, D], BF16) for g in range(2)] * 2
-        g_split = [[keep("g_split%d_%d" % (h, pair), [P, 4, P], F32) for pair in range(2)] for h in range(PASSES)]
-        g_t = [[keep("g_t%d_%d" % (g, h), [P, GROUP * PACK], BF16) for h in range(PASSES)] for g in range(2)] * 2
-        g_codes = [[keep("g_codes%d_%d" % (g, h), [P, GROUP], U32) for h in range(PASSES)] for g in range(2)] * 2
-        g_planes = [[keep("g_plane%d_%d" % (g, h), [P, GROUP], U8) for h in range(PASSES)] for g in range(2)] * 2
+        g_split = keep("g_split", [P, PASSES, 8, P], F32)
+        g_t = [keep("g_t%d" % g, [P, PASSES * GROUP * PACK], BF16) for g in range(2)] * 2
+        g_codes = [keep("g_codes%d" % g, [P, PASSES * GROUP], U32) for g in range(2)] * 2
+        g_planes = [keep("g_plane%d" % g, [P, PASSES * GROUP], U8) for g in range(2)] * 2
         v_raw = [keep("v_raw%d" % h, [P, PACK, E], BF16) for h in range(PASSES)]
         v_t = [keep("v_t%d" % h, [P, E * PACK], BF16) for h in range(PASSES)]
         v_codes = [keep("v_codes%d" % h, [P, E], U32) for h in range(PASSES)]
         v_planes = [keep("v_plane%d" % h, [P, E], U8) for h in range(PASSES)]
         p_sb = [keep("p_sb%d" % g, [P, PACK, E], BF16) for g in range(GROUPS)]
         shifted = [keep("shifted%d" % n, [P, E * PACK], F32) for n in range(2)]
-        l_bf = [keep("l_bf%d" % n, [P, E * PACK], BF16) for n in range(2)]
-        l_codes = [keep("l_codes%d" % g, [P, E], U32) for g in range(GROUPS)]
-        l_planes = [keep("l_plane%d" % g, [P, E], U8) for g in range(GROUPS)]
-        x_bf = [[keep("x_bf%d_%d" % (g, n), [P, 512 * PACK], BF16) for n in range(2)] for g in range(GROUPS)]
-        x_codes = [[keep("x_codes%d_%d" % (g, n), [P, 512], U32) for n in range(2)] for g in range(GROUPS)]
-        x_planes = [[keep("x_plane%d_%d" % (g, n), [P, 512], U8) for n in range(2)] for g in range(GROUPS)]
-        result = [keep("result%d" % j, [P, BANK], F32) for j in range(D // P)]
+        wide, codes, planes, batch = {}, {}, {}, {}
+        for n, members in enumerate(BATCHES):
+            k = len(members)
+            batch[members] = (
+                keep("wide%d" % n, [P, k * BANK * PACK], BF16),
+                keep("codes%d" % n, [P, k * BANK], U32),
+                keep("plane%d" % n, [P, k * BANK], U8),
+            )
+            for m, member in enumerate(members):
+                wide[member] = batch[members][0][:, BANK * PACK * m : BANK * PACK * (m + 1)]
+                codes[member] = batch[members][1][:, BANK * m : BANK * (m + 1)]
+                planes[member] = batch[members][2][:, BANK * m : BANK * (m + 1)]
+        result = [keep("result%d" % j, [P, BANK], F32) for j in range(6)]
 
-        def as_words(tile):
-            return tile[:].bitcast(F32)[:, 0 : 4 * P].rearrange("p (q w) -> p q w", q=4)
-
-        parted = [[[g_split[h][pair][:] for pair in range(2)] for h in range(PASSES)] for g in range(GROUPS)]
+        parted = [[[g_split[:, h, 4 * pair : 4 * pair + 4] for pair in range(2)] for h in range(PASSES)] for g in range(GROUPS)]
+        for g, member in ((1, (0, 0)), (2, (0, 1)), (3, (1, 1))):
+            parted[g][1][1] = wide[member].bitcast(F32)[:, 0 : 4 * P].rearrange("p (q w) -> p q w", q=4)
 
         def load_a(g):
             src = a_words.rearrange("h p n -> p h n")[:, :, 1024 * g : 1024 * (g + 1)]
@@ -126,18 +134,16 @@ def tile_router_weight_gradient_s12_kernel(
         def load_balance(queue):
             queue.dma_start(out=bal_col[:], in_=balance.rearrange("(p j) -> p j", j=PACK))
 
-        def order_a(g, copy):
+        def order_codes(g, copy):
             copy(
                 out=a_codes[g][:].bitcast(I32).rearrange("p t h (c w) -> p t (h c) w", w=2),
                 in_=a_raw[g][:].rearrange("p h (c t w) -> p t (h c) w", t=PACK, w=2),
             )
-            if g == 0:
-                staged = a_sc_first[:]
-            else:
-                staged = a_sc_rest[:, :, 128 * (g - 1) : 128 * g]
+
+        def order_scales(half, copy):
             copy(
-                out=a_planes[g][:].bitcast(I32),
-                in_=staged.rearrange("p h (c t) -> p t h c", t=PACK),
+                out=a_planes[half][:].bitcast(I32).rearrange("p t h g c -> p t (h g c)"),
+                in_=(a_sc_first, a_sc_rest)[half][:].rearrange("p h (gc t) -> p t (h gc)", t=PACK),
             )
 
         def quantize(codes, plane, src):
@@ -162,14 +168,14 @@ def tile_router_weight_gradient_s12_kernel(
                     nc.tensor.matmul_mx(
                         out=bank[:, P * t : P * (t + 1)],
                         lhsT=a_codes[g][:, t, h, :].bitcast(FP4X4),
-                        lhsT_scale=a_planes[g][:, t, h, :],
+                        lhsT_scale=a_planes[g // 2][:, t, h, g % 2, :],
                         rhs=w_codes[n][:, h, 256 * jj : 256 * (jj + 1)].bitcast(FP4X4),
-                        rhs_scale=w_plane[:, h, P * j : P * (j + 1)],
+                        rhs_scale=w_planes[n][:, h, P * jj : P * (jj + 1)],
                         start=(h == 0),
                         stop=(h == PASSES - 1),
                     )
             nc.scalar.copy(
-                out=x_bf[g][n][:, BANK * jj : BANK * (jj + 1)].rearrange("p (d t) -> p d t", t=PACK),
+                out=wide[g, n][:, BANK * jj : BANK * (jj + 1)].rearrange("p (d t) -> p d t", t=PACK),
                 in_=bank[:].rearrange("p (t d) -> p d t", t=PACK),
             )
 
@@ -183,62 +189,62 @@ def tile_router_weight_gradient_s12_kernel(
                     nc.tensor.matmul_mx(
                         out=bank[:, HALF * u : HALF * (u + 1)],
                         lhsT=a_codes[g][:, 2 * pair + u, h, :].bitcast(FP4X4),
-                        lhsT_scale=a_planes[g][:, 2 * pair + u, h, :],
+                        lhsT_scale=a_planes[g // 2][:, 2 * pair + u, h, g % 2, :],
                         rhs=w_codes[n][:, h, 512 * jj : 512 * (jj + 1)].bitcast(FP4X4),
-                        rhs_scale=w_plane[:, h, HALF * jp : HALF * (jp + 1)],
+                        rhs_scale=w_planes[n][:, h, HALF * jj : HALF * (jj + 1)],
                         start=(h == 0),
                         stop=(h == PASSES - 1),
                     )
-            dst = x_bf[g][n][:, 1024 * jj : 1024 * (jj + 1)].rearrange("p (d t) -> p d t", t=PACK)
+            dst = wide[g, n][:, 1024 * jj : 1024 * (jj + 1)].rearrange("p (d t) -> p d t", t=PACK)
             nc.scalar.copy(
                 out=dst[:, :, 2 * pair : 2 * pair + 2],
                 in_=bank[:].rearrange("p (u d) -> p d u", u=2),
             )
 
         made = []
+        units = [8 * g + 4 * n + jj for g, n in ORDER for jj in range(4)]
 
         def x_tiles(count):
             for n in range(count):
-                unit = len(made)
+                unit = units[len(made)]
                 made.append(unit)
                 if unit // 2 in WIDE:
                     x_wide(unit)
                 else:
                     x_narrow(unit)
 
-        def split_grad(g, copies):
-            for n, copy in enumerate(copies):
-                h, pair = divmod(n, 2)
-                words = g_raw[g][:, 2 * pair : 2 * pair + 2, GROUP * h : GROUP * (h + 1)].bitcast(F32)
-                copy(
-                    out=parted[g][h][pair].rearrange("p (s u) w -> p s u w", u=2),
-                    in_=words.rearrange("p s (w u) -> p s u w", u=2),
-                )
+        def grad_words(g):
+            return g_raw[g][:].bitcast(F32).rearrange("p s (h w u) -> p h s u w", h=PASSES, u=2)
+
+        def split_pass(g, h, copy):
+            copy(out=g_split[:, h].rearrange("p (s u) w -> p s u w", u=2), in_=grad_words(g)[:, h])
+
+        def split_piece(g, h, pair, copy):
+            rows = slice(2 * pair, 2 * pair + 2)
+            copy(out=parted[g][h][pair].rearrange("p (s u) w -> p s u w", u=2), in_=grad_words(g)[:, h, rows])
 
         def split_pair(g, pair):
-            for h in range(PASSES):
-                words = g_raw[g][:, 2 * pair : 2 * pair + 2, GROUP * h : GROUP * (h + 1)].bitcast(F32)
-                nc.vector.tensor_copy(
-                    out=parted[g][h][pair].rearrange("p (s u) w -> p s u w", u=2),
-                    in_=words.rearrange("p s (w u) -> p s u w", u=2),
-                )
+            dst = g_split[:].rearrange("p h (s u) w -> p h s u w", u=2)
+            rows = slice(2 * pair, 2 * pair + 2)
+            nc.vector.tensor_copy(out=dst[:, :, rows], in_=grad_words(g)[:, :, rows])
 
-        def turn_grad(g, direct=False):
-            for h in range(PASSES):
-                for pair in range(2):
-                    bank = next_bank()
-                    for q in range(4):
-                        if direct:
-                            s, u = divmod(q, 2)
-                            words = g_raw[g][:, 2 * pair + s, GROUP * h : GROUP * (h + 1)].bitcast(F32)[:, u::2]
-                        else:
-                            words = parted[g][h][pair][:, q, :]
-                        nc.tensor.transpose(bank[:, P * q : P * (q + 1)], words, ident[:])
-                    dst = g_t[g][h][:].bitcast(F32).rearrange("p (t c w) -> p t c w", t=PACK, w=8)
-                    nc.scalar.copy(
-                        out=dst[:, :, :, 4 * pair : 4 * pair + 4],
-                        in_=bank[:].rearrange("p (q c t) -> p t c q", q=4, t=PACK),
-                    )
+        def turn_grad(g, copies, pair_first=False, direct=False):
+            for n, copy in enumerate(copies):
+                h, pair = divmod(n, 2)
+                if pair_first:
+                    h, pair = pair, h
+                bank = next_bank()
+                for q in range(4):
+                    if direct:
+                        words = grad_words(g)[:, h, 2 * pair + q // 2, q % 2]
+                    else:
+                        words = parted[g][h][pair][:, q, :]
+                    nc.tensor.transpose(bank[:, P * q : P * (q + 1)], words, ident[:])
+                dst = g_t[g][:].bitcast(F32).rearrange("p (h t c w) -> p h t c w", h=PASSES, t=PACK, w=8)
+                copy(
+                    out=dst[:, h, :, :, 4 * pair : 4 * pair + 4],
+                    in_=bank[:].rearrange("p (q c t) -> p t c q", q=4, t=PACK),
+                )
 
         def interleave_values(h):
             nc.vector.tensor_copy(
@@ -250,8 +256,8 @@ def tile_router_weight_gradient_s12_kernel(
             for h in range(PASSES):
                 nc.tensor.matmul_mx(
                     out=dst,
-                    lhsT=g_codes[g][h][:, P * t : P * (t + 1)].bitcast(FP8X4),
-                    lhsT_scale=g_planes[g][h][:, P * t : P * (t + 1)],
+                    lhsT=g_codes[g][:, GROUP * h + P * t : GROUP * h + P * (t + 1)].bitcast(FP8X4),
+                    lhsT_scale=g_planes[g][:, GROUP * h + P * t : GROUP * h + P * (t + 1)],
                     rhs=v_codes[h][:, lo:hi].bitcast(FP8X4),
                     rhs_scale=v_planes[h][:, lo:hi],
                     start=(h == 0),
@@ -288,7 +294,7 @@ def tile_router_weight_gradient_s12_kernel(
         def weigh(g, n):
             cs = slice(64 * n, 64 * (n + 1))
             nc.vector.tensor_tensor(
-                out=l_bf[g % 2][:].rearrange("p (c i t) -> p c t i", i=4, t=PACK)[:, cs],
+                out=wide["L", g].rearrange("p (c i t) -> p c t i", i=4, t=PACK)[:, cs],
                 in0=shifted[g % 2][:].rearrange("p (c t i) -> p c t i", t=PACK, i=4)[:, cs],
                 in1=p_sb[g][:].rearrange("p t (c i) -> p c t i", i=4)[:, cs],
                 op=ALU.mult,
@@ -297,24 +303,28 @@ def tile_router_weight_gradient_s12_kernel(
         def quantize_values(h):
             quantize(v_codes[h][:], v_planes[h][:], v_t[h][:])
 
-        def quantize_x(g, n):
-            quantize(x_codes[g][n][:], x_planes[g][n][:], x_bf[g][n][:])
+        def quantize_grad(g, lo=0, hi=PASSES):
+            quantize(
+                g_codes[g][:, GROUP * lo : GROUP * hi],
+                g_planes[g][:, GROUP * lo : GROUP * hi],
+                g_t[g][:, GROUP * PACK * lo : GROUP * PACK * hi],
+            )
 
-        def quantize_grad(g, h):
-            quantize(g_codes[g][h][:], g_planes[g][h][:], g_t[g][h][:])
-
-        def quantize_l(g, lo=0, hi=E):
-            quantize(l_codes[g][:, lo:hi], l_planes[g][:, lo:hi], l_bf[g % 2][:, PACK * lo : PACK * hi])
+        def quantize_batch(n):
+            for member in BATCHES[n]:
+                assert member[0] == "L" or 8 * member[0] + 4 * member[1] + 3 in made
+            src, dst, plane = batch[BATCHES[n]]
+            quantize(dst[:], plane[:], src[:])
 
         def final_passes(dst, j, lo, hi, groups, stop=True):
             n, cols = j // 4, slice(P * (j % 4), P * (j % 4 + 1))
             for g in groups:
                 nc.tensor.matmul_mx(
                     out=dst,
-                    lhsT=x_codes[g][n][:, cols].bitcast(FP8X4),
-                    lhsT_scale=x_planes[g][n][:, cols],
-                    rhs=l_codes[g][:, lo:hi].bitcast(FP8X4),
-                    rhs_scale=l_planes[g][:, lo:hi],
+                    lhsT=codes[g, n][:, cols].bitcast(FP8X4),
+                    lhsT_scale=planes[g, n][:, cols],
+                    rhs=codes["L", g][:, lo:hi].bitcast(FP8X4),
+                    rhs_scale=planes["L", g][:, lo:hi],
                     start=(g == 0),
                     stop=(stop and g == GROUPS - 1),
                 )
@@ -347,74 +357,80 @@ def tile_router_weight_gradient_s12_kernel(
 
         last = GROUPS - 1
         nc.vector.memset(a_sc_first[:], 0)
+        nc.vector.memset(w_planes[0][:].bitcast(I32), 0)
         nc.vector.memset(a_sc_rest[:], 0)
-        nc.vector.memset(w_plane[:].bitcast(I32), 0)
+        nc.vector.memset(w_planes[1][:].bitcast(I32), 0)
         zeros = a_sc_rest[:].rearrange("p h n -> p (h n)").bitcast(BF16)[:, 0 : WARM_N * PACK]
         quantize(warm_codes[:], warm_plane[:], zeros)
         make_identity(nc, ident[:])
 
         load_a(0)
-        load_scales(a_sc_first, a_scales, 0, GROUP)
+        load_scales(a_sc_first, a_scales, 0, 2 * GROUP)
         load_w(0)
-        load_scales(w_plane[:].bitcast(I32), w_scales, 0, D)
-        load_w(1)
+        load_scales(w_planes[0][:].bitcast(I32), w_scales, 0, 512)
+        load_a(1)
         load_values(0)
         load_balance(nc.sync)
-        load_grad(0)
         load_values(1)
+        load_grad(0)
         load_base()
-        load_a(1)
-        load_scales(a_sc_rest, a_scales, GROUP, T)
+        load_w(1)
+        load_scales(w_planes[1][:].bitcast(I32), w_scales, 512, D)
+        load_scales(a_sc_rest, a_scales, 2 * GROUP, T)
         load_grad(1)
         load_prob(0)
 
         warm_up()
-        order_a(0, on_vector)
-        x_tiles(6)
+        order_codes(0, on_vector)
+        order_scales(0, on_vector)
+        order_codes(1, on_vector)
+        x_tiles(8)
         interleave_values(0)
-        spread_balance()
-        turn_grad(0, direct=True)
-        quantize_values(0)
-        quantize_x(0, 0)
         interleave_values(1)
-        x_tiles(2)
-        quantize_grad(0, 0)
+        split_pair(0, 0)
+        quantize_values(0)
+        split_pair(0, 1)
         quantize_values(1)
-        quantize_grad(0, 1)
-        order_a(1, on_vector)
+        turn_grad(0, [on_scalar, on_scalar, on_vector, on_scalar], pair_first=True)
+        spread_balance()
+        x_tiles(NH)
+        quantize_grad(0, 0, 1)
+        quantize_grad(0, 1, 2)
+        quantize_batch(0)
         for g in range(last):
             utilities(g)
-            split_grad(g + 1, [on_scalar] * 4)
+            split_pass(g + 1, 0, on_scalar)
+            split_piece(g + 1, 1, 0, on_scalar)
+            split_piece(g + 1, 1, 1, on_gpsimd)
+            if g == 0:
+                order_scales(1, on_gpsimd)
+            else:
+                order_codes(g + 1, on_gpsimd)
             if g + 2 < GROUPS:
                 load_a(g + 2)
                 load_grad(g + 2)
             load_prob(g + 1)
-            turn_grad(g + 1)
-            quantize_x(g, 1 if g == 0 else 0)
+            turn_grad(g + 1, [on_scalar] * 4)
+            quantize_batch(2 * g + 1)
             weigh(g, 0)
+            quantize_grad(g + 1)
             weigh(g, 1)
-            quantize_grad(g + 1, 0)
-            if g + 2 < GROUPS:
-                order_a(g + 2, on_vector)
-            quantize_grad(g + 1, 1)
-            quantize_l(g)
             x_tiles(ROUND[g])
+            quantize_batch(2 * g + 2)
         utilities(last)
         x_tiles(32 - len(made))
-        quantize_x(last, 0)
+        quantize_batch(7)
         weigh(last, 0)
         weigh(last, 1)
-        quantize_x(LATE, 1)
-        quantize_l(last)
-        for g in range(LATE + 1, GROUPS):
-            quantize_x(g, 1)
-        early = [next_bank() for j in range(4)]
-        for j in range(4):
+        quantize_batch(9)
+        quantize_batch(8)
+        early = [next_bank() for j in range(EARLY)]
+        for j in range(EARLY):
             final_passes(early[j][:], j, 0, E, range(last))
-        for j in range(4):
+        for j in range(EARLY):
             final_passes(early[j][:], j, 0, E, [last])
             store(early[j][:], out_tiles[:, j, :], on_scalar if j % 2 == 0 else on_vector)
-        for j in range(4, 7):
+        for j in range(EARLY, 7):
             bank = next_bank()
             final_passes(bank[:], j, 0, E, range(GROUPS))
             store(bank[:], out_tiles[:, j, :], on_scalar if j % 2 == 0 else on_vector)

@@ -25,14 +25,15 @@ HALF = 256
 BANKS = 8
 ALIGN = 64
 WARM_N = 256
-WARM_PASSES = 6
+WARM_PASSES = 5
+KEEP_WARM_PASSES = 8
 PORT_ORDER = (0, 2, 1, 3)
 WIDE = ()
 ORDER = ((0, 0), (1, 0), (0, 1), (1, 1), (2, 0), (2, 1), (3, 0), (3, 1))
 BATCHES = (((0, 0),), ((1, 0),), ((0, 1),), (("L", 0),), ((1, 1),), (("L", 1), (2, 0)), ((2, 1),), (("L", 2), (3, 0)), ((3, 1),), (("L", 3),))
-EARLY = 5
 NH = 3
-ROUND = (5, 6, 6)
+ROUND = (5, 6, 7)
+BEFORE = (0, 0, 0)
 
 
 def tile_router_weight_gradient_s12_kernel(
@@ -66,12 +67,12 @@ def tile_router_weight_gradient_s12_kernel(
         a_codes = [keep("a_codes%d" % g, [P, PACK, PASSES, 256], U8) for g in range(GROUPS)]
         a_sc_first = keep("a_sc_first", [P, PASSES, 256], I32)
         a_sc_rest = keep("a_sc_rest", [P, PASSES, 256], I32)
-        a_planes = [keep("a_plane%d" % half, [P, PACK, PASSES, 2, P], U8) for half in range(2)]
+        a_planes = [keep("a_plane%d" % g, [P, PACK, PASSES, P], U8) for g in range(GROUPS)]
         w_codes = [keep("w_codes%d" % n, [P, PASSES, 1024], U8) for n in range(2)]
-        w_planes = [keep("w_plane%d" % n, [P, PASSES, 512], U8) for n in range(2)]
+        w_plane = keep("w_plane", [P, PASSES, D], U8)
 
         g_raw = [keep("g_raw%d" % g, [P, PACK, D], BF16) for g in range(2)] * 2
-        g_split = keep("g_split", [P, PASSES, 8, P], F32)
+        g_split = [keep("g_split%d" % h, [P, 8, P], F32) for h in range(PASSES)]
         g_t = [keep("g_t%d" % g, [P, PASSES * GROUP * PACK], BF16) for g in range(2)] * 2
         g_codes = [keep("g_codes%d" % g, [P, PASSES * GROUP], U32) for g in range(2)] * 2
         g_planes = [keep("g_plane%d" % g, [P, PASSES * GROUP], U8) for g in range(2)] * 2
@@ -93,9 +94,9 @@ def tile_router_weight_gradient_s12_kernel(
                 wide[member] = batch[members][0][:, BANK * PACK * m : BANK * PACK * (m + 1)]
                 codes[member] = batch[members][1][:, BANK * m : BANK * (m + 1)]
                 planes[member] = batch[members][2][:, BANK * m : BANK * (m + 1)]
-        result = [keep("result%d" % j, [P, BANK], F32) for j in range(6)]
+        result = [keep("result%d" % j, [P, HALF], F32) for j in range(12)]
 
-        parted = [[[g_split[:, h, 4 * pair : 4 * pair + 4] for pair in range(2)] for h in range(PASSES)] for g in range(GROUPS)]
+        parted = [[[g_split[h][:, 4 * pair : 4 * pair + 4] for pair in range(2)] for h in range(PASSES)] for g in range(GROUPS)]
         for g, member in ((1, (0, 0)), (2, (0, 1)), (3, (1, 1))):
             parted[g][1][1] = wide[member].bitcast(F32)[:, 0 : 4 * P].rearrange("p (q w) -> p q w", q=4)
 
@@ -103,18 +104,18 @@ def tile_router_weight_gradient_s12_kernel(
             src = a_words.rearrange("h p n -> p h n")[:, :, 1024 * g : 1024 * (g + 1)]
             nc.sync.dma_start(out=a_raw[g][:], in_=src.bitcast(I32))
 
-        def load_scales(dst, scales, lo, hi):
-            for q in PORT_ORDER:
+        def load_scales(dst, scales, lo, hi, quadrants=PORT_ORDER, queue=nc.sync):
+            for q in quadrants:
                 src = scales.rearrange("h r n -> r h n")[4 * q : 4 * q + 4, :, lo:hi]
-                nc.sync.dma_start(out=dst[32 * q : 32 * q + 4], in_=src.bitcast(I32))
+                queue.dma_start(out=dst[32 * q : 32 * q + 4], in_=src.bitcast(I32))
 
         def load_w(n):
             src = w_words.rearrange("h p n -> p h n")[:, :, 1024 * n : 1024 * (n + 1)]
             nc.sync.dma_start(out=w_codes[n][:].bitcast(I32), in_=src.bitcast(I32))
 
-        def load_grad(g):
+        def load_grad(g, pairs=range(2)):
             rows = grad[GROUP * g : GROUP * (g + 1), :].rearrange("(m s) d -> m s d", s=PACK)
-            for pair in range(2):
+            for pair in pairs:
                 nc.sync.dma_start(out=g_raw[g][:, 2 * pair : 2 * pair + 2, :], in_=rows[:, 2 * pair : 2 * pair + 2, :])
 
         def load_values(h):
@@ -126,10 +127,9 @@ def tile_router_weight_gradient_s12_kernel(
             for s in range(PACK):
                 nc.sync.dma_start(out=p_sb[g][s:P:PACK, :, :], in_=rows[s])
 
-        def load_base():
+        def load_base(s):
             rows = base.rearrange("(g c w) -> c g w", g=GROUPS, w=16)
-            for s in range(PACK):
-                nc.sync.dma_start(out=base_sb[s:P:PACK, :, 0:13], in_=rows[:, :, s : s + 13])
+            nc.sync.dma_start(out=base_sb[s:P:PACK, :, 0:13], in_=rows[:, :, s : s + 13])
 
         def load_balance(queue):
             queue.dma_start(out=bal_col[:], in_=balance.rearrange("(p j) -> p j", j=PACK))
@@ -140,11 +140,9 @@ def tile_router_weight_gradient_s12_kernel(
                 in_=a_raw[g][:].rearrange("p h (c t w) -> p t (h c) w", t=PACK, w=2),
             )
 
-        def order_scales(half, copy):
-            copy(
-                out=a_planes[half][:].bitcast(I32).rearrange("p t h g c -> p t (h g c)"),
-                in_=(a_sc_first, a_sc_rest)[half][:].rearrange("p h (gc t) -> p t (h gc)", t=PACK),
-            )
+        def order_scales(g, copy):
+            staged = (a_sc_first, a_sc_rest)[g // 2][:, :, 128 * (g % 2) : 128 * (g % 2 + 1)]
+            copy(out=a_planes[g][:].bitcast(I32), in_=staged.rearrange("p h (c t) -> p t h c", t=PACK))
 
         def quantize(codes, plane, src):
             nc.vector.quantize_mx(out=codes.bitcast(FP8X4), scales=plane, in_=src)
@@ -168,9 +166,9 @@ def tile_router_weight_gradient_s12_kernel(
                     nc.tensor.matmul_mx(
                         out=bank[:, P * t : P * (t + 1)],
                         lhsT=a_codes[g][:, t, h, :].bitcast(FP4X4),
-                        lhsT_scale=a_planes[g // 2][:, t, h, g % 2, :],
+                        lhsT_scale=a_planes[g][:, t, h, :],
                         rhs=w_codes[n][:, h, 256 * jj : 256 * (jj + 1)].bitcast(FP4X4),
-                        rhs_scale=w_planes[n][:, h, P * jj : P * (jj + 1)],
+                        rhs_scale=w_plane[:, h, P * j : P * (j + 1)],
                         start=(h == 0),
                         stop=(h == PASSES - 1),
                     )
@@ -189,9 +187,9 @@ def tile_router_weight_gradient_s12_kernel(
                     nc.tensor.matmul_mx(
                         out=bank[:, HALF * u : HALF * (u + 1)],
                         lhsT=a_codes[g][:, 2 * pair + u, h, :].bitcast(FP4X4),
-                        lhsT_scale=a_planes[g // 2][:, 2 * pair + u, h, g % 2, :],
+                        lhsT_scale=a_planes[g][:, 2 * pair + u, h, :],
                         rhs=w_codes[n][:, h, 512 * jj : 512 * (jj + 1)].bitcast(FP4X4),
-                        rhs_scale=w_planes[n][:, h, HALF * jj : HALF * (jj + 1)],
+                        rhs_scale=w_plane[:, h, HALF * jp : HALF * (jp + 1)],
                         start=(h == 0),
                         stop=(h == PASSES - 1),
                     )
@@ -217,16 +215,15 @@ def tile_router_weight_gradient_s12_kernel(
             return g_raw[g][:].bitcast(F32).rearrange("p s (h w u) -> p h s u w", h=PASSES, u=2)
 
         def split_pass(g, h, copy):
-            copy(out=g_split[:, h].rearrange("p (s u) w -> p s u w", u=2), in_=grad_words(g)[:, h])
+            copy(out=g_split[h][:].rearrange("p (s u) w -> p s u w", u=2), in_=grad_words(g)[:, h])
 
         def split_piece(g, h, pair, copy):
             rows = slice(2 * pair, 2 * pair + 2)
             copy(out=parted[g][h][pair].rearrange("p (s u) w -> p s u w", u=2), in_=grad_words(g)[:, h, rows])
 
         def split_pair(g, pair):
-            dst = g_split[:].rearrange("p h (s u) w -> p h s u w", u=2)
-            rows = slice(2 * pair, 2 * pair + 2)
-            nc.vector.tensor_copy(out=dst[:, :, rows], in_=grad_words(g)[:, :, rows])
+            for h in range(PASSES):
+                split_piece(g, h, pair, on_vector)
 
         def turn_grad(g, copies, pair_first=False, direct=False):
             for n, copy in enumerate(copies):
@@ -316,6 +313,13 @@ def tile_router_weight_gradient_s12_kernel(
             src, dst, plane = batch[BATCHES[n]]
             quantize(dst[:], plane[:], src[:])
 
+        def quantize_half(member, n):
+            quantize(
+                codes[member][:, HALF * n : HALF * (n + 1)],
+                planes[member][:, HALF * n : HALF * (n + 1)],
+                wide[member][:, HALF * PACK * n : HALF * PACK * (n + 1)],
+            )
+
         def final_passes(dst, j, lo, hi, groups, stop=True):
             n, cols = j // 4, slice(P * (j % 4), P * (j % 4 + 1))
             for g in groups:
@@ -355,34 +359,52 @@ def tile_router_weight_gradient_s12_kernel(
                     stop=(n == WARM_PASSES - 1),
                 )
 
+        def keep_warm():
+            bank = next_bank()
+            for n in range(KEEP_WARM_PASSES):
+                nc.tensor.matmul_mx(
+                    out=bank[:, 0:P],
+                    lhsT=a_codes[0][:, 0, 0, :].bitcast(FP4X4),
+                    lhsT_scale=a_planes[0][:, 0, 0, :],
+                    rhs=a_codes[0][:, 0, 0, :].bitcast(FP4X4),
+                    rhs_scale=a_planes[0][:, 0, 0, :],
+                    start=(n == 0),
+                    stop=(n == KEEP_WARM_PASSES - 1),
+                )
+
         last = GROUPS - 1
+        nc.vector.memset(w_plane[:].bitcast(I32), 0)
         nc.vector.memset(a_sc_first[:], 0)
-        nc.vector.memset(w_planes[0][:].bitcast(I32), 0)
         nc.vector.memset(a_sc_rest[:], 0)
-        nc.vector.memset(w_planes[1][:].bitcast(I32), 0)
         zeros = a_sc_rest[:].rearrange("p h n -> p (h n)").bitcast(BF16)[:, 0 : WARM_N * PACK]
         quantize(warm_codes[:], warm_plane[:], zeros)
         make_identity(nc, ident[:])
-
         load_a(0)
+        load_scales(w_plane[:].bitcast(I32), w_scales, 0, D, PORT_ORDER[:2])
         load_scales(a_sc_first, a_scales, 0, 2 * GROUP)
         load_w(0)
-        load_scales(w_planes[0][:].bitcast(I32), w_scales, 0, 512)
+        load_scales(w_plane[:].bitcast(I32), w_scales, 0, D, PORT_ORDER[2:])
         load_a(1)
         load_values(0)
-        load_balance(nc.sync)
+        load_base(0)
         load_values(1)
-        load_grad(0)
-        load_base()
+        load_base(1)
+        load_grad(0, [0])
+        load_balance(nc.sync)
+        load_grad(0, [1])
+        load_base(2)
         load_w(1)
-        load_scales(w_planes[1][:].bitcast(I32), w_scales, 512, D)
-        load_scales(a_sc_rest, a_scales, 2 * GROUP, T)
+        load_base(3)
         load_grad(1)
-        load_prob(0)
 
         warm_up()
         order_codes(0, on_vector)
         order_scales(0, on_vector)
+        keep_warm()
+        load_a(2)
+        load_prob(0)
+        load_scales(a_sc_rest, a_scales, 2 * GROUP, T)
+        order_scales(1, on_vector)
         order_codes(1, on_vector)
         x_tiles(8)
         interleave_values(0)
@@ -402,39 +424,39 @@ def tile_router_weight_gradient_s12_kernel(
             split_pass(g + 1, 0, on_scalar)
             split_piece(g + 1, 1, 0, on_scalar)
             split_piece(g + 1, 1, 1, on_gpsimd)
-            if g == 0:
-                order_scales(1, on_gpsimd)
+            if g == 1:
+                order_scales(2, on_gpsimd)
+                order_scales(3, on_gpsimd)
             else:
-                order_codes(g + 1, on_gpsimd)
+                order_codes(2 + g // 2, on_gpsimd)
             if g + 2 < GROUPS:
-                load_a(g + 2)
                 load_grad(g + 2)
             load_prob(g + 1)
+            if g == 0:
+                load_a(3)
+            x_tiles(BEFORE[g])
             turn_grad(g + 1, [on_scalar] * 4)
             quantize_batch(2 * g + 1)
             weigh(g, 0)
             quantize_grad(g + 1)
             weigh(g, 1)
-            x_tiles(ROUND[g])
+            x_tiles(ROUND[g] - BEFORE[g])
             quantize_batch(2 * g + 2)
         utilities(last)
         x_tiles(32 - len(made))
         quantize_batch(7)
         weigh(last, 0)
-        weigh(last, 1)
-        quantize_batch(9)
         quantize_batch(8)
-        early = [next_bank() for j in range(EARLY)]
-        for j in range(EARLY):
-            final_passes(early[j][:], j, 0, E, range(last))
-        for j in range(EARLY):
-            final_passes(early[j][:], j, 0, E, [last])
-            store(early[j][:], out_tiles[:, j, :], on_scalar if j % 2 == 0 else on_vector)
-        for j in range(EARLY, 7):
-            bank = next_bank()
-            final_passes(bank[:], j, 0, E, range(GROUPS))
-            store(bank[:], out_tiles[:, j, :], on_scalar if j % 2 == 0 else on_vector)
-        for n in range(2):
-            bank = next_bank()
-            final_passes(bank[:, 0:HALF], 7, HALF * n, HALF * (n + 1), range(GROUPS))
-            store(bank[:, 0:HALF], out_tiles[:, 7, HALF * n : HALF * (n + 1)], on_vector if n == 0 else on_scalar)
+        quantize_half(("L", last), 0)
+        weigh(last, 1)
+        quantize_half(("L", last), 1)
+        banks = [next_bank() for j in range(BANKS)]
+        for g in range(last):
+            for j in range(BANKS):
+                final_passes(banks[j][:, 0:HALF], j, 0, HALF, [g])
+        for j in range(BANKS):
+            final_passes(banks[j][:, 0:HALF], j, 0, HALF, [last])
+            store(banks[j][:, 0:HALF], out_tiles[:, j, 0:HALF], on_scalar)
+        for j in range(BANKS):
+            final_passes(banks[j][:, HALF:E], j, HALF, E, range(GROUPS))
+            store(banks[j][:, HALF:E], out_tiles[:, j, HALF:E], on_vector if j % 2 == 0 else on_scalar)

@@ -25,10 +25,10 @@ HALF = 256
 BANKS = 8
 ALIGN = 64
 WARM_N = 256
-WARM_PASSES = 5
-KEEP_WARM_PASSES = 8
+WARM_PASSES = 6
+KEEP_WARM_PASSES = 4
 PORT_ORDER = (0, 2, 1, 3)
-WIDE = ()
+WIDE = (8, 11, 12)
 ORDER = ((0, 0), (1, 0), (0, 1), (1, 1), (2, 0), (2, 1), (3, 0), (3, 1))
 BATCHES = (((0, 0),), ((1, 0),), ((0, 1),), (("L", 0),), ((1, 1),), (("L", 1), (2, 0)), ((2, 1),), (("L", 2), (3, 0)), ((3, 1),), (("L", 3),))
 NH = 3
@@ -421,8 +421,9 @@ def tile_router_weight_gradient_s12_kernel(
         quantize_batch(0)
         for g in range(last):
             utilities(g)
-            split_pass(g + 1, 0, on_scalar)
-            split_piece(g + 1, 1, 0, on_scalar)
+            if g == 0:
+                split_pass(1, 0, on_scalar)
+                split_piece(1, 1, 0, on_scalar)
             split_piece(g + 1, 1, 1, on_gpsimd)
             if g == 1:
                 order_scales(2, on_gpsimd)
@@ -440,7 +441,11 @@ def tile_router_weight_gradient_s12_kernel(
             weigh(g, 0)
             quantize_grad(g + 1)
             weigh(g, 1)
-            x_tiles(ROUND[g] - BEFORE[g])
+            x_tiles(ROUND[g] - BEFORE[g] - 1)
+            if g + 2 < GROUPS:
+                split_pass(g + 2, 0, on_scalar)
+                split_piece(g + 2, 1, 0, on_scalar)
+            x_tiles(1)
             quantize_batch(2 * g + 2)
         utilities(last)
         x_tiles(32 - len(made))

@@ -28,9 +28,10 @@ WARM_N = 256
 WARM_PASSES = 6
 KEEP_WARM_PASSES = 4
 PORT_ORDER = (0, 2, 1, 3)
-WIDE = (8, 11, 12)
+WIDE = (11, 12)
 ORDER = ((0, 0), (1, 0), (0, 1), (1, 1), (2, 0), (2, 1), (3, 0), (3, 1))
 BATCHES = (((0, 0),), ((1, 0),), ((0, 1),), (("L", 0),), ((1, 1),), (("L", 1), (2, 0)), ((2, 1),), (("L", 2), (3, 0)), ((3, 1),), (("L", 3),))
+SECOND = (3, 4)
 NH = 3
 ROUND = (5, 6, 7)
 BEFORE = (0, 0, 0)
@@ -96,9 +97,9 @@ def tile_router_weight_gradient_s12_kernel(
                 planes[member] = batch[members][2][:, BANK * m : BANK * (m + 1)]
         result = [keep("result%d" % j, [P, HALF], F32) for j in range(12)]
 
-        parted = [[[g_split[h][:, 4 * pair : 4 * pair + 4] for pair in range(2)] for h in range(PASSES)] for g in range(GROUPS)]
+        parted = [[[g_split[h][:, 2 * s : 2 * s + 2] for s in range(PACK)] for h in range(PASSES)] for g in range(GROUPS)]
         for g, member in ((1, (0, 0)), (2, (0, 1)), (3, (1, 1))):
-            parted[g][1][1] = wide[member].bitcast(F32)[:, 0 : 4 * P].rearrange("p (q w) -> p q w", q=4)
+            parted[g][1][3] = wide[member].bitcast(F32)[:, 0 : 2 * P].rearrange("p (u w) -> p u w", u=2)
 
         def load_a(g):
             src = a_words.rearrange("h p n -> p h n")[:, :, 1024 * g : 1024 * (g + 1)]
@@ -214,16 +215,16 @@ def tile_router_weight_gradient_s12_kernel(
         def grad_words(g):
             return g_raw[g][:].bitcast(F32).rearrange("p s (h w u) -> p h s u w", h=PASSES, u=2)
 
-        def split_pass(g, h, copy):
-            copy(out=g_split[h][:].rearrange("p (s u) w -> p s u w", u=2), in_=grad_words(g)[:, h])
+        def split_rows(g, h, lo, hi, copy):
+            dst = g_split[h][:, 2 * lo : 2 * hi].rearrange("p (s u) w -> p s u w", u=2)
+            copy(out=dst, in_=grad_words(g)[:, h, lo:hi])
 
-        def split_piece(g, h, pair, copy):
-            rows = slice(2 * pair, 2 * pair + 2)
-            copy(out=parted[g][h][pair].rearrange("p (s u) w -> p s u w", u=2), in_=grad_words(g)[:, h, rows])
+        def split_last_row(g):
+            nc.gpsimd.tensor_copy(out=parted[g][1][3], in_=grad_words(g)[:, 1, 3])
 
         def split_pair(g, pair):
             for h in range(PASSES):
-                split_piece(g, h, pair, on_vector)
+                split_rows(g, h, 2 * pair, 2 * pair + 2, on_vector)
 
         def turn_grad(g, copies, pair_first=False, direct=False):
             for n, copy in enumerate(copies):
@@ -235,7 +236,7 @@ def tile_router_weight_gradient_s12_kernel(
                     if direct:
                         words = grad_words(g)[:, h, 2 * pair + q // 2, q % 2]
                     else:
-                        words = parted[g][h][pair][:, q, :]
+                        words = parted[g][h][2 * pair + q // 2][:, q % 2, :]
                     nc.tensor.transpose(bank[:, P * q : P * (q + 1)], words, ident[:])
                 dst = g_t[g][:].bitcast(F32).rearrange("p (h t c w) -> p h t c w", h=PASSES, t=PACK, w=8)
                 copy(
@@ -422,9 +423,9 @@ def tile_router_weight_gradient_s12_kernel(
         for g in range(last):
             utilities(g)
             if g == 0:
-                split_pass(1, 0, on_scalar)
-                split_piece(1, 1, 0, on_scalar)
-            split_piece(g + 1, 1, 1, on_gpsimd)
+                split_rows(1, 0, 0, PACK, on_scalar)
+                split_rows(1, 1, 0, PACK - 1, on_scalar)
+            split_last_row(g + 1)
             if g == 1:
                 order_scales(2, on_gpsimd)
                 order_scales(3, on_gpsimd)
@@ -443,25 +444,33 @@ def tile_router_weight_gradient_s12_kernel(
             weigh(g, 1)
             x_tiles(ROUND[g] - BEFORE[g] - 1)
             if g + 2 < GROUPS:
-                split_pass(g + 2, 0, on_scalar)
-                split_piece(g + 2, 1, 0, on_scalar)
+                split_rows(g + 2, 0, 0, PACK, on_scalar)
+                split_rows(g + 2, 1, 0, PACK - 1, on_scalar)
             x_tiles(1)
             quantize_batch(2 * g + 2)
-        utilities(last)
+        first = half_utilities(last, 0)
+        second = half_utilities(last, 1)
         x_tiles(32 - len(made))
+        half_shift(last, 0, first)
         quantize_batch(7)
         weigh(last, 0)
         quantize_batch(8)
         quantize_half(("L", last), 0)
+        half_shift(last, 1, second)
         weigh(last, 1)
-        quantize_half(("L", last), 1)
-        banks = [next_bank() for j in range(BANKS)]
-        for g in range(last):
-            for j in range(BANKS):
-                final_passes(banks[j][:, 0:HALF], j, 0, HALF, [g])
+        turn = [next_bank() for j in range(BANKS)]
+        banks = [bank for bank in range(BANKS) if bank not in SECOND]
+        banks = [turn[bank] for bank in banks + list(SECOND)]
+        for chunk in (range(0, 3), range(3, 6)):
+            for g in range(last):
+                for j in chunk:
+                    final_passes(banks[j][:, 0:HALF], j, 0, HALF, [g])
         for j in range(BANKS):
-            final_passes(banks[j][:, 0:HALF], j, 0, HALF, [last])
+            final_passes(banks[j][:, 0:HALF], j, 0, HALF, [last] if j < 6 else range(GROUPS))
             store(banks[j][:, 0:HALF], out_tiles[:, j, 0:HALF], on_scalar)
+        quantize_half(("L", last), 1)
+        for j in range(4):
+            final_passes(banks[j][:, HALF:E], j, HALF, E, range(last))
         for j in range(BANKS):
-            final_passes(banks[j][:, HALF:E], j, HALF, E, range(GROUPS))
+            final_passes(banks[j][:, HALF:E], j, HALF, E, [last] if j < 4 else range(GROUPS))
             store(banks[j][:, HALF:E], out_tiles[:, j, HALF:E], on_vector if j % 2 == 0 else on_scalar)

@@ -24,17 +24,15 @@ BANK = 512
 HALF = 256
 BANKS = 8
 ALIGN = 64
-WARM_N = 256
-WARM_PASSES = 6
-KEEP_WARM_PASSES = 4
+WARM_N = 512
 PORT_ORDER = (0, 2, 1, 3)
-WIDE = (11, 12)
-ORDER = ((0, 0), (1, 0), (0, 1), (1, 1), (2, 0), (2, 1), (3, 0), (3, 1))
-BATCHES = (((0, 0),), ((1, 0),), ((0, 1),), (("L", 0),), ((1, 1),), (("L", 1), (2, 0)), ((2, 1),), (("L", 2), (3, 0)), ((3, 1),), (("L", 3),))
+WIDE = ()
+ORDER = ((0, 0), (0, 1), (1, 0), (1, 1), (2, 0), (2, 1), (3, 0), (3, 1))
+BATCHES = (((0, 0),), ((0, 1),), ((1, 0),), (("L", 0),), ((1, 1),), (("L", 1), (2, 0)), ((2, 1),), (("L", 2), (3, 0)), ((3, 1),), (("L", 3),))
 SECOND = (3, 4)
 NH = 3
-ROUND = (5, 6, 7)
-BEFORE = (0, 0, 0)
+ROUND = (6, 7, 7)
+AHEAD = (1, 4, 0)
 
 
 def tile_router_weight_gradient_s12_kernel(
@@ -98,8 +96,14 @@ def tile_router_weight_gradient_s12_kernel(
         result = [keep("result%d" % j, [P, HALF], F32) for j in range(12)]
 
         parted = [[[g_split[h][:, 2 * s : 2 * s + 2] for s in range(PACK)] for h in range(PASSES)] for g in range(GROUPS)]
-        for g, member in ((1, (0, 0)), (2, (0, 1)), (3, (1, 1))):
+        for g, member in ((1, (0, 0)), (2, (1, 0))):
             parted[g][1][3] = wide[member].bitcast(F32)[:, 0 : 2 * P].rearrange("p (u w) -> p u w", u=2)
+
+        last = GROUPS - 1
+        turned = g_raw[0][:].rearrange("p s d -> p (s d)").bitcast(F32)[:, 0 : 8 * P]
+        halves = g_raw[last][:].rearrange("p s d -> p (s d)")
+        last_rows = halves[:, 0 : PACK * GROUP].rearrange("p (s d) -> p s d", s=PACK)
+        last_blocks = halves[:, PACK * GROUP : 2 * PACK * GROUP].rearrange("p (b e) -> p b e", e=P)
 
         def load_a(g):
             src = a_words.rearrange("h p n -> p h n")[:, :, 1024 * g : 1024 * (g + 1)]
@@ -118,6 +122,13 @@ def tile_router_weight_gradient_s12_kernel(
             rows = grad[GROUP * g : GROUP * (g + 1), :].rearrange("(m s) d -> m s d", s=PACK)
             for pair in pairs:
                 nc.sync.dma_start(out=g_raw[g][:, 2 * pair : 2 * pair + 2, :], in_=rows[:, 2 * pair : 2 * pair + 2, :])
+
+        def load_last_grad():
+            rows = grad[GROUP * last : GROUP * (last + 1), :]
+            nc.sync.dma_start(out=last_rows, in_=rows[:, 0:GROUP].rearrange("(m s) d -> m s d", s=PACK))
+            slices = rows[:, GROUP:D].rearrange("(b j) (q e) -> q j b e", j=32, q=4)
+            for q in PORT_ORDER:
+                nc.sync.dma_start(out=last_blocks[32 * q : 32 * (q + 1)], in_=slices[q])
 
         def load_values(h):
             rows = values[GROUP * h : GROUP * (h + 1), :].rearrange("(p j) e -> p j e", j=PACK)
@@ -226,23 +237,32 @@ def tile_router_weight_gradient_s12_kernel(
             for h in range(PASSES):
                 split_rows(g, h, 2 * pair, 2 * pair + 2, on_vector)
 
-        def turn_grad(g, copies, pair_first=False, direct=False):
-            for n, copy in enumerate(copies):
-                h, pair = divmod(n, 2)
-                if pair_first:
-                    h, pair = pair, h
+        def turn_grad(g, copies, pieces=((0, 0), (0, 1), (1, 0), (1, 1))):
+            for (h, pair), copy in zip(pieces, copies):
                 bank = next_bank()
                 for q in range(4):
-                    if direct:
-                        words = grad_words(g)[:, h, 2 * pair + q // 2, q % 2]
-                    else:
-                        words = parted[g][h][2 * pair + q // 2][:, q % 2, :]
+                    words = parted[g][h][2 * pair + q // 2][:, q % 2, :]
                     nc.tensor.transpose(bank[:, P * q : P * (q + 1)], words, ident[:])
                 dst = g_t[g][:].bitcast(F32).rearrange("p (h t c w) -> p h t c w", h=PASSES, t=PACK, w=8)
                 copy(
                     out=dst[:, h, :, :, 4 * pair : 4 * pair + 4],
                     in_=bank[:].rearrange("p (q c t) -> p t c q", q=4, t=PACK),
                 )
+
+        def split_last():
+            blocks = last_blocks.bitcast(F32).rearrange("p b (i u) -> p u b i", u=2)
+            dst = g_split[1][:].rearrange("p q w -> p (q w)").rearrange("p (u b i) -> p u b i", u=2, i=32)
+            nc.scalar.copy(out=dst, in_=blocks)
+            rows = last_rows.bitcast(F32).rearrange("p s (w u) -> p s u w", u=2)
+            nc.scalar.copy(out=g_split[0][:].rearrange("p (s u) w -> p s u w", u=2), in_=rows)
+
+        def turn_blocks():
+            nc.vector.transpose(out=turned, in_=g_split[1][:].rearrange("p q w -> p (q w)"))
+
+        def join_blocks(lo, hi, copy):
+            dst = g_t[last][:].bitcast(F32).rearrange("p (h t c s u) -> p h t c s u", h=PASSES, t=PACK, s=PACK, u=2)
+            src = turned.rearrange("p (u c t s) -> p t c s u", u=2, t=PACK, s=PACK)
+            copy(out=dst[:, 1, lo:hi], in_=src[:, lo:hi])
 
         def interleave_values(h):
             nc.vector.tensor_copy(
@@ -347,9 +367,9 @@ def tile_router_weight_gradient_s12_kernel(
         out_tiles = out.rearrange("(j p) e -> p j e", p=P)
         on_vector, on_scalar, on_gpsimd = nc.vector.tensor_copy, nc.scalar.copy, nc.gpsimd.tensor_copy
 
-        def warm_up():
+        def warm_up(count):
             bank = next_bank()
-            for n in range(WARM_PASSES):
+            for n in range(count):
                 nc.tensor.matmul_mx(
                     out=bank[:, 0:WARM_N],
                     lhsT=warm_codes[:, 0:P].bitcast(FP8X4),
@@ -357,97 +377,100 @@ def tile_router_weight_gradient_s12_kernel(
                     rhs=warm_codes[:].bitcast(FP8X4),
                     rhs_scale=warm_plane[:],
                     start=(n == 0),
-                    stop=(n == WARM_PASSES - 1),
+                    stop=(n == count - 1),
                 )
 
-        def keep_warm():
-            bank = next_bank()
-            for n in range(KEEP_WARM_PASSES):
-                nc.tensor.matmul_mx(
-                    out=bank[:, 0:P],
-                    lhsT=a_codes[0][:, 0, 0, :].bitcast(FP4X4),
-                    lhsT_scale=a_planes[0][:, 0, 0, :],
-                    rhs=a_codes[0][:, 0, 0, :].bitcast(FP4X4),
-                    rhs_scale=a_planes[0][:, 0, 0, :],
-                    start=(n == 0),
-                    stop=(n == KEEP_WARM_PASSES - 1),
-                )
-
-        last = GROUPS - 1
         nc.vector.memset(w_plane[:].bitcast(I32), 0)
         nc.vector.memset(a_sc_first[:], 0)
+        nc.vector.memset(ident[:], 0.0)
+        nc.vector.memset(v_t[0][:].bitcast(I32), 0)
+        make_identity(nc, ident[:], nomemset=True)
         nc.vector.memset(a_sc_rest[:], 0)
-        zeros = a_sc_rest[:].rearrange("p h n -> p (h n)").bitcast(BF16)[:, 0 : WARM_N * PACK]
-        quantize(warm_codes[:], warm_plane[:], zeros)
-        make_identity(nc, ident[:])
-        load_a(0)
-        load_scales(w_plane[:].bitcast(I32), w_scales, 0, D, PORT_ORDER[:2])
-        load_scales(a_sc_first, a_scales, 0, 2 * GROUP)
-        load_w(0)
-        load_scales(w_plane[:].bitcast(I32), w_scales, 0, D, PORT_ORDER[2:])
-        load_a(1)
-        load_values(0)
-        load_base(0)
-        load_values(1)
-        load_base(1)
+        quantize(warm_codes[:], warm_plane[:], v_t[0][:])
         load_grad(0, [0])
-        load_balance(nc.sync)
+        load_scales(w_plane[:].bitcast(I32), w_scales, 0, D, (0, 2))
+        load_scales(a_sc_first, a_scales, 0, 2 * GROUP, (0, 2))
         load_grad(0, [1])
-        load_base(2)
+        load_a(0)
+        load_scales(a_sc_first, a_scales, 0, 2 * GROUP, (1,))
+        load_balance(nc.sync)
+        load_scales(a_sc_first, a_scales, 0, 2 * GROUP, (3,))
+        load_w(0)
+        load_scales(w_plane[:].bitcast(I32), w_scales, 0, D, (1, 3))
+        load_values(0)
         load_w(1)
+        load_values(1)
+        load_base(0)
+        load_a(1)
+        load_base(1)
+        load_grad(1, [0])
+        load_base(2)
         load_base(3)
-        load_grad(1)
+        load_grad(1, [1])
 
-        warm_up()
+        warm_up(3)
+        split_pair(0, 0)
+        turn_grad(0, [on_scalar] * 2, ((0, 0), (1, 0)))
+        warm_up(2)
+        split_pair(0, 1)
+        turn_grad(0, [on_scalar] * 2, ((0, 1), (1, 1)))
+        spread_balance()
         order_codes(0, on_vector)
         order_scales(0, on_vector)
-        keep_warm()
         load_a(2)
         load_prob(0)
         load_scales(a_sc_rest, a_scales, 2 * GROUP, T)
         order_scales(1, on_vector)
-        order_codes(1, on_vector)
         x_tiles(8)
-        interleave_values(0)
-        interleave_values(1)
-        split_pair(0, 0)
-        quantize_values(0)
-        split_pair(0, 1)
-        quantize_values(1)
-        turn_grad(0, [on_scalar, on_scalar, on_vector, on_scalar], pair_first=True)
-        spread_balance()
-        x_tiles(NH)
         quantize_grad(0, 0, 1)
+        interleave_values(0)
         quantize_grad(0, 1, 2)
+        interleave_values(1)
+        quantize_values(0)
+        order_codes(1, on_vector)
+        quantize_values(1)
+        x_tiles(1)
         quantize_batch(0)
         for g in range(last):
             utilities(g)
             if g == 0:
                 split_rows(1, 0, 0, PACK, on_scalar)
                 split_rows(1, 1, 0, PACK - 1, on_scalar)
-            split_last_row(g + 1)
+            if g + 1 < last:
+                split_last_row(g + 1)
+            else:
+                join_blocks(PACK - 1, PACK, on_gpsimd)
+                join_blocks(0, PACK - 1, on_scalar)
             if g == 1:
                 order_scales(2, on_gpsimd)
                 order_scales(3, on_gpsimd)
             else:
                 order_codes(2 + g // 2, on_gpsimd)
-            if g + 2 < GROUPS:
-                load_grad(g + 2)
-            load_prob(g + 1)
             if g == 0:
+                load_grad(2)
+                load_prob(1)
                 load_a(3)
-            x_tiles(BEFORE[g])
-            turn_grad(g + 1, [on_scalar] * 4)
+                load_last_grad()
+            else:
+                load_prob(g + 1)
+            if g + 1 < last:
+                turn_grad(g + 1, [on_scalar] * 4)
+            else:
+                turn_grad(last, [on_scalar] * 2, ((0, 0), (0, 1)))
             quantize_batch(2 * g + 1)
             weigh(g, 0)
             quantize_grad(g + 1)
             weigh(g, 1)
-            x_tiles(ROUND[g] - BEFORE[g] - 1)
-            if g + 2 < GROUPS:
-                split_rows(g + 2, 0, 0, PACK, on_scalar)
-                split_rows(g + 2, 1, 0, PACK - 1, on_scalar)
-            x_tiles(1)
+            x_tiles(ROUND[g] - AHEAD[g])
+            if g == 0:
+                split_rows(2, 0, 0, PACK, on_scalar)
+                split_rows(2, 1, 0, PACK - 1, on_scalar)
+            if g == 1:
+                split_last()
+            x_tiles(AHEAD[g])
             quantize_batch(2 * g + 2)
+            if g == 1:
+                turn_blocks()
         first = half_utilities(last, 0)
         second = half_utilities(last, 1)
         x_tiles(32 - len(made))

@@ -19,20 +19,36 @@ P = 128
 PACK = 4
 GROUP = P * PACK
 GROUPS = T // GROUP
+LAST = GROUPS - 1
 PASSES = 2
 BANK = 512
-HALF = 256
 BANKS = 8
+HALF = E // 2
 ALIGN = 64
-WARM_N = 512
-PORT_ORDER = (0, 2, 1, 3)
-WIDE = ()
-ORDER = ((0, 0), (0, 1), (1, 0), (1, 1), (2, 0), (2, 1), (3, 0), (3, 1))
-BATCHES = (((0, 0),), ((0, 1),), ((1, 0),), (("L", 0),), ((1, 1),), (("L", 1), (2, 0)), ((2, 1),), (("L", 2), (3, 0)), ((3, 1),), (("L", 3),))
-SECOND = (3, 4)
-NH = 3
-ROUND = (6, 7, 7)
-AHEAD = (1, 4, 0)
+TILES = D // P
+X_TILES = GROUPS * TILES
+PIECE = 4
+QUADRANTS = (0, 2, 1, 3)
+HEAD_TILES = 9
+ROUND_TILES = (6, 7, 7)
+PART_AHEAD = (1, 4)
+EARLY_FIRST = BANKS - 2
+EARLY_SECOND = 4
+STORE_BUFFERS = 12
+WARM_N = 256
+WARM_PASSES = (5, 2)
+CALLS = (
+    ((0, 0),),
+    ((0, 1),),
+    ((1, 0),),
+    (("L", 0),),
+    ((1, 1),),
+    (("L", 1), (2, 0)),
+    ((2, 1),),
+    (("L", 2), (3, 0)),
+    ((3, 1),),
+    (("L", 3),),
+)
 
 
 def tile_router_weight_gradient_s12_kernel(
@@ -43,6 +59,7 @@ def tile_router_weight_gradient_s12_kernel(
         sb = ctx.enter_context(tc.tile_pool(name="sb", bufs=1))
         psum = ctx.enter_context(tc.psum_pool(name="psum", bufs=1))
         ctx.enter_context(tc.manual_schedule())
+        on_vector, on_scalar, on_gpsimd = nc.vector.tensor_copy, nc.scalar.copy, nc.gpsimd.tensor_copy
 
         def keep(name, shape, dtype):
             return sb.tile(shape, dtype, name=name, align_bytes=ALIGN)
@@ -51,9 +68,8 @@ def tile_router_weight_gradient_s12_kernel(
 
         def next_bank():
             n = len(taken)
-            bank = psum.tile([P, BANK], F32, name="bank%d" % n, tag="bank%d" % (n % BANKS))
-            taken.append(bank)
-            return bank
+            taken.append(psum.tile([P, BANK], F32, name="bank%d" % n, tag="bank%d" % (n % BANKS)))
+            return taken[n]
 
         ident = keep("ident", [P, P], F32)
         bal_col = keep("bal_col", [P, PACK], BF16)
@@ -63,75 +79,82 @@ def tile_router_weight_gradient_s12_kernel(
         base_sb = keep("base_sb", [P, GROUPS, 16], BF16)
 
         a_raw = [keep("a_raw%d" % g, [P, PASSES, 256], I32) for g in range(2)] * 2
-        a_codes = [keep("a_codes%d" % g, [P, PACK, PASSES, 256], U8) for g in range(GROUPS)]
-        a_sc_first = keep("a_sc_first", [P, PASSES, 256], I32)
-        a_sc_rest = keep("a_sc_rest", [P, PASSES, 256], I32)
+        a_codes = [keep("a_codes%d" % g, [P, PACK, PASSES, 2 * P], U8) for g in range(GROUPS)]
+        a_staged = [keep("a_staged%d" % n, [P, PASSES, 256], I32) for n in range(2)]
         a_planes = [keep("a_plane%d" % g, [P, PACK, PASSES, P], U8) for g in range(GROUPS)]
-        w_codes = [keep("w_codes%d" % n, [P, PASSES, 1024], U8) for n in range(2)]
+        w_codes = [keep("w_codes%d" % n, [P, PASSES, D], U8) for n in range(2)]
         w_plane = keep("w_plane", [P, PASSES, D], U8)
 
         g_raw = [keep("g_raw%d" % g, [P, PACK, D], BF16) for g in range(2)] * 2
-        g_split = [keep("g_split%d" % h, [P, 8, P], F32) for h in range(PASSES)]
-        g_t = [keep("g_t%d" % g, [P, PASSES * GROUP * PACK], BF16) for g in range(2)] * 2
+        g_parted = [keep("g_parted%d" % h, [P, 2 * PACK, P], F32) for h in range(PASSES)]
+        g_wide = [keep("g_wide%d" % g, [P, PASSES * GROUP * PACK], BF16) for g in range(2)] * 2
         g_codes = [keep("g_codes%d" % g, [P, PASSES * GROUP], U32) for g in range(2)] * 2
         g_planes = [keep("g_plane%d" % g, [P, PASSES * GROUP], U8) for g in range(2)] * 2
         v_raw = [keep("v_raw%d" % h, [P, PACK, E], BF16) for h in range(PASSES)]
-        v_t = [keep("v_t%d" % h, [P, E * PACK], BF16) for h in range(PASSES)]
+        v_wide = [keep("v_wide%d" % h, [P, E * PACK], BF16) for h in range(PASSES)]
         v_codes = [keep("v_codes%d" % h, [P, E], U32) for h in range(PASSES)]
         v_planes = [keep("v_plane%d" % h, [P, E], U8) for h in range(PASSES)]
         p_sb = [keep("p_sb%d" % g, [P, PACK, E], BF16) for g in range(GROUPS)]
         shifted = [keep("shifted%d" % n, [P, E * PACK], F32) for n in range(2)]
-        wide, codes, planes, batch = {}, {}, {}, {}
-        for n, members in enumerate(BATCHES):
-            k = len(members)
-            batch[members] = (
-                keep("wide%d" % n, [P, k * BANK * PACK], BF16),
-                keep("codes%d" % n, [P, k * BANK], U32),
-                keep("plane%d" % n, [P, k * BANK], U8),
+
+        wide, codes, planes, call_tiles = {}, {}, {}, []
+        for n, members in enumerate(CALLS):
+            width = len(members) * BANK
+            call_tiles.append(
+                (
+                    keep("wide%d" % n, [P, width * PACK], BF16),
+                    keep("codes%d" % n, [P, width], U32),
+                    keep("plane%d" % n, [P, width], U8),
+                )
             )
             for m, member in enumerate(members):
-                wide[member] = batch[members][0][:, BANK * PACK * m : BANK * PACK * (m + 1)]
-                codes[member] = batch[members][1][:, BANK * m : BANK * (m + 1)]
-                planes[member] = batch[members][2][:, BANK * m : BANK * (m + 1)]
-        result = [keep("result%d" % j, [P, HALF], F32) for j in range(12)]
+                wide[member] = call_tiles[n][0][:, BANK * PACK * m : BANK * PACK * (m + 1)]
+                codes[member] = call_tiles[n][1][:, BANK * m : BANK * (m + 1)]
+                planes[member] = call_tiles[n][2][:, BANK * m : BANK * (m + 1)]
+        staged_out = [keep("staged_out%d" % n, [P, HALF], F32) for n in range(STORE_BUFFERS)]
 
-        parted = [[[g_split[h][:, 2 * s : 2 * s + 2] for s in range(PACK)] for h in range(PASSES)] for g in range(GROUPS)]
-        for g, member in ((1, (0, 0)), (2, (1, 0))):
-            parted[g][1][3] = wide[member].bitcast(F32)[:, 0 : 2 * P].rearrange("p (u w) -> p u w", u=2)
+        parted = [[[g_parted[h][:, 2 * s : 2 * s + 2] for s in range(PACK)] for h in range(PASSES)] for g in range(GROUPS)]
+        for g in (1, 2):
+            spent = wide[CALLS[2 * g - 2][0]].bitcast(F32)
+            parted[g][1][PACK - 1] = spent[:, 0 : 2 * P].rearrange("p (u w) -> p u w", u=2)
 
-        last = GROUPS - 1
-        turned = g_raw[0][:].rearrange("p s d -> p (s d)").bitcast(F32)[:, 0 : 8 * P]
-        halves = g_raw[last][:].rearrange("p s d -> p (s d)")
-        last_rows = halves[:, 0 : PACK * GROUP].rearrange("p (s d) -> p s d", s=PACK)
-        last_blocks = halves[:, PACK * GROUP : 2 * PACK * GROUP].rearrange("p (b e) -> p b e", e=P)
+        last_raw = g_raw[LAST][:].rearrange("p s d -> p (s d)")
+        last_rows = last_raw[:, 0 : PACK * GROUP].rearrange("p (s d) -> p s d", s=PACK)
+        last_slices = last_raw[:, PACK * GROUP : 2 * PACK * GROUP].rearrange("p (b e) -> p b e", e=P)
+        turned = g_raw[LAST - 1][:].rearrange("p s d -> p (s d)").bitcast(F32)[:, 0 : 2 * GROUP]
 
         def load_a(g):
-            src = a_words.rearrange("h p n -> p h n")[:, :, 1024 * g : 1024 * (g + 1)]
+            src = a_words.rearrange("h p n -> p h n")[:, :, 2 * GROUP * g : 2 * GROUP * (g + 1)]
             nc.sync.dma_start(out=a_raw[g][:], in_=src.bitcast(I32))
 
-        def load_scales(dst, scales, lo, hi, quadrants=PORT_ORDER, queue=nc.sync):
+        def load_scale_rows(dst, scales, lo, hi, quadrants):
             for q in quadrants:
                 src = scales.rearrange("h r n -> r h n")[4 * q : 4 * q + 4, :, lo:hi]
-                queue.dma_start(out=dst[32 * q : 32 * q + 4], in_=src.bitcast(I32))
+                nc.sync.dma_start(out=dst[32 * q : 32 * q + 4], in_=src.bitcast(I32))
+
+        def load_a_scales(n, quadrants):
+            load_scale_rows(a_staged[n], a_scales, 2 * GROUP * n, 2 * GROUP * (n + 1), quadrants)
+
+        def load_w_scales(quadrants):
+            load_scale_rows(w_plane[:].bitcast(I32), w_scales, 0, D, quadrants)
 
         def load_w(n):
-            src = w_words.rearrange("h p n -> p h n")[:, :, 1024 * n : 1024 * (n + 1)]
+            src = w_words.rearrange("h p n -> p h n")[:, :, D * n : D * (n + 1)]
             nc.sync.dma_start(out=w_codes[n][:].bitcast(I32), in_=src.bitcast(I32))
 
-        def load_grad(g, pairs=range(2)):
+        def load_grad(g, pair):
             rows = grad[GROUP * g : GROUP * (g + 1), :].rearrange("(m s) d -> m s d", s=PACK)
-            for pair in pairs:
-                nc.sync.dma_start(out=g_raw[g][:, 2 * pair : 2 * pair + 2, :], in_=rows[:, 2 * pair : 2 * pair + 2, :])
+            nc.sync.dma_start(out=g_raw[g][:, 2 * pair : 2 * pair + 2, :], in_=rows[:, 2 * pair : 2 * pair + 2, :])
 
         def load_last_grad():
-            rows = grad[GROUP * last : GROUP * (last + 1), :]
+            rows = grad[GROUP * LAST : GROUP * (LAST + 1), :]
             nc.sync.dma_start(out=last_rows, in_=rows[:, 0:GROUP].rearrange("(m s) d -> m s d", s=PACK))
             slices = rows[:, GROUP:D].rearrange("(b j) (q e) -> q j b e", j=32, q=4)
-            for q in PORT_ORDER:
-                nc.sync.dma_start(out=last_blocks[32 * q : 32 * (q + 1)], in_=slices[q])
+            for q in QUADRANTS:
+                nc.sync.dma_start(out=last_slices[32 * q : 32 * (q + 1)], in_=slices[q])
 
         def load_values(h):
-            rows = values[GROUP * h : GROUP * (h + 1), :].rearrange("(p j) e -> p j e", j=PACK)
+            rows = values[GROUP * h : GROUP * (h + 1), :].rearrange("(p t) e -> p t e", t=PACK)
             nc.sync.dma_start(out=v_raw[h][:], in_=rows)
 
         def load_prob(g):
@@ -143,8 +166,8 @@ def tile_router_weight_gradient_s12_kernel(
             rows = base.rearrange("(g c w) -> c g w", g=GROUPS, w=16)
             nc.sync.dma_start(out=base_sb[s:P:PACK, :, 0:13], in_=rows[:, :, s : s + 13])
 
-        def load_balance(queue):
-            queue.dma_start(out=bal_col[:], in_=balance.rearrange("(p j) -> p j", j=PACK))
+        def load_balance():
+            nc.sync.dma_start(out=bal_col[:], in_=balance.rearrange("(p j) -> p j", j=PACK))
 
         def order_codes(g, copy):
             copy(
@@ -153,11 +176,11 @@ def tile_router_weight_gradient_s12_kernel(
             )
 
         def order_scales(g, copy):
-            staged = (a_sc_first, a_sc_rest)[g // 2][:, :, 128 * (g % 2) : 128 * (g % 2 + 1)]
+            staged = a_staged[g // 2][:, :, P * (g % 2) : P * (g % 2 + 1)]
             copy(out=a_planes[g][:].bitcast(I32), in_=staged.rearrange("p h (c t) -> p t h c", t=PACK))
 
-        def quantize(codes, plane, src):
-            nc.vector.quantize_mx(out=codes.bitcast(FP8X4), scales=plane, in_=src)
+        def quantize(dst, plane, src):
+            nc.vector.quantize_mx(out=dst.bitcast(FP8X4), scales=plane, in_=src)
 
         def spread_balance():
             bank = next_bank()
@@ -169,113 +192,83 @@ def tile_router_weight_gradient_s12_kernel(
                 in_=bank[:, 0 : 2 * P].bitcast(BF16).rearrange("p (u n e) -> p n u e", u=2, e=2),
             )
 
-        def x_narrow(unit):
-            g, j = divmod(unit, 8)
-            n, jj = divmod(j, 4)
-            bank = next_bank()
-            for t in range(PACK):
-                for h in range(PASSES):
-                    nc.tensor.matmul_mx(
-                        out=bank[:, P * t : P * (t + 1)],
-                        lhsT=a_codes[g][:, t, h, :].bitcast(FP4X4),
-                        lhsT_scale=a_planes[g][:, t, h, :],
-                        rhs=w_codes[n][:, h, 256 * jj : 256 * (jj + 1)].bitcast(FP4X4),
-                        rhs_scale=w_plane[:, h, P * j : P * (j + 1)],
-                        start=(h == 0),
-                        stop=(h == PASSES - 1),
-                    )
-            nc.scalar.copy(
-                out=wide[g, n][:, BANK * jj : BANK * (jj + 1)].rearrange("p (d t) -> p d t", t=PACK),
-                in_=bank[:].rearrange("p (t d) -> p d t", t=PACK),
-            )
-
-        def x_wide(unit):
-            g, rest = divmod(unit, 8)
-            jp, pair = divmod(rest, 2)
-            n, jj = divmod(jp, 2)
-            bank = next_bank()
-            for u in range(2):
-                for h in range(PASSES):
-                    nc.tensor.matmul_mx(
-                        out=bank[:, HALF * u : HALF * (u + 1)],
-                        lhsT=a_codes[g][:, 2 * pair + u, h, :].bitcast(FP4X4),
-                        lhsT_scale=a_planes[g][:, 2 * pair + u, h, :],
-                        rhs=w_codes[n][:, h, 512 * jj : 512 * (jj + 1)].bitcast(FP4X4),
-                        rhs_scale=w_plane[:, h, HALF * jp : HALF * (jp + 1)],
-                        start=(h == 0),
-                        stop=(h == PASSES - 1),
-                    )
-            dst = wide[g, n][:, 1024 * jj : 1024 * (jj + 1)].rearrange("p (d t) -> p d t", t=PACK)
-            nc.scalar.copy(
-                out=dst[:, :, 2 * pair : 2 * pair + 2],
-                in_=bank[:].rearrange("p (u d) -> p d u", u=2),
-            )
-
         made = []
-        units = [8 * g + 4 * n + jj for g, n in ORDER for jj in range(4)]
 
         def x_tiles(count):
-            for n in range(count):
-                unit = units[len(made)]
-                made.append(unit)
-                if unit // 2 in WIDE:
-                    x_wide(unit)
-                else:
-                    x_narrow(unit)
+            for tile in range(len(made), len(made) + count):
+                made.append(tile)
+                g, j = divmod(tile, TILES)
+                n, jj = divmod(j, PIECE)
+                bank = next_bank()
+                for t in range(PACK):
+                    for h in range(PASSES):
+                        nc.tensor.matmul_mx(
+                            out=bank[:, P * t : P * (t + 1)],
+                            lhsT=a_codes[g][:, t, h, :].bitcast(FP4X4),
+                            lhsT_scale=a_planes[g][:, t, h, :],
+                            rhs=w_codes[n][:, h, 2 * P * jj : 2 * P * (jj + 1)].bitcast(FP4X4),
+                            rhs_scale=w_plane[:, h, P * j : P * (j + 1)],
+                            start=(h == 0),
+                            stop=(h == PASSES - 1),
+                        )
+                nc.scalar.copy(
+                    out=wide[g, n][:, BANK * jj : BANK * (jj + 1)].rearrange("p (d t) -> p d t", t=PACK),
+                    in_=bank[:].rearrange("p (t d) -> p d t", t=PACK),
+                )
 
         def grad_words(g):
             return g_raw[g][:].bitcast(F32).rearrange("p s (h w u) -> p h s u w", h=PASSES, u=2)
 
-        def split_rows(g, h, lo, hi, copy):
-            dst = g_split[h][:, 2 * lo : 2 * hi].rearrange("p (s u) w -> p s u w", u=2)
+        def part_rows(g, h, lo, hi, copy):
+            dst = g_parted[h][:, 2 * lo : 2 * hi].rearrange("p (s u) w -> p s u w", u=2)
             copy(out=dst, in_=grad_words(g)[:, h, lo:hi])
 
-        def split_last_row(g):
-            nc.gpsimd.tensor_copy(out=parted[g][1][3], in_=grad_words(g)[:, 1, 3])
+        def part_on_scalar(g):
+            part_rows(g, 0, 0, PACK, on_scalar)
+            part_rows(g, 1, 0, PACK - 1, on_scalar)
 
-        def split_pair(g, pair):
-            for h in range(PASSES):
-                split_rows(g, h, 2 * pair, 2 * pair + 2, on_vector)
+        def part_on_gpsimd(g):
+            on_gpsimd(out=parted[g][1][PACK - 1], in_=grad_words(g)[:, 1, PACK - 1])
 
-        def turn_grad(g, copies, pieces=((0, 0), (0, 1), (1, 0), (1, 1))):
-            for (h, pair), copy in zip(pieces, copies):
-                bank = next_bank()
-                for q in range(4):
-                    words = parted[g][h][2 * pair + q // 2][:, q % 2, :]
-                    nc.tensor.transpose(bank[:, P * q : P * (q + 1)], words, ident[:])
-                dst = g_t[g][:].bitcast(F32).rearrange("p (h t c w) -> p h t c w", h=PASSES, t=PACK, w=8)
-                copy(
-                    out=dst[:, h, :, :, 4 * pair : 4 * pair + 4],
-                    in_=bank[:].rearrange("p (q c t) -> p t c q", q=4, t=PACK),
-                )
-
-        def split_last():
-            blocks = last_blocks.bitcast(F32).rearrange("p b (i u) -> p u b i", u=2)
-            dst = g_split[1][:].rearrange("p q w -> p (q w)").rearrange("p (u b i) -> p u b i", u=2, i=32)
-            nc.scalar.copy(out=dst, in_=blocks)
+        def part_last():
+            slices = last_slices.bitcast(F32).rearrange("p b (i u) -> p u b i", u=2)
+            dst = g_parted[1][:].rearrange("p q w -> p (q w)").rearrange("p (u b i) -> p u b i", u=2, i=32)
+            nc.scalar.copy(out=dst, in_=slices)
             rows = last_rows.bitcast(F32).rearrange("p s (w u) -> p s u w", u=2)
-            nc.scalar.copy(out=g_split[0][:].rearrange("p (s u) w -> p s u w", u=2), in_=rows)
+            nc.scalar.copy(out=g_parted[0][:].rearrange("p (s u) w -> p s u w", u=2), in_=rows)
 
-        def turn_blocks():
-            nc.vector.transpose(out=turned, in_=g_split[1][:].rearrange("p q w -> p (q w)"))
+        def turn_on_tensor(g, h, pair):
+            bank = next_bank()
+            for q in range(4):
+                words = parted[g][h][2 * pair + q // 2][:, q % 2, :]
+                nc.tensor.transpose(bank[:, P * q : P * (q + 1)], words, ident[:])
+            dst = g_wide[g][:].bitcast(F32).rearrange("p (h t c w) -> p h t c w", h=PASSES, t=PACK, w=8)
+            nc.scalar.copy(
+                out=dst[:, h, :, :, 4 * pair : 4 * pair + 4],
+                in_=bank[:].rearrange("p (q c t) -> p t c q", q=4, t=PACK),
+            )
 
-        def join_blocks(lo, hi, copy):
-            dst = g_t[last][:].bitcast(F32).rearrange("p (h t c s u) -> p h t c s u", h=PASSES, t=PACK, s=PACK, u=2)
+        def turn_on_vector():
+            nc.vector.transpose(out=turned, in_=g_parted[1][:].rearrange("p q w -> p (q w)"))
+
+        def join_turned(lo, hi, copy):
+            dst = g_wide[LAST][:].bitcast(F32).rearrange("p (h t c s u) -> p h t c s u", h=PASSES, t=PACK, s=PACK, u=2)
             src = turned.rearrange("p (u c t s) -> p t c s u", u=2, t=PACK, s=PACK)
             copy(out=dst[:, 1, lo:hi], in_=src[:, lo:hi])
 
         def interleave_values(h):
             nc.vector.tensor_copy(
-                out=v_t[h][:].rearrange("p (c i t) -> p c t i", i=4, t=PACK),
+                out=v_wide[h][:].rearrange("p (c i t) -> p c t i", i=4, t=PACK),
                 in_=v_raw[h][:].rearrange("p t (c i) -> p c t i", i=4),
             )
 
         def utility_passes(g, t, dst, lo, hi):
             for h in range(PASSES):
+                tokens = slice(GROUP * h + P * t, GROUP * h + P * (t + 1))
                 nc.tensor.matmul_mx(
                     out=dst,
-                    lhsT=g_codes[g][:, GROUP * h + P * t : GROUP * h + P * (t + 1)].bitcast(FP8X4),
-                    lhsT_scale=g_planes[g][:, GROUP * h + P * t : GROUP * h + P * (t + 1)],
+                    lhsT=g_codes[g][:, tokens].bitcast(FP8X4),
+                    lhsT_scale=g_planes[g][:, tokens],
                     rhs=v_codes[h][:, lo:hi].bitcast(FP8X4),
                     rhs_scale=v_planes[h][:, lo:hi],
                     start=(h == 0),
@@ -299,18 +292,19 @@ def tile_router_weight_gradient_s12_kernel(
                 utility_passes(g, t, bank[:], 0, E)
                 shift(g, t, bank[:], 0, E)
 
-        def half_utilities(g, n):
+        def last_utilities(n):
             banks = [next_bank() for pair in range(2)]
+            parts = [banks[t // 2][:, HALF * (t % 2) : HALF * (t % 2 + 1)] for t in range(PACK)]
             for t in range(PACK):
-                utility_passes(g, t, banks[t // 2][:, HALF * (t % 2) : HALF * (t % 2 + 1)], HALF * n, HALF * (n + 1))
-            return banks
+                utility_passes(LAST, t, parts[t], HALF * n, HALF * (n + 1))
+            return parts
 
-        def half_shift(g, n, banks):
+        def last_shift(n, parts):
             for t in range(PACK):
-                shift(g, t, banks[t // 2][:, HALF * (t % 2) : HALF * (t % 2 + 1)], HALF * n, HALF * (n + 1))
+                shift(LAST, t, parts[t], HALF * n, HALF * (n + 1))
 
         def weigh(g, n):
-            cs = slice(64 * n, 64 * (n + 1))
+            cs = slice(HALF // 4 * n, HALF // 4 * (n + 1))
             nc.vector.tensor_tensor(
                 out=wide["L", g].rearrange("p (c i t) -> p c t i", i=4, t=PACK)[:, cs],
                 in0=shifted[g % 2][:].rearrange("p (c t i) -> p c t i", t=PACK, i=4)[:, cs],
@@ -319,53 +313,45 @@ def tile_router_weight_gradient_s12_kernel(
             )
 
         def quantize_values(h):
-            quantize(v_codes[h][:], v_planes[h][:], v_t[h][:])
+            quantize(v_codes[h][:], v_planes[h][:], v_wide[h][:])
 
-        def quantize_grad(g, lo=0, hi=PASSES):
+        def quantize_grad(g, lo, hi):
             quantize(
                 g_codes[g][:, GROUP * lo : GROUP * hi],
                 g_planes[g][:, GROUP * lo : GROUP * hi],
-                g_t[g][:, GROUP * PACK * lo : GROUP * PACK * hi],
+                g_wide[g][:, GROUP * PACK * lo : GROUP * PACK * hi],
             )
 
-        def quantize_batch(n):
-            for member in BATCHES[n]:
-                assert member[0] == "L" or 8 * member[0] + 4 * member[1] + 3 in made
-            src, dst, plane = batch[BATCHES[n]]
+        def quantize_call(n):
+            src, dst, plane = call_tiles[n]
             quantize(dst[:], plane[:], src[:])
 
-        def quantize_half(member, n):
+        def quantize_last(n):
             quantize(
-                codes[member][:, HALF * n : HALF * (n + 1)],
-                planes[member][:, HALF * n : HALF * (n + 1)],
-                wide[member][:, HALF * PACK * n : HALF * PACK * (n + 1)],
+                codes["L", LAST][:, HALF * n : HALF * (n + 1)],
+                planes["L", LAST][:, HALF * n : HALF * (n + 1)],
+                wide["L", LAST][:, HALF * PACK * n : HALF * PACK * (n + 1)],
             )
 
-        def final_passes(dst, j, lo, hi, groups, stop=True):
-            n, cols = j // 4, slice(P * (j % 4), P * (j % 4 + 1))
+        def final_passes(bank, j, n, groups):
+            experts = slice(HALF * n, HALF * (n + 1))
+            cols = slice(P * (j % PIECE), P * (j % PIECE + 1))
             for g in groups:
                 nc.tensor.matmul_mx(
-                    out=dst,
-                    lhsT=codes[g, n][:, cols].bitcast(FP8X4),
-                    lhsT_scale=planes[g, n][:, cols],
-                    rhs=codes["L", g][:, lo:hi].bitcast(FP8X4),
-                    rhs_scale=planes["L", g][:, lo:hi],
+                    out=bank[:, experts],
+                    lhsT=codes[g, j // PIECE][:, cols].bitcast(FP8X4),
+                    lhsT_scale=planes[g, j // PIECE][:, cols],
+                    rhs=codes["L", g][:, experts].bitcast(FP8X4),
+                    rhs_scale=planes["L", g][:, experts],
                     start=(g == 0),
-                    stop=(stop and g == GROUPS - 1),
+                    stop=(g == LAST),
                 )
 
-        stored = []
-
-        def store(src, dst, copy):
-            staged = result[len(stored) % len(result)][:, 0 : src.shape[1]]
-            stored.append(staged)
-            copy(out=staged, in_=src)
-            if len(dst.shape) == 3:
-                staged = staged.rearrange("p (j e) -> p j e", j=dst.shape[1])
-            nc.sync.dma_start(out=dst, in_=staged)
-
-        out_tiles = out.rearrange("(j p) e -> p j e", p=P)
-        on_vector, on_scalar, on_gpsimd = nc.vector.tensor_copy, nc.scalar.copy, nc.gpsimd.tensor_copy
+        def store(bank, j, n, copy):
+            experts = slice(HALF * n, HALF * (n + 1))
+            staged = staged_out[(TILES * n + j) % STORE_BUFFERS]
+            copy(out=staged[:], in_=bank[:, experts])
+            nc.sync.dma_start(out=out.rearrange("(j p) e -> p j e", p=P)[:, j, experts], in_=staged[:])
 
         def warm_up(count):
             bank = next_bank()
@@ -381,119 +367,121 @@ def tile_router_weight_gradient_s12_kernel(
                 )
 
         nc.vector.memset(w_plane[:].bitcast(I32), 0)
-        nc.vector.memset(a_sc_first[:], 0)
+        nc.vector.memset(a_staged[1][:], 0)
+        nc.vector.memset(a_staged[0][:], 0)
+        quantize(warm_codes[:], warm_plane[:], a_staged[1][:].rearrange("p h n -> p (h n)").bitcast(BF16))
         nc.vector.memset(ident[:], 0.0)
-        nc.vector.memset(v_t[0][:].bitcast(I32), 0)
         make_identity(nc, ident[:], nomemset=True)
-        nc.vector.memset(a_sc_rest[:], 0)
-        quantize(warm_codes[:], warm_plane[:], v_t[0][:])
-        load_grad(0, [0])
-        load_scales(w_plane[:].bitcast(I32), w_scales, 0, D, (0, 2))
-        load_scales(a_sc_first, a_scales, 0, 2 * GROUP, (0, 2))
-        load_grad(0, [1])
+
+        load_grad(0, 0)
+        load_w_scales(QUADRANTS[:2])
+        load_a_scales(0, QUADRANTS[:2])
+        load_grad(0, 1)
         load_a(0)
-        load_scales(a_sc_first, a_scales, 0, 2 * GROUP, (1,))
-        load_balance(nc.sync)
-        load_scales(a_sc_first, a_scales, 0, 2 * GROUP, (3,))
+        load_a_scales(0, QUADRANTS[2:3])
+        load_balance()
+        load_a_scales(0, QUADRANTS[3:])
         load_w(0)
-        load_scales(w_plane[:].bitcast(I32), w_scales, 0, D, (1, 3))
+        load_w_scales(QUADRANTS[2:])
         load_values(0)
         load_w(1)
         load_values(1)
         load_base(0)
         load_a(1)
         load_base(1)
-        load_grad(1, [0])
+        load_grad(1, 0)
         load_base(2)
         load_base(3)
-        load_grad(1, [1])
+        load_grad(1, 1)
 
-        warm_up(3)
-        split_pair(0, 0)
-        turn_grad(0, [on_scalar] * 2, ((0, 0), (1, 0)))
-        warm_up(2)
-        split_pair(0, 1)
-        turn_grad(0, [on_scalar] * 2, ((0, 1), (1, 1)))
+        for pair in range(2):
+            warm_up(WARM_PASSES[pair])
+            for h in range(PASSES):
+                part_rows(0, h, 2 * pair, 2 * pair + 2, on_vector)
+            for h in range(PASSES):
+                turn_on_tensor(0, h, pair)
         spread_balance()
         order_codes(0, on_vector)
         order_scales(0, on_vector)
         load_a(2)
         load_prob(0)
-        load_scales(a_sc_rest, a_scales, 2 * GROUP, T)
+        load_a_scales(1, QUADRANTS)
         order_scales(1, on_vector)
-        x_tiles(8)
-        quantize_grad(0, 0, 1)
-        interleave_values(0)
-        quantize_grad(0, 1, 2)
-        interleave_values(1)
+        x_tiles(TILES)
+        for h in range(PASSES):
+            quantize_grad(0, h, h + 1)
+            interleave_values(h)
         quantize_values(0)
         order_codes(1, on_vector)
         quantize_values(1)
-        x_tiles(1)
-        quantize_batch(0)
-        for g in range(last):
+        x_tiles(HEAD_TILES - TILES)
+        quantize_call(0)
+
+        for g in range(LAST):
             utilities(g)
             if g == 0:
-                split_rows(1, 0, 0, PACK, on_scalar)
-                split_rows(1, 1, 0, PACK - 1, on_scalar)
-            if g + 1 < last:
-                split_last_row(g + 1)
+                part_on_scalar(1)
+            if g + 1 < LAST:
+                part_on_gpsimd(g + 1)
             else:
-                join_blocks(PACK - 1, PACK, on_gpsimd)
-                join_blocks(0, PACK - 1, on_scalar)
+                join_turned(PACK - 1, PACK, on_gpsimd)
+                join_turned(0, PACK - 1, on_scalar)
             if g == 1:
                 order_scales(2, on_gpsimd)
                 order_scales(3, on_gpsimd)
             else:
                 order_codes(2 + g // 2, on_gpsimd)
             if g == 0:
-                load_grad(2)
-                load_prob(1)
+                load_grad(2, 0)
+                load_grad(2, 1)
+            load_prob(g + 1)
+            if g == 0:
                 load_a(3)
                 load_last_grad()
-            else:
-                load_prob(g + 1)
-            if g + 1 < last:
-                turn_grad(g + 1, [on_scalar] * 4)
-            else:
-                turn_grad(last, [on_scalar] * 2, ((0, 0), (0, 1)))
-            quantize_batch(2 * g + 1)
+            for h in range(PASSES if g + 1 < LAST else 1):
+                for pair in range(2):
+                    turn_on_tensor(g + 1, h, pair)
+            quantize_call(2 * g + 1)
             weigh(g, 0)
-            quantize_grad(g + 1)
+            quantize_grad(g + 1, 0, PASSES)
             weigh(g, 1)
-            x_tiles(ROUND[g] - AHEAD[g])
             if g == 0:
-                split_rows(2, 0, 0, PACK, on_scalar)
-                split_rows(2, 1, 0, PACK - 1, on_scalar)
+                x_tiles(ROUND_TILES[g] - PART_AHEAD[g])
+                part_on_scalar(2)
+                x_tiles(PART_AHEAD[g])
+            elif g == 1:
+                x_tiles(ROUND_TILES[g] - PART_AHEAD[g])
+                part_last()
+                x_tiles(PART_AHEAD[g])
+            else:
+                x_tiles(ROUND_TILES[g])
+            quantize_call(2 * g + 2)
             if g == 1:
-                split_last()
-            x_tiles(AHEAD[g])
-            quantize_batch(2 * g + 2)
-            if g == 1:
-                turn_blocks()
-        first = half_utilities(last, 0)
-        second = half_utilities(last, 1)
-        x_tiles(32 - len(made))
-        half_shift(last, 0, first)
-        quantize_batch(7)
-        weigh(last, 0)
-        quantize_batch(8)
-        quantize_half(("L", last), 0)
-        half_shift(last, 1, second)
-        weigh(last, 1)
-        turn = [next_bank() for j in range(BANKS)]
-        banks = [bank for bank in range(BANKS) if bank not in SECOND]
-        banks = [turn[bank] for bank in banks + list(SECOND)]
-        for chunk in (range(0, 3), range(3, 6)):
-            for g in range(last):
-                for j in chunk:
-                    final_passes(banks[j][:, 0:HALF], j, 0, HALF, [g])
-        for j in range(BANKS):
-            final_passes(banks[j][:, 0:HALF], j, 0, HALF, [last] if j < 6 else range(GROUPS))
-            store(banks[j][:, 0:HALF], out_tiles[:, j, 0:HALF], on_scalar)
-        quantize_half(("L", last), 1)
-        for j in range(4):
-            final_passes(banks[j][:, HALF:E], j, HALF, E, range(last))
-        for j in range(BANKS):
-            final_passes(banks[j][:, HALF:E], j, HALF, E, [last] if j < 4 else range(GROUPS))
-            store(banks[j][:, HALF:E], out_tiles[:, j, HALF:E], on_vector if j % 2 == 0 else on_scalar)
+                turn_on_vector()
+
+        first = last_utilities(0)
+        second = last_utilities(1)
+        held = [n % BANKS for n in (len(taken) - 2, len(taken) - 1)]
+        x_tiles(X_TILES - len(made))
+        last_shift(0, first)
+        quantize_call(2 * LAST + 1)
+        weigh(LAST, 0)
+        quantize_call(2 * LAST + 2)
+        quantize_last(0)
+        last_shift(1, second)
+        weigh(LAST, 1)
+        numbered = [(len(taken) % BANKS, next_bank()) for j in range(BANKS)]
+        banks = [bank for n, bank in numbered if n not in held] + [bank for n, bank in numbered if n in held]
+        for some in (range(0, EARLY_FIRST // 2), range(EARLY_FIRST // 2, EARLY_FIRST)):
+            for g in range(LAST):
+                for j in some:
+                    final_passes(banks[j], j, 0, [g])
+        for j in range(TILES):
+            final_passes(banks[j], j, 0, [LAST] if j < EARLY_FIRST else range(GROUPS))
+            store(banks[j], j, 0, on_scalar)
+        quantize_last(1)
+        for j in range(EARLY_SECOND):
+            final_passes(banks[j], j, 1, range(LAST))
+        for j in range(TILES):
+            final_passes(banks[j], j, 1, [LAST] if j < EARLY_SECOND else range(GROUPS))
+            store(banks[j], j, 1, on_vector if j % 2 == 0 else on_scalar)

@@ -35,8 +35,8 @@ PART_AHEAD = (1, 4)
 EARLY_FIRST = BANKS - 2
 EARLY_SECOND = 4
 STORE_BUFFERS = 12
-WARM_N = 256
-WARM_PASSES = (5, 2)
+WARM_N = 512
+WARM_PASSES = (3, 2)
 CALLS = (
     ((0, 0),),
     ((0, 1),),
@@ -367,11 +367,12 @@ def tile_router_weight_gradient_s12_kernel(
                 )
 
         nc.vector.memset(w_plane[:].bitcast(I32), 0)
-        nc.vector.memset(a_staged[1][:], 0)
+        nc.vector.memset(v_wide[0][:].bitcast(I32), 0)
         nc.vector.memset(a_staged[0][:], 0)
-        quantize(warm_codes[:], warm_plane[:], a_staged[1][:].rearrange("p h n -> p (h n)").bitcast(BF16))
+        quantize(warm_codes[:], warm_plane[:], v_wide[0][:])
         nc.vector.memset(ident[:], 0.0)
         make_identity(nc, ident[:], nomemset=True)
+        nc.vector.memset(a_staged[1][:], 0)
 
         load_grad(0, 0)
         load_w_scales(QUADRANTS[:2])

@@ -31,7 +31,6 @@ PIECE = 4
 QUADRANTS = (0, 2, 1, 3)
 HEAD_TILES = 9
 ROUND_TILES = (6, 7, 7)
-PART_AHEAD = (1, 4)
 EARLY_FIRST = BANKS - 2
 EARLY_SECOND = 4
 STORE_BUFFERS = 12
@@ -114,14 +113,9 @@ def tile_router_weight_gradient_s12_kernel(
         staged_out = [keep("staged_out%d" % n, [P, HALF], F32) for n in range(STORE_BUFFERS)]
 
         parted = [[[g_parted[h][:, 2 * s : 2 * s + 2] for s in range(PACK)] for h in range(PASSES)] for g in range(GROUPS)]
-        for g in (1, 2):
+        for g in range(1, GROUPS):
             spent = wide[CALLS[2 * g - 2][0]].bitcast(F32)
             parted[g][1][PACK - 1] = spent[:, 0 : 2 * P].rearrange("p (u w) -> p u w", u=2)
-
-        last_raw = g_raw[LAST][:].rearrange("p s d -> p (s d)")
-        last_rows = last_raw[:, 0 : PACK * GROUP].rearrange("p (s d) -> p s d", s=PACK)
-        last_slices = last_raw[:, PACK * GROUP : 2 * PACK * GROUP].rearrange("p (b e) -> p b e", e=P)
-        turned = g_raw[LAST - 1][:].rearrange("p s d -> p (s d)").bitcast(F32)[:, 0 : 2 * GROUP]
 
         def load_a(g):
             src = a_words.rearrange("h p n -> p h n")[:, :, 2 * GROUP * g : 2 * GROUP * (g + 1)]
@@ -145,13 +139,6 @@ def tile_router_weight_gradient_s12_kernel(
         def load_grad(g, pair):
             rows = grad[GROUP * g : GROUP * (g + 1), :].rearrange("(m s) d -> m s d", s=PACK)
             nc.sync.dma_start(out=g_raw[g][:, 2 * pair : 2 * pair + 2, :], in_=rows[:, 2 * pair : 2 * pair + 2, :])
-
-        def load_last_grad():
-            rows = grad[GROUP * LAST : GROUP * (LAST + 1), :]
-            nc.sync.dma_start(out=last_rows, in_=rows[:, 0:GROUP].rearrange("(m s) d -> m s d", s=PACK))
-            slices = rows[:, GROUP:D].rearrange("(b j) (q e) -> q j b e", j=32, q=4)
-            for q in QUADRANTS:
-                nc.sync.dma_start(out=last_slices[32 * q : 32 * (q + 1)], in_=slices[q])
 
         def load_values(h):
             rows = values[GROUP * h : GROUP * (h + 1), :].rearrange("(p t) e -> p t e", t=PACK)
@@ -230,14 +217,7 @@ def tile_router_weight_gradient_s12_kernel(
         def part_on_gpsimd(g):
             on_gpsimd(out=parted[g][1][PACK - 1], in_=grad_words(g)[:, 1, PACK - 1])
 
-        def part_last():
-            slices = last_slices.bitcast(F32).rearrange("p b (i u) -> p u b i", u=2)
-            dst = g_parted[1][:].rearrange("p q w -> p (q w)").rearrange("p (u b i) -> p u b i", u=2, i=32)
-            nc.scalar.copy(out=dst, in_=slices)
-            rows = last_rows.bitcast(F32).rearrange("p s (w u) -> p s u w", u=2)
-            nc.scalar.copy(out=g_parted[0][:].rearrange("p (s u) w -> p s u w", u=2), in_=rows)
-
-        def turn_on_tensor(g, h, pair):
+        def turn(g, h, pair):
             bank = next_bank()
             for q in range(4):
                 words = parted[g][h][2 * pair + q // 2][:, q % 2, :]
@@ -247,14 +227,6 @@ def tile_router_weight_gradient_s12_kernel(
                 out=dst[:, h, :, :, 4 * pair : 4 * pair + 4],
                 in_=bank[:].rearrange("p (q c t) -> p t c q", q=4, t=PACK),
             )
-
-        def turn_on_vector():
-            nc.vector.transpose(out=turned, in_=g_parted[1][:].rearrange("p q w -> p (q w)"))
-
-        def join_turned(lo, hi, copy):
-            dst = g_wide[LAST][:].bitcast(F32).rearrange("p (h t c s u) -> p h t c s u", h=PASSES, t=PACK, s=PACK, u=2)
-            src = turned.rearrange("p (u c t s) -> p t c s u", u=2, t=PACK, s=PACK)
-            copy(out=dst[:, 1, lo:hi], in_=src[:, lo:hi])
 
         def interleave_values(h):
             nc.vector.tensor_copy(
@@ -400,7 +372,7 @@ def tile_router_weight_gradient_s12_kernel(
             for h in range(PASSES):
                 part_rows(0, h, 2 * pair, 2 * pair + 2, on_vector)
             for h in range(PASSES):
-                turn_on_tensor(0, h, pair)
+                turn(0, h, pair)
         spread_balance()
         order_codes(0, on_vector)
         order_scales(0, on_vector)
@@ -422,11 +394,7 @@ def tile_router_weight_gradient_s12_kernel(
             utilities(g)
             if g == 0:
                 part_on_scalar(1)
-            if g + 1 < LAST:
-                part_on_gpsimd(g + 1)
-            else:
-                join_turned(PACK - 1, PACK, on_gpsimd)
-                join_turned(0, PACK - 1, on_scalar)
+            part_on_gpsimd(g + 1)
             if g == 1:
                 order_scales(2, on_gpsimd)
                 order_scales(3, on_gpsimd)
@@ -438,27 +406,20 @@ def tile_router_weight_gradient_s12_kernel(
             load_prob(g + 1)
             if g == 0:
                 load_a(3)
-                load_last_grad()
-            for h in range(PASSES if g + 1 < LAST else 1):
+                load_grad(3, 0)
+                load_grad(3, 1)
+            for h in range(PASSES):
                 for pair in range(2):
-                    turn_on_tensor(g + 1, h, pair)
+                    turn(g + 1, h, pair)
             quantize_call(2 * g + 1)
             weigh(g, 0)
             quantize_grad(g + 1, 0, PASSES)
             weigh(g, 1)
-            if g == 0:
-                x_tiles(ROUND_TILES[g] - PART_AHEAD[g])
-                part_on_scalar(2)
-                x_tiles(PART_AHEAD[g])
-            elif g == 1:
-                x_tiles(ROUND_TILES[g] - PART_AHEAD[g])
-                part_last()
-                x_tiles(PART_AHEAD[g])
-            else:
-                x_tiles(ROUND_TILES[g])
+            x_tiles(ROUND_TILES[g] - 1)
+            if g + 2 < GROUPS:
+                part_on_scalar(g + 2)
+            x_tiles(1)
             quantize_call(2 * g + 2)
-            if g == 1:
-                turn_on_vector()
 
         first = last_utilities(0)
         second = last_utilities(1)

@@ -30,10 +30,9 @@ X_TILES = GROUPS * TILES
 PIECE = 4
 QUADRANTS = (0, 2, 1, 3)
 HEAD_TILES = 9
-ROUND_TILES = (6, 7, 7)
-EARLY_FIRST = BANKS - 2
-EARLY_SECOND = 4
-STORE_BUFFERS = 12
+ROUND_TILES = (6, 7, 6)
+EARLY = 4
+STORE_BUFFERS = 7
 WARM_N = 512
 WARM_PASSES = (3, 2)
 CALLS = (
@@ -43,10 +42,11 @@ CALLS = (
     (("L", 0),),
     ((1, 1),),
     (("L", 1), (2, 0)),
-    ((2, 1),),
-    (("L", 2), (3, 0)),
-    ((3, 1),),
+    (("L", 2),),
+    ((3, 0),),
     (("L", 3),),
+    ((2, 1),),
+    ((3, 1),),
 )
 
 
@@ -110,7 +110,7 @@ def tile_router_weight_gradient_s12_kernel(
                 wide[member] = call_tiles[n][0][:, BANK * PACK * m : BANK * PACK * (m + 1)]
                 codes[member] = call_tiles[n][1][:, BANK * m : BANK * (m + 1)]
                 planes[member] = call_tiles[n][2][:, BANK * m : BANK * (m + 1)]
-        staged_out = [keep("staged_out%d" % n, [P, HALF], F32) for n in range(STORE_BUFFERS)]
+        staged_out = [keep("staged_out%d" % n, [P, E], F32) for n in range(STORE_BUFFERS)]
 
         parted = [[[g_parted[h][:, 2 * s : 2 * s + 2] for s in range(PACK)] for h in range(PASSES)] for g in range(GROUPS)]
         for g in range(1, GROUPS):
@@ -234,49 +234,32 @@ def tile_router_weight_gradient_s12_kernel(
                 in_=v_raw[h][:].rearrange("p t (c i) -> p c t i", i=4),
             )
 
-        def utility_passes(g, t, dst, lo, hi):
-            for h in range(PASSES):
-                tokens = slice(GROUP * h + P * t, GROUP * h + P * (t + 1))
-                nc.tensor.matmul_mx(
-                    out=dst,
-                    lhsT=g_codes[g][:, tokens].bitcast(FP8X4),
-                    lhsT_scale=g_planes[g][:, tokens],
-                    rhs=v_codes[h][:, lo:hi].bitcast(FP8X4),
-                    rhs_scale=v_planes[h][:, lo:hi],
-                    start=(h == 0),
-                    stop=(h == PASSES - 1),
-                )
-
-        def shift(g, t, src, lo, hi):
-            dst = shifted[g % 2][:].rearrange("p (c t i) -> p c t i", t=PACK, i=4)
-            nc.vector.scalar_tensor_tensor(
-                out=dst[:, lo // 4 : hi // 4, t, :],
-                in0=src.rearrange("p (c i) -> p c i", i=4),
-                scalar=base_sb[:, g, 4 * t : 4 * t + 1],
-                in1=bal_row[:, lo:hi].rearrange("p (c i) -> p c i", i=4),
-                op0=ALU.subtract,
-                op1=ALU.add,
-            )
-
         def utilities(g):
+            dst = shifted[g % 2][:].rearrange("p (c t i) -> p c t i", t=PACK, i=4)
             for t in range(PACK):
                 bank = next_bank()
-                utility_passes(g, t, bank[:], 0, E)
-                shift(g, t, bank[:], 0, E)
+                for h in range(PASSES):
+                    tokens = slice(GROUP * h + P * t, GROUP * h + P * (t + 1))
+                    nc.tensor.matmul_mx(
+                        out=bank[:],
+                        lhsT=g_codes[g][:, tokens].bitcast(FP8X4),
+                        lhsT_scale=g_planes[g][:, tokens],
+                        rhs=v_codes[h][:].bitcast(FP8X4),
+                        rhs_scale=v_planes[h][:],
+                        start=(h == 0),
+                        stop=(h == PASSES - 1),
+                    )
+                nc.vector.scalar_tensor_tensor(
+                    out=dst[:, :, t, :],
+                    in0=bank[:].rearrange("p (c i) -> p c i", i=4),
+                    scalar=base_sb[:, g, 4 * t : 4 * t + 1],
+                    in1=bal_row[:].rearrange("p (c i) -> p c i", i=4),
+                    op0=ALU.subtract,
+                    op1=ALU.add,
+                )
 
-        def last_utilities(n):
-            banks = [next_bank() for pair in range(2)]
-            parts = [banks[t // 2][:, HALF * (t % 2) : HALF * (t % 2 + 1)] for t in range(PACK)]
-            for t in range(PACK):
-                utility_passes(LAST, t, parts[t], HALF * n, HALF * (n + 1))
-            return parts
-
-        def last_shift(n, parts):
-            for t in range(PACK):
-                shift(LAST, t, parts[t], HALF * n, HALF * (n + 1))
-
-        def weigh(g, n):
-            cs = slice(HALF // 4 * n, HALF // 4 * (n + 1))
+        def weigh(g, lo, hi):
+            cs = slice(lo // 4, hi // 4)
             nc.vector.tensor_tensor(
                 out=wide["L", g].rearrange("p (c i t) -> p c t i", i=4, t=PACK)[:, cs],
                 in0=shifted[g % 2][:].rearrange("p (c t i) -> p c t i", t=PACK, i=4)[:, cs],
@@ -298,32 +281,26 @@ def tile_router_weight_gradient_s12_kernel(
             src, dst, plane = call_tiles[n]
             quantize(dst[:], plane[:], src[:])
 
-        def quantize_last(n):
-            quantize(
-                codes["L", LAST][:, HALF * n : HALF * (n + 1)],
-                planes["L", LAST][:, HALF * n : HALF * (n + 1)],
-                wide["L", LAST][:, HALF * PACK * n : HALF * PACK * (n + 1)],
-            )
-
-        def final_passes(bank, j, n, groups):
-            experts = slice(HALF * n, HALF * (n + 1))
+        def final_passes(bank, j, lo, hi, groups):
             cols = slice(P * (j % PIECE), P * (j % PIECE + 1))
             for g in groups:
                 nc.tensor.matmul_mx(
-                    out=bank[:, experts],
+                    out=bank[:, 0 : hi - lo],
                     lhsT=codes[g, j // PIECE][:, cols].bitcast(FP8X4),
                     lhsT_scale=planes[g, j // PIECE][:, cols],
-                    rhs=codes["L", g][:, experts].bitcast(FP8X4),
-                    rhs_scale=planes["L", g][:, experts],
+                    rhs=codes["L", g][:, lo:hi].bitcast(FP8X4),
+                    rhs_scale=planes["L", g][:, lo:hi],
                     start=(g == 0),
                     stop=(g == LAST),
                 )
 
-        def store(bank, j, n, copy):
-            experts = slice(HALF * n, HALF * (n + 1))
-            staged = staged_out[(TILES * n + j) % STORE_BUFFERS]
-            copy(out=staged[:], in_=bank[:, experts])
-            nc.sync.dma_start(out=out.rearrange("(j p) e -> p j e", p=P)[:, j, experts], in_=staged[:])
+        stored = []
+
+        def store(bank, j, lo, hi, copy):
+            staged = staged_out[len(stored) % STORE_BUFFERS][:, 0 : hi - lo]
+            stored.append(j)
+            copy(out=staged, in_=bank[:, 0 : hi - lo])
+            nc.sync.dma_start(out=out.rearrange("(j p) e -> p j e", p=P)[:, j, lo:hi], in_=staged)
 
         def warm_up(count):
             bank = next_bank()
@@ -412,38 +389,33 @@ def tile_router_weight_gradient_s12_kernel(
                 for pair in range(2):
                     turn(g + 1, h, pair)
             quantize_call(2 * g + 1)
-            weigh(g, 0)
+            weigh(g, 0, HALF)
             quantize_grad(g + 1, 0, PASSES)
-            weigh(g, 1)
+            weigh(g, HALF, E)
             x_tiles(ROUND_TILES[g] - 1)
             if g + 2 < GROUPS:
                 part_on_scalar(g + 2)
             x_tiles(1)
-            quantize_call(2 * g + 2)
+            if g + 1 < LAST:
+                quantize_call(2 * g + 2)
 
-        first = last_utilities(0)
-        second = last_utilities(1)
-        held = [n % BANKS for n in (len(taken) - 2, len(taken) - 1)]
+        utilities(LAST)
         x_tiles(X_TILES - len(made))
-        last_shift(0, first)
-        quantize_call(2 * LAST + 1)
-        weigh(LAST, 0)
-        quantize_call(2 * LAST + 2)
-        quantize_last(0)
-        last_shift(1, second)
-        weigh(LAST, 1)
-        numbered = [(len(taken) % BANKS, next_bank()) for j in range(BANKS)]
-        banks = [bank for n, bank in numbered if n not in held] + [bank for n, bank in numbered if n in held]
-        for some in (range(0, EARLY_FIRST // 2), range(EARLY_FIRST // 2, EARLY_FIRST)):
+        quantize_call(2 * LAST)
+        weigh(LAST, 0, E)
+        for n in range(2 * LAST + 1, len(CALLS)):
+            quantize_call(n)
+        banks = [next_bank() for j in range(EARLY)]
+        for some in (range(0, EARLY // 2), range(EARLY // 2, EARLY)):
             for g in range(LAST):
                 for j in some:
-                    final_passes(banks[j], j, 0, [g])
-        for j in range(TILES):
-            final_passes(banks[j], j, 0, [LAST] if j < EARLY_FIRST else range(GROUPS))
-            store(banks[j], j, 0, on_scalar)
-        quantize_last(1)
-        for j in range(EARLY_SECOND):
-            final_passes(banks[j], j, 1, range(LAST))
-        for j in range(TILES):
-            final_passes(banks[j], j, 1, [LAST] if j < EARLY_SECOND else range(GROUPS))
-            store(banks[j], j, 1, on_vector if j % 2 == 0 else on_scalar)
+                    final_passes(banks[j], j, 0, E, [g])
+        for j in range(TILES - 1):
+            if j >= EARLY:
+                banks.append(next_bank())
+            final_passes(banks[j], j, 0, E, [LAST] if j < EARLY else range(GROUPS))
+            store(banks[j], j, 0, E, on_scalar if j % 2 == 0 else on_vector)
+        for lo, copy in ((0, on_vector), (HALF, on_scalar)):
+            bank = next_bank()
+            final_passes(bank, TILES - 1, lo, lo + HALF, range(GROUPS))
+            store(bank, TILES - 1, lo, lo + HALF, copy)

@@ -26,28 +26,22 @@ BANKS = 8
 HALF = E // 2
 ALIGN = 64
 TILES = D // P
-X_TILES = GROUPS * TILES
-PIECE = 4
 QUADRANTS = (0, 2, 1, 3)
-HEAD_TILES = 9
-ROUND_TILES = (6, 7, 6)
-EARLY = 4
-STORE_BUFFERS = 7
-WARM_N = 512
-WARM_PASSES = (3, 2)
-CALLS = (
-    ((0, 0),),
-    ((0, 1),),
-    ((1, 0),),
-    (("L", 0),),
-    ((1, 1),),
-    (("L", 1), (2, 0)),
-    (("L", 2),),
-    ((3, 0),),
-    (("L", 3),),
-    ((2, 1),),
-    ((3, 1),),
+HEAD_BANKS = (4, 2, 2)
+ROUND_BANKS = (6, 5, 5)
+PIECE = 4
+PAIRS = (
+    [(g, n) for g in (0, 1) for n in range(4)]
+    + [(g, n) for g in (2, 3) for n in (0, 1)]
+    + [(g, n) for n in (2, 3) for g in (2, 3)]
 )
+NARROW_PAIRS = 12
+SPLIT = 320
+POOL_ROWS = 2
+EARLY = 3
+STORE_BUFFERS = 6
+WARM_N = 512
+WARM_PASSES = 4
 
 
 def tile_router_weight_gradient_s12_kernel(
@@ -72,7 +66,7 @@ def tile_router_weight_gradient_s12_kernel(
 
         ident = keep("ident", [P, P], F32)
         bal_col = keep("bal_col", [P, PACK], BF16)
-        bal_row = keep("bal_row", [P, E], F32)
+        bal_row = keep("bal_row", [P, E], BF16)
         warm_codes = keep("warm_codes", [P, WARM_N], U32)
         warm_plane = keep("warm_plane", [P, WARM_N], U8)
         base_sb = keep("base_sb", [P, GROUPS, 16], BF16)
@@ -80,7 +74,7 @@ def tile_router_weight_gradient_s12_kernel(
         a_raw = [keep("a_raw%d" % g, [P, PASSES, 256], I32) for g in range(2)] * 2
         a_codes = [keep("a_codes%d" % g, [P, PACK, PASSES, 2 * P], U8) for g in range(GROUPS)]
         a_staged = [keep("a_staged%d" % n, [P, PASSES, 256], I32) for n in range(2)]
-        a_planes = [keep("a_plane%d" % g, [P, PACK, PASSES, P], U8) for g in range(GROUPS)]
+        a_planes = [keep("a_plane%d" % n, [P, 2, PACK, PASSES, P], U8) for n in range(2)]
         w_codes = [keep("w_codes%d" % n, [P, PASSES, D], U8) for n in range(2)]
         w_plane = keep("w_plane", [P, PASSES, D], U8)
 
@@ -95,27 +89,20 @@ def tile_router_weight_gradient_s12_kernel(
         v_planes = [keep("v_plane%d" % h, [P, E], U8) for h in range(PASSES)]
         p_sb = [keep("p_sb%d" % g, [P, PACK, E], BF16) for g in range(GROUPS)]
         shifted = [keep("shifted%d" % n, [P, E * PACK], F32) for n in range(2)]
-
-        wide, codes, planes, call_tiles = {}, {}, {}, []
-        for n, members in enumerate(CALLS):
-            width = len(members) * BANK
-            call_tiles.append(
-                (
-                    keep("wide%d" % n, [P, width * PACK], BF16),
-                    keep("codes%d" % n, [P, width], U32),
-                    keep("plane%d" % n, [P, width], U8),
-                )
-            )
-            for m, member in enumerate(members):
-                wide[member] = call_tiles[n][0][:, BANK * PACK * m : BANK * PACK * (m + 1)]
-                codes[member] = call_tiles[n][1][:, BANK * m : BANK * (m + 1)]
-                planes[member] = call_tiles[n][2][:, BANK * m : BANK * (m + 1)]
+        l_wide = [keep("l_wide%d" % g, [P, E * PACK], BF16) for g in range(2)] * 2
+        l_codes = [keep("l_codes%d" % g, [P, E], U32) for g in range(GROUPS)]
+        l_planes = [keep("l_plane%d" % g, [P, E], U8) for g in range(GROUPS)]
+        x_wide = [keep("x_wide%d" % n, [P, PIECE * BANK], BF16) for n in range(len(PAIRS) // 2)]
+        x_codes = [keep("x_codes%d" % n, [P, PIECE * P], U32) for n in range(len(PAIRS) // 2)]
+        x_planes = [keep("x_plane%d" % n, [P, PIECE * P], U8) for n in range(len(PAIRS) // 2)]
         staged_out = [keep("staged_out%d" % n, [P, E], F32) for n in range(STORE_BUFFERS)]
 
         parted = [[[g_parted[h][:, 2 * s : 2 * s + 2] for s in range(PACK)] for h in range(PASSES)] for g in range(GROUPS)]
+        spent = [None, x_wide[0][:].bitcast(F32), x_wide[2][:].bitcast(F32), shifted[1][:, PACK * SPLIT :]]
         for g in range(1, GROUPS):
-            spent = wide[CALLS[2 * g - 2][0]].bitcast(F32)
-            parted[g][1][PACK - 1] = spent[:, 0 : 2 * P].rearrange("p (u w) -> p u w", u=2)
+            for r in range(POOL_ROWS):
+                row = spent[g][:, 2 * P * r : 2 * P * (r + 1)]
+                parted[g][1][PACK - POOL_ROWS + r] = row.rearrange("p (u w) -> p u w", u=2)
 
         def load_a(g):
             src = a_words.rearrange("h p n -> p h n")[:, :, 2 * GROUP * g : 2 * GROUP * (g + 1)]
@@ -162,9 +149,11 @@ def tile_router_weight_gradient_s12_kernel(
                 in_=a_raw[g][:].rearrange("p h (c t w) -> p t (h c) w", t=PACK, w=2),
             )
 
-        def order_scales(g, copy):
-            staged = a_staged[g // 2][:, :, P * (g % 2) : P * (g % 2 + 1)]
-            copy(out=a_planes[g][:].bitcast(I32), in_=staged.rearrange("p h (c t) -> p t h c", t=PACK))
+        def order_scales(n, rows, groups, copy):
+            copy(
+                out=a_planes[n][rows].bitcast(I32)[:, groups],
+                in_=a_staged[n][rows].rearrange("p h (g c t) -> p g t h c", g=2, t=PACK)[:, groups],
+            )
 
         def quantize(dst, plane, src):
             nc.vector.quantize_mx(out=dst.bitcast(FP8X4), scales=plane, in_=src)
@@ -175,33 +164,40 @@ def tile_router_weight_gradient_s12_kernel(
             for u in range(2):
                 nc.tensor.transpose(bank[:, P * u : P * (u + 1)], words[:, u : u + 1].to_broadcast([P, P]), ident[:])
             nc.scalar.copy(
-                out=bal_row[:].rearrange("p (n u e) -> p n u e", u=2, e=2),
-                in_=bank[:, 0 : 2 * P].bitcast(BF16).rearrange("p (u n e) -> p n u e", u=2, e=2),
+                out=bal_row[:].bitcast(F32).rearrange("p (n u) -> p n u", u=2),
+                in_=bank[:, 0 : 2 * P].rearrange("p (u n) -> p n u", u=2),
             )
+
+        def x_passes(dst, g, t, j, width):
+            n, jj = divmod(j, TILES // 2)
+            for h in range(PASSES):
+                nc.tensor.matmul_mx(
+                    out=dst,
+                    lhsT=a_codes[g][:, t, h, :].bitcast(FP4X4),
+                    lhsT_scale=a_planes[g // 2][:, g % 2, t, h, :],
+                    rhs=w_codes[n][:, h, 2 * P * jj : 2 * (P * jj + width)].bitcast(FP4X4),
+                    rhs_scale=w_plane[:, h, P * j : P * j + width],
+                    start=(h == 0),
+                    stop=(h == PASSES - 1),
+                )
 
         made = []
 
-        def x_tiles(count):
-            for tile in range(len(made), len(made) + count):
-                made.append(tile)
-                g, j = divmod(tile, TILES)
-                n, jj = divmod(j, PIECE)
+        def x_banks(count):
+            for b in range(len(made), len(made) + count):
+                made.append(b)
+                k, u = divmod(b, 2)
+                g, n = PAIRS[k]
+                words = x_wide[k // 2][:, 2 * BANK * (k % 2) : 2 * BANK * (k % 2 + 1)].rearrange("p (d t) -> p d t", t=PACK)
                 bank = next_bank()
-                for t in range(PACK):
-                    for h in range(PASSES):
-                        nc.tensor.matmul_mx(
-                            out=bank[:, P * t : P * (t + 1)],
-                            lhsT=a_codes[g][:, t, h, :].bitcast(FP4X4),
-                            lhsT_scale=a_planes[g][:, t, h, :],
-                            rhs=w_codes[n][:, h, 2 * P * jj : 2 * P * (jj + 1)].bitcast(FP4X4),
-                            rhs_scale=w_plane[:, h, P * j : P * (j + 1)],
-                            start=(h == 0),
-                            stop=(h == PASSES - 1),
-                        )
-                nc.scalar.copy(
-                    out=wide[g, n][:, BANK * jj : BANK * (jj + 1)].rearrange("p (d t) -> p d t", t=PACK),
-                    in_=bank[:].rearrange("p (t d) -> p d t", t=PACK),
-                )
+                if k < NARROW_PAIRS:
+                    for t in range(PACK):
+                        x_passes(bank[:, P * t : P * (t + 1)], g, t, 2 * n + u, P)
+                    nc.scalar.copy(out=words[:, P * u : P * (u + 1)], in_=bank[:].rearrange("p (t d) -> p d t", t=PACK))
+                else:
+                    for e in range(2):
+                        x_passes(bank[:, 2 * P * e : 2 * P * (e + 1)], g, 2 * u + e, 2 * n, 2 * P)
+                    nc.scalar.copy(out=words[:, :, 2 * u : 2 * u + 2], in_=bank[:].rearrange("p (e d) -> p d e", e=2))
 
         def grad_words(g):
             return g_raw[g][:].bitcast(F32).rearrange("p s (h w u) -> p h s u w", h=PASSES, u=2)
@@ -212,10 +208,11 @@ def tile_router_weight_gradient_s12_kernel(
 
         def part_on_scalar(g):
             part_rows(g, 0, 0, PACK, on_scalar)
-            part_rows(g, 1, 0, PACK - 1, on_scalar)
+            part_rows(g, 1, 0, PACK - POOL_ROWS, on_scalar)
 
         def part_on_gpsimd(g):
-            on_gpsimd(out=parted[g][1][PACK - 1], in_=grad_words(g)[:, 1, PACK - 1])
+            dst = spent[g][:, 0 : 2 * P * POOL_ROWS].rearrange("p (s u w) -> p s u w", s=POOL_ROWS, u=2)
+            on_gpsimd(out=dst, in_=grad_words(g)[:, 1, PACK - POOL_ROWS : PACK])
 
         def turn(g, h, pair):
             bank = next_bank()
@@ -236,22 +233,23 @@ def tile_router_weight_gradient_s12_kernel(
 
         def utilities(g):
             dst = shifted[g % 2][:].rearrange("p (c t i) -> p c t i", t=PACK, i=4)
+            banks = [next_bank() for t in range(PACK)]
+            steps = [(t, h) for t in range(PACK) for h in range(PASSES)]
+            for t, h in sorted(steps, key=lambda step: step[1]) if g == 0 else steps:
+                tokens = slice(GROUP * h + P * t, GROUP * h + P * (t + 1))
+                nc.tensor.matmul_mx(
+                    out=banks[t][:],
+                    lhsT=g_codes[g][:, tokens].bitcast(FP8X4),
+                    lhsT_scale=g_planes[g][:, tokens],
+                    rhs=v_codes[h][:].bitcast(FP8X4),
+                    rhs_scale=v_planes[h][:],
+                    start=(h == 0),
+                    stop=(h == PASSES - 1),
+                )
             for t in range(PACK):
-                bank = next_bank()
-                for h in range(PASSES):
-                    tokens = slice(GROUP * h + P * t, GROUP * h + P * (t + 1))
-                    nc.tensor.matmul_mx(
-                        out=bank[:],
-                        lhsT=g_codes[g][:, tokens].bitcast(FP8X4),
-                        lhsT_scale=g_planes[g][:, tokens],
-                        rhs=v_codes[h][:].bitcast(FP8X4),
-                        rhs_scale=v_planes[h][:],
-                        start=(h == 0),
-                        stop=(h == PASSES - 1),
-                    )
                 nc.vector.scalar_tensor_tensor(
                     out=dst[:, :, t, :],
-                    in0=bank[:].rearrange("p (c i) -> p c i", i=4),
+                    in0=banks[t][:].rearrange("p (c i) -> p c i", i=4),
                     scalar=base_sb[:, g, 4 * t : 4 * t + 1],
                     in1=bal_row[:].rearrange("p (c i) -> p c i", i=4),
                     op0=ALU.subtract,
@@ -261,7 +259,7 @@ def tile_router_weight_gradient_s12_kernel(
         def weigh(g, lo, hi):
             cs = slice(lo // 4, hi // 4)
             nc.vector.tensor_tensor(
-                out=wide["L", g].rearrange("p (c i t) -> p c t i", i=4, t=PACK)[:, cs],
+                out=l_wide[g][:].rearrange("p (c i t) -> p c t i", i=4, t=PACK)[:, cs],
                 in0=shifted[g % 2][:].rearrange("p (c t i) -> p c t i", t=PACK, i=4)[:, cs],
                 in1=p_sb[g][:].rearrange("p t (c i) -> p c t i", i=4)[:, cs],
                 op=ALU.mult,
@@ -277,19 +275,22 @@ def tile_router_weight_gradient_s12_kernel(
                 g_wide[g][:, GROUP * PACK * lo : GROUP * PACK * hi],
             )
 
-        def quantize_call(n):
-            src, dst, plane = call_tiles[n]
-            quantize(dst[:], plane[:], src[:])
+        def quantize_l(g):
+            quantize(l_codes[g][:], l_planes[g][:], l_wide[g][:])
+
+        def quantize_x(n):
+            quantize(x_codes[n][:], x_planes[n][:], x_wide[n][:])
 
         def final_passes(bank, j, lo, hi, groups):
-            cols = slice(P * (j % PIECE), P * (j % PIECE + 1))
             for g in groups:
+                n, k = divmod(PAIRS.index((g, j // 2)), 2)
+                cols = slice(P * (2 * k + j % 2), P * (2 * k + j % 2 + 1))
                 nc.tensor.matmul_mx(
                     out=bank[:, 0 : hi - lo],
-                    lhsT=codes[g, j // PIECE][:, cols].bitcast(FP8X4),
-                    lhsT_scale=planes[g, j // PIECE][:, cols],
-                    rhs=codes["L", g][:, lo:hi].bitcast(FP8X4),
-                    rhs_scale=planes["L", g][:, lo:hi],
+                    lhsT=x_codes[n][:, cols].bitcast(FP8X4),
+                    lhsT_scale=x_planes[n][:, cols],
+                    rhs=l_codes[g][:, lo:hi].bitcast(FP8X4),
+                    rhs_scale=l_planes[g][:, lo:hi],
                     start=(g == 0),
                     stop=(g == LAST),
                 )
@@ -317,67 +318,65 @@ def tile_router_weight_gradient_s12_kernel(
 
         nc.vector.memset(w_plane[:].bitcast(I32), 0)
         nc.vector.memset(v_wide[0][:].bitcast(I32), 0)
-        nc.vector.memset(a_staged[0][:], 0)
+        nc.vector.memset(a_planes[0][:].bitcast(I32), 0)
         quantize(warm_codes[:], warm_plane[:], v_wide[0][:])
         nc.vector.memset(ident[:], 0.0)
         make_identity(nc, ident[:], nomemset=True)
-        nc.vector.memset(a_staged[1][:], 0)
 
-        load_grad(0, 0)
+        load_a_scales(0, QUADRANTS)
         load_w_scales(QUADRANTS[:2])
-        load_a_scales(0, QUADRANTS[:2])
-        load_grad(0, 1)
         load_a(0)
-        load_a_scales(0, QUADRANTS[2:3])
-        load_balance()
-        load_a_scales(0, QUADRANTS[3:])
         load_w(0)
         load_w_scales(QUADRANTS[2:])
+        load_grad(0, 0)
         load_values(0)
         load_w(1)
-        load_values(1)
+        load_balance()
+        load_grad(0, 1)
         load_base(0)
-        load_a(1)
+        load_values(1)
         load_base(1)
         load_grad(1, 0)
         load_base(2)
+        load_a(1)
         load_base(3)
         load_grad(1, 1)
 
-        for pair in range(2):
-            warm_up(WARM_PASSES[pair])
-            for h in range(PASSES):
-                part_rows(0, h, 2 * pair, 2 * pair + 2, on_vector)
-            for h in range(PASSES):
-                turn(0, h, pair)
-        spread_balance()
+        warm_up(WARM_PASSES)
+        for q in QUADRANTS:
+            order_scales(0, slice(32 * q, 32 * q + 4), slice(0, 2), on_vector)
         order_codes(0, on_vector)
-        order_scales(0, on_vector)
-        load_a(2)
+        nc.vector.memset(a_staged[1][:], 0)
         load_prob(0)
-        load_a_scales(1, QUADRANTS)
-        order_scales(1, on_vector)
-        x_tiles(TILES)
         for h in range(PASSES):
-            quantize_grad(0, h, h + 1)
-            interleave_values(h)
+            part_rows(0, h, 0, 2, on_vector)
+        interleave_values(0)
+        x_banks(HEAD_BANKS[0])
+        for h in range(PASSES):
+            turn(0, h, 0)
+        for h in range(PASSES):
+            part_rows(0, h, 2, 4, on_vector)
         quantize_values(0)
-        order_codes(1, on_vector)
+        x_banks(HEAD_BANKS[1])
+        for h in range(PASSES):
+            turn(0, h, 1)
+        spread_balance()
+        x_banks(HEAD_BANKS[2])
+        interleave_values(1)
+        quantize_grad(0, 0, 1)
         quantize_values(1)
-        x_tiles(HEAD_TILES - TILES)
-        quantize_call(0)
+        quantize_grad(0, 1, 2)
+        quantize_x(0)
 
         for g in range(LAST):
             utilities(g)
             if g == 0:
                 part_on_scalar(1)
             part_on_gpsimd(g + 1)
-            if g == 1:
-                order_scales(2, on_gpsimd)
-                order_scales(3, on_gpsimd)
-            else:
-                order_codes(2 + g // 2, on_gpsimd)
+            order_codes(g + 1, on_gpsimd)
             if g == 0:
+                load_a(2)
+                load_a_scales(1, QUADRANTS)
                 load_grad(2, 0)
                 load_grad(2, 1)
             load_prob(g + 1)
@@ -388,28 +387,32 @@ def tile_router_weight_gradient_s12_kernel(
             for h in range(PASSES):
                 for pair in range(2):
                     turn(g + 1, h, pair)
-            quantize_call(2 * g + 1)
-            weigh(g, 0, HALF)
+            if g > 0:
+                quantize_l(g - 1)
+            else:
+                order_scales(1, slice(0, P), slice(0, 2), on_vector)
+            weigh(g, 0, SPLIT)
             quantize_grad(g + 1, 0, PASSES)
-            weigh(g, HALF, E)
-            x_tiles(ROUND_TILES[g] - 1)
+            weigh(g, SPLIT, E)
+            x_banks(ROUND_BANKS[g] - 1)
             if g + 2 < GROUPS:
                 part_on_scalar(g + 2)
-            x_tiles(1)
-            if g + 1 < LAST:
-                quantize_call(2 * g + 2)
+            x_banks(1)
+            if g == 0:
+                quantize_x(2)
 
         utilities(LAST)
-        x_tiles(X_TILES - len(made))
-        quantize_call(2 * LAST)
+        x_banks(2 * len(PAIRS) - len(made))
+        quantize_l(LAST - 1)
+        quantize_x(4)
         weigh(LAST, 0, E)
-        for n in range(2 * LAST + 1, len(CALLS)):
-            quantize_call(n)
+        quantize_x(5)
+        quantize_l(LAST)
+        for n in (1, 3, 6, 7):
+            quantize_x(n)
         banks = [next_bank() for j in range(EARLY)]
-        for some in (range(0, EARLY // 2), range(EARLY // 2, EARLY)):
-            for g in range(LAST):
-                for j in some:
-                    final_passes(banks[j], j, 0, E, [g])
+        for j in range(EARLY):
+            final_passes(banks[j], j, 0, E, range(LAST))
         for j in range(TILES - 1):
             if j >= EARLY:
                 banks.append(next_bank())

@@ -27,8 +27,8 @@ HALF = E // 2
 ALIGN = 64
 TILES = D // P
 QUADRANTS = (0, 2, 1, 3)
-HEAD_BANKS = (4, 2, 2)
-ROUND_BANKS = (6, 5, 5)
+HEAD_BANKS = 9
+ROUND_BANKS = (5, 5, 5)
 PIECE = 4
 PAIRS = (
     [(g, n) for g in (0, 1) for n in range(4)]
@@ -37,11 +37,11 @@ PAIRS = (
 )
 NARROW_PAIRS = 12
 SPLIT = 320
-POOL_ROWS = 2
+POOL_ROWS = 1
 EARLY = 3
 STORE_BUFFERS = 6
 WARM_N = 512
-WARM_PASSES = 4
+WARM_PASSES = (3, 2)
 
 
 def tile_router_weight_gradient_s12_kernel(
@@ -98,7 +98,7 @@ def tile_router_weight_gradient_s12_kernel(
         staged_out = [keep("staged_out%d" % n, [P, E], F32) for n in range(STORE_BUFFERS)]
 
         parted = [[[g_parted[h][:, 2 * s : 2 * s + 2] for s in range(PACK)] for h in range(PASSES)] for g in range(GROUPS)]
-        spent = [None, x_wide[0][:].bitcast(F32), x_wide[2][:].bitcast(F32), shifted[1][:, PACK * SPLIT :]]
+        spent = [None, x_wide[0][:].bitcast(F32), shifted[0][:, PACK * SPLIT :], shifted[1][:, PACK * SPLIT :]]
         for g in range(1, GROUPS):
             for r in range(POOL_ROWS):
                 row = spent[g][:, 2 * P * r : 2 * P * (r + 1)]
@@ -234,8 +234,7 @@ def tile_router_weight_gradient_s12_kernel(
         def utilities(g):
             dst = shifted[g % 2][:].rearrange("p (c t i) -> p c t i", t=PACK, i=4)
             banks = [next_bank() for t in range(PACK)]
-            steps = [(t, h) for t in range(PACK) for h in range(PASSES)]
-            for t, h in sorted(steps, key=lambda step: step[1]) if g == 0 else steps:
+            for t, h in [(t, h) for t in range(PACK) for h in range(PASSES)]:
                 tokens = slice(GROUP * h + P * t, GROUP * h + P * (t + 1))
                 nc.tensor.matmul_mx(
                     out=banks[t][:],
@@ -318,54 +317,54 @@ def tile_router_weight_gradient_s12_kernel(
 
         nc.vector.memset(w_plane[:].bitcast(I32), 0)
         nc.vector.memset(v_wide[0][:].bitcast(I32), 0)
-        nc.vector.memset(a_planes[0][:].bitcast(I32), 0)
+        nc.vector.memset(a_staged[0][:], 0)
         quantize(warm_codes[:], warm_plane[:], v_wide[0][:])
         nc.vector.memset(ident[:], 0.0)
         make_identity(nc, ident[:], nomemset=True)
 
-        load_a_scales(0, QUADRANTS)
+        nc.vector.memset(a_staged[1][:], 0)
+
+        load_grad(0, 0)
         load_w_scales(QUADRANTS[:2])
+        load_a_scales(0, QUADRANTS[:2])
+        load_grad(0, 1)
         load_a(0)
+        load_a_scales(0, QUADRANTS[2:3])
+        load_balance()
+        load_a_scales(0, QUADRANTS[3:])
         load_w(0)
         load_w_scales(QUADRANTS[2:])
-        load_grad(0, 0)
         load_values(0)
         load_w(1)
-        load_balance()
-        load_grad(0, 1)
-        load_base(0)
         load_values(1)
+        load_base(0)
+        load_a(1)
         load_base(1)
         load_grad(1, 0)
         load_base(2)
-        load_a(1)
         load_base(3)
         load_grad(1, 1)
 
-        warm_up(WARM_PASSES)
-        for q in QUADRANTS:
-            order_scales(0, slice(32 * q, 32 * q + 4), slice(0, 2), on_vector)
-        order_codes(0, on_vector)
-        nc.vector.memset(a_staged[1][:], 0)
-        load_prob(0)
-        for h in range(PASSES):
-            part_rows(0, h, 0, 2, on_vector)
-        interleave_values(0)
-        x_banks(HEAD_BANKS[0])
-        for h in range(PASSES):
-            turn(0, h, 0)
-        for h in range(PASSES):
-            part_rows(0, h, 2, 4, on_vector)
-        quantize_values(0)
-        x_banks(HEAD_BANKS[1])
-        for h in range(PASSES):
-            turn(0, h, 1)
+        for pair in range(2):
+            warm_up(WARM_PASSES[pair])
+            for h in range(PASSES):
+                part_rows(0, h, 2 * pair, 2 * pair + 2, on_vector)
+            for h in range(PASSES):
+                turn(0, h, pair)
         spread_balance()
-        x_banks(HEAD_BANKS[2])
-        interleave_values(1)
-        quantize_grad(0, 0, 1)
+        order_codes(0, on_vector)
+        order_scales(0, slice(0, P), slice(0, 2), on_vector)
+        load_a(2)
+        load_prob(0)
+        load_a_scales(1, QUADRANTS)
+        x_banks(TILES)
+        for h in range(PASSES):
+            quantize_grad(0, h, h + 1)
+            interleave_values(h)
+        quantize_values(0)
+        order_codes(1, on_vector)
         quantize_values(1)
-        quantize_grad(0, 1, 2)
+        x_banks(HEAD_BANKS - TILES)
         quantize_x(0)
 
         for g in range(LAST):
@@ -373,10 +372,11 @@ def tile_router_weight_gradient_s12_kernel(
             if g == 0:
                 part_on_scalar(1)
             part_on_gpsimd(g + 1)
-            order_codes(g + 1, on_gpsimd)
+            if g == 1:
+                order_scales(1, slice(0, P), slice(0, 2), on_gpsimd)
+            else:
+                order_codes(2 + g // 2, on_gpsimd)
             if g == 0:
-                load_a(2)
-                load_a_scales(1, QUADRANTS)
                 load_grad(2, 0)
                 load_grad(2, 1)
             load_prob(g + 1)
@@ -390,7 +390,7 @@ def tile_router_weight_gradient_s12_kernel(
             if g > 0:
                 quantize_l(g - 1)
             else:
-                order_scales(1, slice(0, P), slice(0, 2), on_vector)
+                quantize_x(1)
             weigh(g, 0, SPLIT)
             quantize_grad(g + 1, 0, PASSES)
             weigh(g, SPLIT, E)
@@ -398,17 +398,16 @@ def tile_router_weight_gradient_s12_kernel(
             if g + 2 < GROUPS:
                 part_on_scalar(g + 2)
             x_banks(1)
-            if g == 0:
-                quantize_x(2)
 
         utilities(LAST)
         x_banks(2 * len(PAIRS) - len(made))
         quantize_l(LAST - 1)
+        quantize_x(2)
         quantize_x(4)
         weigh(LAST, 0, E)
         quantize_x(5)
         quantize_l(LAST)
-        for n in (1, 3, 6, 7):
+        for n in (3, 6, 7):
             quantize_x(n)
         banks = [next_bank() for j in range(EARLY)]
         for j in range(EARLY):

@@ -27,18 +27,16 @@ HALF = E // 2
 ALIGN = 64
 TILES = D // P
 QUADRANTS = (0, 2, 1, 3)
-HEAD_BANKS = 9
-ROUND_BANKS = (5, 5, 5)
+ROUND_BANKS = (6, 6, 6)
 PIECE = 4
 PAIRS = (
     [(g, n) for g in (0, 1) for n in range(4)]
     + [(g, n) for g in (2, 3) for n in (0, 1)]
     + [(g, n) for n in (2, 3) for g in (2, 3)]
 )
-NARROW_PAIRS = 12
 SPLIT = 320
-POOL_ROWS = 1
-EARLY = 3
+SCALAR_ROWS = 3
+EARLY = 4
 STORE_BUFFERS = 6
 WARM_N = 512
 WARM_PASSES = (3, 2)
@@ -78,8 +76,9 @@ def tile_router_weight_gradient_s12_kernel(
         w_codes = [keep("w_codes%d" % n, [P, PASSES, D], U8) for n in range(2)]
         w_plane = keep("w_plane", [P, PASSES, D], U8)
 
-        g_raw = [keep("g_raw%d" % g, [P, PACK, D], BF16) for g in range(2)] * 2
-        g_parted = [keep("g_parted%d" % h, [P, 2 * PACK, P], F32) for h in range(PASSES)]
+        g_raw = [keep("g_raw%d" % g, [P, PACK, D], BF16) for g in range(LAST)]
+        g_raw = g_raw[:2] + [g_raw[0], g_raw[2]]
+        g_parted = [keep("g_parted%d" % n, [P, PASSES * 4 * P], F32) for n in range(2)]
         g_wide = [keep("g_wide%d" % g, [P, PASSES * GROUP * PACK], BF16) for g in range(2)] * 2
         g_codes = [keep("g_codes%d" % g, [P, PASSES * GROUP], U32) for g in range(2)] * 2
         g_planes = [keep("g_plane%d" % g, [P, PASSES * GROUP], U8) for g in range(2)] * 2
@@ -97,12 +96,7 @@ def tile_router_weight_gradient_s12_kernel(
         x_planes = [keep("x_plane%d" % n, [P, PIECE * P], U8) for n in range(len(PAIRS) // 2)]
         staged_out = [keep("staged_out%d" % n, [P, E], F32) for n in range(STORE_BUFFERS)]
 
-        parted = [[[g_parted[h][:, 2 * s : 2 * s + 2] for s in range(PACK)] for h in range(PASSES)] for g in range(GROUPS)]
-        spent = [None, x_wide[0][:].bitcast(F32), shifted[0][:, PACK * SPLIT :], shifted[1][:, PACK * SPLIT :]]
-        for g in range(1, GROUPS):
-            for r in range(POOL_ROWS):
-                row = spent[g][:, 2 * P * r : 2 * P * (r + 1)]
-                parted[g][1][PACK - POOL_ROWS + r] = row.rearrange("p (u w) -> p u w", u=2)
+        spent = [None, x_wide[0][:].bitcast(F32), x_wide[2][:].bitcast(F32), shifted[1][:, PACK * SPLIT :]]
 
         def load_a(g):
             src = a_words.rearrange("h p n -> p h n")[:, :, 2 * GROUP * g : 2 * GROUP * (g + 1)]
@@ -190,34 +184,41 @@ def tile_router_weight_gradient_s12_kernel(
                 g, n = PAIRS[k]
                 words = x_wide[k // 2][:, 2 * BANK * (k % 2) : 2 * BANK * (k % 2 + 1)].rearrange("p (d t) -> p d t", t=PACK)
                 bank = next_bank()
-                if k < NARROW_PAIRS:
-                    for t in range(PACK):
-                        x_passes(bank[:, P * t : P * (t + 1)], g, t, 2 * n + u, P)
-                    nc.scalar.copy(out=words[:, P * u : P * (u + 1)], in_=bank[:].rearrange("p (t d) -> p d t", t=PACK))
-                else:
-                    for e in range(2):
-                        x_passes(bank[:, 2 * P * e : 2 * P * (e + 1)], g, 2 * u + e, 2 * n, 2 * P)
-                    nc.scalar.copy(out=words[:, :, 2 * u : 2 * u + 2], in_=bank[:].rearrange("p (e d) -> p d e", e=2))
+                for t in range(PACK):
+                    x_passes(bank[:, P * t : P * (t + 1)], g, t, 2 * n + u, P)
+                nc.scalar.copy(out=words[:, P * u : P * (u + 1)], in_=bank[:].rearrange("p (t d) -> p d t", t=PACK))
 
         def grad_words(g):
             return g_raw[g][:].bitcast(F32).rearrange("p s (h w u) -> p h s u w", h=PASSES, u=2)
 
-        def part_rows(g, h, lo, hi, copy):
-            dst = g_parted[h][:, 2 * lo : 2 * hi].rearrange("p (s u) w -> p s u w", u=2)
-            copy(out=dst, in_=grad_words(g)[:, h, lo:hi])
+        def parted(pair):
+            return g_parted[pair][:].rearrange("p (h s u w) -> p h s u w", h=PASSES, s=2, u=2)
+
+        def part_rows(g, pair, rows, copy):
+            copy(out=parted(pair)[:, :, 0:rows], in_=grad_words(g)[:, :, 2 * pair : 2 * pair + rows])
 
         def part_on_scalar(g):
-            part_rows(g, 0, 0, PACK, on_scalar)
-            part_rows(g, 1, 0, PACK - POOL_ROWS, on_scalar)
+            part_rows(g, 0, 2, on_scalar)
+            if SCALAR_ROWS > 2:
+                part_rows(g, 1, SCALAR_ROWS - 2, on_scalar)
+
+        def pool_row(g):
+            return spent[g][:, 0 : 2 * P].rearrange("p (u w) -> p u w", u=2)
 
         def part_on_gpsimd(g):
-            dst = spent[g][:, 0 : 2 * P * POOL_ROWS].rearrange("p (s u w) -> p s u w", s=POOL_ROWS, u=2)
-            on_gpsimd(out=dst, in_=grad_words(g)[:, 1, PACK - POOL_ROWS : PACK])
+            on_gpsimd(out=pool_row(g), in_=grad_words(g)[:, PASSES - 1, PACK - 1])
+
+        def words_to_turn(g, h, s, u):
+            if g == 0 or s < SCALAR_ROWS:
+                return parted(s // 2)[:, h, s % 2, u]
+            if (h, s) == (PASSES - 1, PACK - 1):
+                return pool_row(g)[:, u]
+            return grad_words(g)[:, h, s, u]
 
         def turn(g, h, pair):
             bank = next_bank()
             for q in range(4):
-                words = parted[g][h][2 * pair + q // 2][:, q % 2, :]
+                words = words_to_turn(g, h, 2 * pair + q // 2, q % 2)
                 nc.tensor.transpose(bank[:, P * q : P * (q + 1)], words, ident[:])
             dst = g_wide[g][:].bitcast(F32).rearrange("p (h t c w) -> p h t c w", h=PASSES, t=PACK, w=8)
             nc.scalar.copy(
@@ -347,8 +348,7 @@ def tile_router_weight_gradient_s12_kernel(
 
         for pair in range(2):
             warm_up(WARM_PASSES[pair])
-            for h in range(PASSES):
-                part_rows(0, h, 2 * pair, 2 * pair + 2, on_vector)
+            part_rows(0, pair, 2, on_vector)
             for h in range(PASSES):
                 turn(0, h, pair)
         spread_balance()
@@ -362,9 +362,8 @@ def tile_router_weight_gradient_s12_kernel(
             quantize_grad(0, h, h + 1)
             interleave_values(h)
         quantize_values(0)
-        order_codes(1, on_vector)
         quantize_values(1)
-        x_banks(HEAD_BANKS - TILES)
+        order_codes(1, on_vector)
         quantize_x(0)
 
         for g in range(LAST):
@@ -384,13 +383,11 @@ def tile_router_weight_gradient_s12_kernel(
                 load_a(3)
                 load_grad(3, 0)
                 load_grad(3, 1)
-            for h in range(PASSES):
-                for pair in range(2):
+            for pair in range(2):
+                for h in range(PASSES):
                     turn(g + 1, h, pair)
             if g > 0:
                 quantize_l(g - 1)
-            else:
-                quantize_x(1)
             weigh(g, 0, SPLIT)
             quantize_grad(g + 1, 0, PASSES)
             weigh(g, SPLIT, E)
@@ -398,16 +395,16 @@ def tile_router_weight_gradient_s12_kernel(
             if g + 2 < GROUPS:
                 part_on_scalar(g + 2)
             x_banks(1)
+            if g != 1:
+                quantize_x(2 + g)
 
         utilities(LAST)
         x_banks(2 * len(PAIRS) - len(made))
         quantize_l(LAST - 1)
-        quantize_x(2)
-        quantize_x(4)
         weigh(LAST, 0, E)
         quantize_x(5)
         quantize_l(LAST)
-        for n in (3, 6, 7):
+        for n in (1, 3, 6, 7):
             quantize_x(n)
         banks = [next_bank() for j in range(EARLY)]
         for j in range(EARLY):
@@ -416,7 +413,7 @@ def tile_router_weight_gradient_s12_kernel(
             if j >= EARLY:
                 banks.append(next_bank())
             final_passes(banks[j], j, 0, E, [LAST] if j < EARLY else range(GROUPS))
-            store(banks[j], j, 0, E, on_scalar if j % 2 == 0 else on_vector)
+            store(banks[j], j, 0, E, on_vector if j == 5 else on_scalar)
         for lo, copy in ((0, on_vector), (HALF, on_scalar)):
             bank = next_bank()
             final_passes(bank, TILES - 1, lo, lo + HALF, range(GROUPS))

@@ -27,6 +27,7 @@ HALF = E // 2
 ALIGN = 64
 TILES = D // P
 QUADRANTS = (0, 2, 1, 3)
+HEAD_BANKS = 8
 ROUND_BANKS = (6, 6, 6)
 PIECE = 4
 PAIRS = (
@@ -37,7 +38,6 @@ PAIRS = (
 SPLIT = 320
 SCALAR_ROWS = 3
 EARLY = 4
-STORE_BUFFERS = 6
 WARM_N = 512
 WARM_PASSES = (3, 2)
 
@@ -94,7 +94,7 @@ def tile_router_weight_gradient_s12_kernel(
         x_wide = [keep("x_wide%d" % n, [P, PIECE * BANK], BF16) for n in range(len(PAIRS) // 2)]
         x_codes = [keep("x_codes%d" % n, [P, PIECE * P], U32) for n in range(len(PAIRS) // 2)]
         x_planes = [keep("x_plane%d" % n, [P, PIECE * P], U8) for n in range(len(PAIRS) // 2)]
-        staged_out = [keep("staged_out%d" % n, [P, E], F32) for n in range(STORE_BUFFERS)]
+        staged_out = [keep("staged_out%d" % n, [P, E], F32) for n in range(TILES)]
 
         spent = [None, x_wide[0][:].bitcast(F32), x_wide[2][:].bitcast(F32), shifted[1][:, PACK * SPLIT :]]
 
@@ -148,6 +148,10 @@ def tile_router_weight_gradient_s12_kernel(
                 out=a_planes[n][rows].bitcast(I32)[:, groups],
                 in_=a_staged[n][rows].rearrange("p h (g c t) -> p g t h c", g=2, t=PACK)[:, groups],
             )
+
+        def order_quadrants(quadrants):
+            for q in quadrants:
+                order_scales(0, slice(32 * q, 32 * q + 4), slice(0, 2), on_vector)
 
         def quantize(dst, plane, src):
             nc.vector.quantize_mx(out=dst.bitcast(FP8X4), scales=plane, in_=src)
@@ -235,7 +239,8 @@ def tile_router_weight_gradient_s12_kernel(
         def utilities(g):
             dst = shifted[g % 2][:].rearrange("p (c t i) -> p c t i", t=PACK, i=4)
             banks = [next_bank() for t in range(PACK)]
-            for t, h in [(t, h) for t in range(PACK) for h in range(PASSES)]:
+            steps = [(t, h) for t in range(PACK) for h in range(PASSES)]
+            for t, h in sorted(steps, key=lambda step: step[1]) if g == 0 else steps:
                 tokens = slice(GROUP * h + P * t, GROUP * h + P * (t + 1))
                 nc.tensor.matmul_mx(
                     out=banks[t][:],
@@ -295,11 +300,8 @@ def tile_router_weight_gradient_s12_kernel(
                     stop=(g == LAST),
                 )
 
-        stored = []
-
         def store(bank, j, lo, hi, copy):
-            staged = staged_out[len(stored) % STORE_BUFFERS][:, 0 : hi - lo]
-            stored.append(j)
+            staged = staged_out[j][:, lo:hi]
             copy(out=staged, in_=bank[:, 0 : hi - lo])
             nc.sync.dma_start(out=out.rearrange("(j p) e -> p j e", p=P)[:, j, lo:hi], in_=staged)
 
@@ -318,23 +320,22 @@ def tile_router_weight_gradient_s12_kernel(
 
         nc.vector.memset(w_plane[:].bitcast(I32), 0)
         nc.vector.memset(v_wide[0][:].bitcast(I32), 0)
-        nc.vector.memset(a_staged[0][:], 0)
         quantize(warm_codes[:], warm_plane[:], v_wide[0][:])
         nc.vector.memset(ident[:], 0.0)
         make_identity(nc, ident[:], nomemset=True)
 
+        nc.vector.memset(a_planes[0][:].bitcast(I32), 0)
         nc.vector.memset(a_staged[1][:], 0)
 
+        load_balance()
         load_grad(0, 0)
-        load_w_scales(QUADRANTS[:2])
         load_a_scales(0, QUADRANTS[:2])
+        load_w_scales(QUADRANTS[:2])
         load_grad(0, 1)
         load_a(0)
-        load_a_scales(0, QUADRANTS[2:3])
-        load_balance()
-        load_a_scales(0, QUADRANTS[3:])
-        load_w(0)
+        load_a_scales(0, QUADRANTS[2:])
         load_w_scales(QUADRANTS[2:])
+        load_w(0)
         load_values(0)
         load_w(1)
         load_values(1)
@@ -349,21 +350,24 @@ def tile_router_weight_gradient_s12_kernel(
         for pair in range(2):
             warm_up(WARM_PASSES[pair])
             part_rows(0, pair, 2, on_vector)
+            if pair == 0:
+                order_quadrants(QUADRANTS[:2])
             for h in range(PASSES):
                 turn(0, h, pair)
         spread_balance()
         order_codes(0, on_vector)
-        order_scales(0, slice(0, P), slice(0, 2), on_vector)
+        order_quadrants(QUADRANTS[2:])
         load_a(2)
         load_prob(0)
         load_a_scales(1, QUADRANTS)
-        x_banks(TILES)
-        for h in range(PASSES):
-            quantize_grad(0, h, h + 1)
-            interleave_values(h)
+        x_banks(HEAD_BANKS)
+        quantize_grad(0, 0, 1)
+        interleave_values(0)
+        quantize_grad(0, 1, 2)
         quantize_values(0)
-        quantize_values(1)
+        interleave_values(1)
         order_codes(1, on_vector)
+        quantize_values(1)
         quantize_x(0)
 
         for g in range(LAST):
@@ -414,7 +418,7 @@ def tile_router_weight_gradient_s12_kernel(
                 banks.append(next_bank())
             final_passes(banks[j], j, 0, E, [LAST] if j < EARLY else range(GROUPS))
             store(banks[j], j, 0, E, on_vector if j == 5 else on_scalar)
-        for lo, copy in ((0, on_vector), (HALF, on_scalar)):
+        for lo, hi, copy in ((0, HALF, on_vector), (HALF, HALF + P, on_scalar), (HALF + P, E, on_vector)):
             bank = next_bank()
-            final_passes(bank, TILES - 1, lo, lo + HALF, range(GROUPS))
-            store(bank, TILES - 1, lo, lo + HALF, copy)
+            final_passes(bank, TILES - 1, lo, hi, range(GROUPS))
+            store(bank, TILES - 1, lo, hi, copy)

@@ -149,10 +149,6 @@ def tile_router_weight_gradient_s12_kernel(
                 in_=a_staged[n][rows].rearrange("p h (g c t) -> p g t h c", g=2, t=PACK)[:, groups],
             )
 
-        def order_quadrants(quadrants):
-            for q in quadrants:
-                order_scales(0, slice(32 * q, 32 * q + 4), slice(0, 2), on_vector)
-
         def quantize(dst, plane, src):
             nc.vector.quantize_mx(out=dst.bitcast(FP8X4), scales=plane, in_=src)
 
@@ -320,22 +316,23 @@ def tile_router_weight_gradient_s12_kernel(
 
         nc.vector.memset(w_plane[:].bitcast(I32), 0)
         nc.vector.memset(v_wide[0][:].bitcast(I32), 0)
+        nc.vector.memset(a_staged[0][:], 0)
         quantize(warm_codes[:], warm_plane[:], v_wide[0][:])
         nc.vector.memset(ident[:], 0.0)
         make_identity(nc, ident[:], nomemset=True)
 
-        nc.vector.memset(a_planes[0][:].bitcast(I32), 0)
         nc.vector.memset(a_staged[1][:], 0)
 
-        load_balance()
         load_grad(0, 0)
-        load_a_scales(0, QUADRANTS[:2])
         load_w_scales(QUADRANTS[:2])
+        load_a_scales(0, QUADRANTS[:2])
         load_grad(0, 1)
         load_a(0)
-        load_a_scales(0, QUADRANTS[2:])
-        load_w_scales(QUADRANTS[2:])
+        load_a_scales(0, QUADRANTS[2:3])
+        load_balance()
+        load_a_scales(0, QUADRANTS[3:])
         load_w(0)
+        load_w_scales(QUADRANTS[2:])
         load_values(0)
         load_w(1)
         load_values(1)
@@ -350,13 +347,11 @@ def tile_router_weight_gradient_s12_kernel(
         for pair in range(2):
             warm_up(WARM_PASSES[pair])
             part_rows(0, pair, 2, on_vector)
-            if pair == 0:
-                order_quadrants(QUADRANTS[:2])
             for h in range(PASSES):
                 turn(0, h, pair)
         spread_balance()
         order_codes(0, on_vector)
-        order_quadrants(QUADRANTS[2:])
+        order_scales(0, slice(0, P), slice(0, 2), on_vector)
         load_a(2)
         load_prob(0)
         load_a_scales(1, QUADRANTS)

@@ -72,7 +72,7 @@ def tile_router_weight_gradient_s12_kernel(
         a_raw = [keep("a_raw%d" % g, [P, PASSES, 256], I32) for g in range(2)] * 2
         a_codes = [keep("a_codes%d" % g, [P, PACK, PASSES, 2 * P], U8) for g in range(GROUPS)]
         a_staged = [keep("a_staged%d" % n, [P, PASSES, 256], I32) for n in range(2)]
-        a_planes = [keep("a_plane%d" % n, [P, 2, PACK, PASSES, P], U8) for n in range(2)]
+        a_planes = [keep("a_plane%d" % n, [P, PACK, PASSES, 2, P], U8) for n in range(2)]
         w_codes = [keep("w_codes%d" % n, [P, PASSES, D], U8) for n in range(2)]
         w_plane = keep("w_plane", [P, PASSES, D], U8)
 
@@ -139,14 +139,14 @@ def tile_router_weight_gradient_s12_kernel(
 
         def order_codes(g, copy):
             copy(
-                out=a_codes[g][:].bitcast(I32).rearrange("p t h (c w) -> p t (h c) w", w=2),
-                in_=a_raw[g][:].rearrange("p h (c t w) -> p t (h c) w", t=PACK, w=2),
+                out=a_codes[g][:].bitcast(I32).rearrange("p t h (b i w) -> p (h b) t i w", i=2, w=2),
+                in_=a_raw[g][:].rearrange("p h (b i t w) -> p (h b) t i w", i=2, t=PACK, w=2),
             )
 
-        def order_scales(n, rows, groups, copy):
+        def order_scales(n, copy):
             copy(
-                out=a_planes[n][rows].bitcast(I32)[:, groups],
-                in_=a_staged[n][rows].rearrange("p h (g c t) -> p g t h c", g=2, t=PACK)[:, groups],
+                out=a_planes[n][:].bitcast(I32).rearrange("p t h g (b i) -> p (h g b) t i", i=4),
+                in_=a_staged[n][:].rearrange("p h (x i t) -> p (h x) t i", i=4, t=PACK),
             )
 
         def quantize(dst, plane, src):
@@ -168,7 +168,7 @@ def tile_router_weight_gradient_s12_kernel(
                 nc.tensor.matmul_mx(
                     out=dst,
                     lhsT=a_codes[g][:, t, h, :].bitcast(FP4X4),
-                    lhsT_scale=a_planes[g // 2][:, g % 2, t, h, :],
+                    lhsT_scale=a_planes[g // 2][:, t, h, g % 2, :],
                     rhs=w_codes[n][:, h, 2 * P * jj : 2 * (P * jj + width)].bitcast(FP4X4),
                     rhs_scale=w_plane[:, h, P * j : P * j + width],
                     start=(h == 0),
@@ -188,32 +188,35 @@ def tile_router_weight_gradient_s12_kernel(
                     x_passes(bank[:, P * t : P * (t + 1)], g, t, 2 * n + u, P)
                 nc.scalar.copy(out=words[:, P * u : P * (u + 1)], in_=bank[:].rearrange("p (t d) -> p d t", t=PACK))
 
-        def grad_words(g):
-            return g_raw[g][:].bitcast(F32).rearrange("p s (h w u) -> p h s u w", h=PASSES, u=2)
+        def part(dst, src, copy):
+            copy(out=dst.rearrange("p u (x i) -> p x u i", i=4), in_=src.rearrange("p (x i u) -> p x u i", i=4, u=2))
+
+        def grad_words(g, lo, hi):
+            return g_raw[g][:, lo:hi].rearrange("p s d -> p (s d)").bitcast(F32)
 
         def parted(pair):
-            return g_parted[pair][:].rearrange("p (h s u w) -> p h s u w", h=PASSES, s=2, u=2)
+            return g_parted[pair][:].rearrange("p (u w) -> p u w", u=2)
 
         def part_rows(g, pair, rows, copy):
-            copy(out=parted(pair)[:, :, 0:rows], in_=grad_words(g)[:, :, 2 * pair : 2 * pair + rows])
+            part(parted(pair)[:, :, 0 : 2 * P * rows], grad_words(g, 2 * pair, 2 * pair + rows), copy)
 
         def part_on_scalar(g):
             part_rows(g, 0, 2, on_scalar)
-            if SCALAR_ROWS > 2:
-                part_rows(g, 1, SCALAR_ROWS - 2, on_scalar)
+            part_rows(g, 1, SCALAR_ROWS - 2, on_scalar)
 
         def pool_row(g):
             return spent[g][:, 0 : 2 * P].rearrange("p (u w) -> p u w", u=2)
 
         def part_on_gpsimd(g):
-            on_gpsimd(out=pool_row(g), in_=grad_words(g)[:, PASSES - 1, PACK - 1])
+            part(pool_row(g), grad_words(g, PACK - 1, PACK)[:, 2 * P :], on_gpsimd)
 
         def words_to_turn(g, h, s, u):
             if g == 0 or s < SCALAR_ROWS:
-                return parted(s // 2)[:, h, s % 2, u]
-            if (h, s) == (PASSES - 1, PACK - 1):
+                first = P * (PASSES * (s % 2) + h)
+                return parted(s // 2)[:, u, first : first + P]
+            if h == PASSES - 1:
                 return pool_row(g)[:, u]
-            return grad_words(g)[:, h, s, u]
+            return grad_words(g, s, s + 1)[:, u : 2 * P : 2]
 
         def turn(g, h, pair):
             bank = next_bank()
@@ -351,7 +354,7 @@ def tile_router_weight_gradient_s12_kernel(
                 turn(0, h, pair)
         spread_balance()
         order_codes(0, on_vector)
-        order_scales(0, slice(0, P), slice(0, 2), on_vector)
+        order_scales(0, on_vector)
         load_a(2)
         load_prob(0)
         load_a_scales(1, QUADRANTS)
@@ -371,7 +374,7 @@ def tile_router_weight_gradient_s12_kernel(
                 part_on_scalar(1)
             part_on_gpsimd(g + 1)
             if g == 1:
-                order_scales(1, slice(0, P), slice(0, 2), on_gpsimd)
+                order_scales(1, on_gpsimd)
             else:
                 order_codes(2 + g // 2, on_gpsimd)
             if g == 0:

@@ -35,7 +35,7 @@ PAIRS = (
     + [(g, n) for g in (2, 3) for n in (0, 1)]
     + [(g, n) for n in (2, 3) for g in (2, 3)]
 )
-SPLIT = 320
+POOL_FROM = 384
 SCALAR_ROWS = 3
 EARLY = 4
 WARM_N = 512
@@ -91,12 +91,19 @@ def tile_router_weight_gradient_s12_kernel(
         l_wide = [keep("l_wide%d" % g, [P, E * PACK], BF16) for g in range(2)] * 2
         l_codes = [keep("l_codes%d" % g, [P, E], U32) for g in range(GROUPS)]
         l_planes = [keep("l_plane%d" % g, [P, E], U8) for g in range(GROUPS)]
-        x_wide = [keep("x_wide%d" % n, [P, PIECE * BANK], BF16) for n in range(len(PAIRS) // 2)]
+        x_room = [keep("x_wide%d" % n, [P, (PIECE + 1) * BANK], BF16) for n in range(len(PAIRS) // 2)]
+        x_wide = [room[:, BANK:] for room in x_room]
         x_codes = [keep("x_codes%d" % n, [P, PIECE * P], U32) for n in range(len(PAIRS) // 2)]
         x_planes = [keep("x_plane%d" % n, [P, PIECE * P], U8) for n in range(len(PAIRS) // 2)]
         staged_out = [keep("staged_out%d" % n, [P, E], F32) for n in range(TILES)]
 
-        spent = [None, x_wide[0][:].bitcast(F32), x_wide[2][:].bitcast(F32), shifted[1][:, PACK * SPLIT :]]
+        pool_row = x_wide[0].bitcast(F32)[:, 0 : 2 * P].rearrange("p (u w) -> p u w", u=2)
+        l_upper = [
+            x_room[2][:, 0 : 2 * BANK],
+            shifted[1][:, 3 * BANK // 2 : 5 * BANK // 2].bitcast(BF16),
+            x_room[4][:, 0 : 2 * BANK],
+            l_wide[LAST][:, 2 * BANK :],
+        ]
 
         def load_a(g):
             src = a_words.rearrange("h p n -> p h n")[:, :, 2 * GROUP * g : 2 * GROUP * (g + 1)]
@@ -204,19 +211,16 @@ def tile_router_weight_gradient_s12_kernel(
             part_rows(g, 0, 2, on_scalar)
             part_rows(g, 1, SCALAR_ROWS - 2, on_scalar)
 
-        def pool_row(g):
-            return spent[g][:, 0 : 2 * P].rearrange("p (u w) -> p u w", u=2)
-
-        def part_on_gpsimd(g):
-            part(pool_row(g), grad_words(g, PACK - 1, PACK)[:, 2 * P :], on_gpsimd)
+        def part_on_gpsimd():
+            part(pool_row, grad_words(1, PACK - 1, PACK)[:, 2 * P :], on_gpsimd)
 
         def words_to_turn(g, h, s, u):
             if g == 0 or s < SCALAR_ROWS:
                 first = P * (PASSES * (s % 2) + h)
                 return parted(s // 2)[:, u, first : first + P]
-            if h == PASSES - 1:
-                return pool_row(g)[:, u]
-            return grad_words(g, s, s + 1)[:, u : 2 * P : 2]
+            if (g, h) == (1, PASSES - 1):
+                return pool_row[:, u]
+            return grad_words(g, s, s + 1)[:, 2 * P * h + u : 2 * P * (h + 1) : 2]
 
         def turn(g, h, pair):
             bank = next_bank()
@@ -260,10 +264,11 @@ def tile_router_weight_gradient_s12_kernel(
                     op1=ALU.add,
                 )
 
-        def weigh(g, lo, hi):
+        def weigh(g, lo, hi, engine):
             cs = slice(lo // 4, hi // 4)
-            nc.vector.tensor_tensor(
-                out=l_wide[g][:].rearrange("p (c i t) -> p c t i", i=4, t=PACK)[:, cs],
+            dst = l_wide[g][:, PACK * lo : PACK * hi] if lo < HALF else l_upper[g][:, PACK * (lo - HALF) : PACK * (hi - HALF)]
+            engine.tensor_tensor(
+                out=dst.rearrange("p (c i t) -> p c t i", i=4, t=PACK),
                 in0=shifted[g % 2][:].rearrange("p (c t i) -> p c t i", t=PACK, i=4)[:, cs],
                 in1=p_sb[g][:].rearrange("p t (c i) -> p c t i", i=4)[:, cs],
                 op=ALU.mult,
@@ -280,10 +285,14 @@ def tile_router_weight_gradient_s12_kernel(
             )
 
         def quantize_l(g):
-            quantize(l_codes[g][:], l_planes[g][:], l_wide[g][:])
+            if g == LAST:
+                quantize(l_codes[g][:], l_planes[g][:], l_wide[g][:])
+            else:
+                quantize(l_codes[g][:, 0:HALF], l_planes[g][:, 0:HALF], l_wide[g][:, 0 : 2 * BANK])
+                quantize(l_codes[g][:, HALF:], l_planes[g][:, HALF:], l_upper[g])
 
         def quantize_x(n):
-            quantize(x_codes[n][:], x_planes[n][:], x_wide[n][:])
+            quantize(x_codes[n][:], x_planes[n][:], x_wide[n])
 
         def final_passes(bank, j, lo, hi, groups):
             for g in groups:
@@ -364,15 +373,18 @@ def tile_router_weight_gradient_s12_kernel(
         quantize_grad(0, 1, 2)
         quantize_values(0)
         interleave_values(1)
-        order_codes(1, on_vector)
         quantize_values(1)
+        order_codes(1, on_vector)
         quantize_x(0)
 
         for g in range(LAST):
             utilities(g)
             if g == 0:
                 part_on_scalar(1)
-            part_on_gpsimd(g + 1)
+            if g == 0:
+                part_on_gpsimd()
+            else:
+                weigh(g - 1, POOL_FROM, E, nc.gpsimd)
             if g == 1:
                 order_scales(1, on_gpsimd)
             else:
@@ -390,9 +402,9 @@ def tile_router_weight_gradient_s12_kernel(
                     turn(g + 1, h, pair)
             if g > 0:
                 quantize_l(g - 1)
-            weigh(g, 0, SPLIT)
+            weigh(g, 0, HALF, nc.vector)
             quantize_grad(g + 1, 0, PASSES)
-            weigh(g, SPLIT, E)
+            weigh(g, HALF, POOL_FROM, nc.vector)
             x_banks(ROUND_BANKS[g] - 1)
             if g + 2 < GROUPS:
                 part_on_scalar(g + 2)
@@ -401,9 +413,10 @@ def tile_router_weight_gradient_s12_kernel(
                 quantize_x(2 + g)
 
         utilities(LAST)
+        weigh(LAST - 1, POOL_FROM, E, nc.gpsimd)
         x_banks(2 * len(PAIRS) - len(made))
         quantize_l(LAST - 1)
-        weigh(LAST, 0, E)
+        weigh(LAST, 0, E, nc.vector)
         quantize_x(5)
         quantize_l(LAST)
         for n in (1, 3, 6, 7):

@@ -184,7 +184,7 @@ def tile_router_weight_gradient_s12_kernel(
 
         made = []
 
-        def x_banks(count):
+        def x_banks(count, copy):
             for b in range(len(made), len(made) + count):
                 made.append(b)
                 k, u = divmod(b, 2)
@@ -193,7 +193,7 @@ def tile_router_weight_gradient_s12_kernel(
                 bank = next_bank()
                 for t in range(PACK):
                     x_passes(bank[:, P * t : P * (t + 1)], g, t, 2 * n + u, P)
-                nc.scalar.copy(out=words[:, P * u : P * (u + 1)], in_=bank[:].rearrange("p (t d) -> p d t", t=PACK))
+                copy(out=words[:, P * u : P * (u + 1)], in_=bank[:].rearrange("p (t d) -> p d t", t=PACK))
 
         def part(dst, src, copy):
             copy(out=dst.rearrange("p u (x i) -> p x u i", i=4), in_=src.rearrange("p (x i u) -> p x u i", i=4, u=2))
@@ -367,7 +367,7 @@ def tile_router_weight_gradient_s12_kernel(
         load_a(2)
         load_prob(0)
         load_a_scales(1, QUADRANTS)
-        x_banks(HEAD_BANKS)
+        x_banks(HEAD_BANKS, on_scalar)
         quantize_grad(0, 0, 1)
         interleave_values(0)
         quantize_grad(0, 1, 2)
@@ -405,16 +405,16 @@ def tile_router_weight_gradient_s12_kernel(
             weigh(g, 0, HALF, nc.vector)
             quantize_grad(g + 1, 0, PASSES)
             weigh(g, HALF, POOL_FROM, nc.vector)
-            x_banks(ROUND_BANKS[g] - 1)
+            x_banks(ROUND_BANKS[g] - 1, on_scalar)
             if g + 2 < GROUPS:
                 part_on_scalar(g + 2)
-            x_banks(1)
             if g != 1:
                 quantize_x(2 + g)
+            x_banks(1, on_vector)
 
         utilities(LAST)
         weigh(LAST - 1, POOL_FROM, E, nc.gpsimd)
-        x_banks(2 * len(PAIRS) - len(made))
+        x_banks(2 * len(PAIRS) - len(made), on_scalar)
         quantize_l(LAST - 1)
         weigh(LAST, 0, E, nc.vector)
         quantize_x(5)

@@ -36,7 +36,6 @@ PAIRS = (
     + [(g, n) for n in (2, 3) for g in (2, 3)]
 )
 POOL_FROM = 384
-SCALAR_ROWS = 3
 EARLY = 4
 WARM_N = 512
 WARM_PASSES = (3, 2)
@@ -204,23 +203,21 @@ def tile_router_weight_gradient_s12_kernel(
         def parted(pair):
             return g_parted[pair][:].rearrange("p (u w) -> p u w", u=2)
 
-        def part_rows(g, pair, rows, copy):
-            part(parted(pair)[:, :, 0 : 2 * P * rows], grad_words(g, 2 * pair, 2 * pair + rows), copy)
+        def part_passes(g, pair, count, copy):
+            part(parted(pair)[:, :, 0 : P * count], grad_words(g, 2 * pair, 2 * pair + 2)[:, 0 : 2 * P * count], copy)
 
         def part_on_scalar(g):
-            part_rows(g, 0, 2, on_scalar)
-            part_rows(g, 1, SCALAR_ROWS - 2, on_scalar)
+            part_passes(g, 0, 4, on_scalar)
+            part_passes(g, 1, 3 if g == 1 else 4, on_scalar)
 
         def part_on_gpsimd():
             part(pool_row, grad_words(1, PACK - 1, PACK)[:, 2 * P :], on_gpsimd)
 
         def words_to_turn(g, h, s, u):
-            if g == 0 or s < SCALAR_ROWS:
-                first = P * (PASSES * (s % 2) + h)
-                return parted(s // 2)[:, u, first : first + P]
-            if (g, h) == (1, PASSES - 1):
+            if (g, h, s) == (1, PASSES - 1, PACK - 1):
                 return pool_row[:, u]
-            return grad_words(g, s, s + 1)[:, 2 * P * h + u : 2 * P * (h + 1) : 2]
+            first = P * (PASSES * (s % 2) + h)
+            return parted(s // 2)[:, u, first : first + P]
 
         def turn(g, h, pair):
             bank = next_bank()
@@ -358,7 +355,7 @@ def tile_router_weight_gradient_s12_kernel(
 
         for pair in range(2):
             warm_up(WARM_PASSES[pair])
-            part_rows(0, pair, 2, on_vector)
+            part_passes(0, pair, 4, on_vector)
             for h in range(PASSES):
                 turn(0, h, pair)
         spread_balance()

@@ -30,13 +30,10 @@ QUADRANTS = (0, 2, 1, 3)
 HEAD_BANKS = 8
 ROUND_BANKS = (6, 6, 6)
 PIECE = 4
-PAIRS = (
-    [(g, n) for g in (0, 1) for n in range(4)]
-    + [(g, n) for g in (2, 3) for n in (0, 1)]
-    + [(g, n) for n in (2, 3) for g in (2, 3)]
-)
+PAIRS = [(g, n) for g in range(GROUPS) for n in range(TILES // 2)]
 POOL_FROM = 384
 EARLY = 4
+LATE = 2
 WARM_N = 512
 WARM_PASSES = (3, 2)
 
@@ -86,7 +83,8 @@ def tile_router_weight_gradient_s12_kernel(
         v_codes = [keep("v_codes%d" % h, [P, E], U32) for h in range(PASSES)]
         v_planes = [keep("v_plane%d" % h, [P, E], U8) for h in range(PASSES)]
         p_sb = [keep("p_sb%d" % g, [P, PACK, E], BF16) for g in range(GROUPS)]
-        shifted = [keep("shifted%d" % n, [P, E * PACK], F32) for n in range(2)]
+        shifted_room = [keep("shifted%d" % n, [P, HALF * n + E * PACK], F32) for n in range(2)]
+        shifted = [room[:, HALF * n :] for n, room in enumerate(shifted_room)]
         l_wide = [keep("l_wide%d" % g, [P, E * PACK], BF16) for g in range(2)] * 2
         l_codes = [keep("l_codes%d" % g, [P, E], U32) for g in range(GROUPS)]
         l_planes = [keep("l_plane%d" % g, [P, E], U8) for g in range(GROUPS)]
@@ -99,7 +97,7 @@ def tile_router_weight_gradient_s12_kernel(
         pool_row = x_wide[0].bitcast(F32)[:, 0 : 2 * P].rearrange("p (u w) -> p u w", u=2)
         l_upper = [
             x_room[2][:, 0 : 2 * BANK],
-            shifted[1][:, 3 * BANK // 2 : 5 * BANK // 2].bitcast(BF16),
+            shifted_room[1][:, 0:BANK].bitcast(BF16),
             x_room[4][:, 0 : 2 * BANK],
             l_wide[LAST][:, 2 * BANK :],
         ]
@@ -237,7 +235,7 @@ def tile_router_weight_gradient_s12_kernel(
             )
 
         def utilities(g):
-            dst = shifted[g % 2][:].rearrange("p (c t i) -> p c t i", t=PACK, i=4)
+            dst = shifted[g % 2].rearrange("p (c t i) -> p c t i", t=PACK, i=4)
             banks = [next_bank() for t in range(PACK)]
             steps = [(t, h) for t in range(PACK) for h in range(PASSES)]
             for t, h in sorted(steps, key=lambda step: step[1]) if g == 0 else steps:
@@ -266,7 +264,7 @@ def tile_router_weight_gradient_s12_kernel(
             dst = l_wide[g][:, PACK * lo : PACK * hi] if lo < HALF else l_upper[g][:, PACK * (lo - HALF) : PACK * (hi - HALF)]
             engine.tensor_tensor(
                 out=dst.rearrange("p (c i t) -> p c t i", i=4, t=PACK),
-                in0=shifted[g % 2][:].rearrange("p (c t i) -> p c t i", t=PACK, i=4)[:, cs],
+                in0=shifted[g % 2].rearrange("p (c t i) -> p c t i", t=PACK, i=4)[:, cs],
                 in1=p_sb[g][:].rearrange("p t (c i) -> p c t i", i=4)[:, cs],
                 op=ALU.mult,
             )
@@ -323,25 +321,24 @@ def tile_router_weight_gradient_s12_kernel(
                     stop=(n == count - 1),
                 )
 
+        nc.vector.memset(a_staged[0][:], 0)
         nc.vector.memset(w_plane[:].bitcast(I32), 0)
         nc.vector.memset(v_wide[0][:].bitcast(I32), 0)
-        nc.vector.memset(a_staged[0][:], 0)
         quantize(warm_codes[:], warm_plane[:], v_wide[0][:])
         nc.vector.memset(ident[:], 0.0)
         make_identity(nc, ident[:], nomemset=True)
 
         nc.vector.memset(a_staged[1][:], 0)
 
+        load_balance()
         load_grad(0, 0)
-        load_w_scales(QUADRANTS[:2])
         load_a_scales(0, QUADRANTS[:2])
+        load_w_scales(QUADRANTS[:2])
         load_grad(0, 1)
         load_a(0)
-        load_a_scales(0, QUADRANTS[2:3])
-        load_balance()
-        load_a_scales(0, QUADRANTS[3:])
-        load_w(0)
+        load_a_scales(0, QUADRANTS[2:])
         load_w_scales(QUADRANTS[2:])
+        load_w(0)
         load_values(0)
         load_w(1)
         load_values(1)
@@ -399,9 +396,9 @@ def tile_router_weight_gradient_s12_kernel(
                     turn(g + 1, h, pair)
             if g > 0:
                 quantize_l(g - 1)
-            weigh(g, 0, HALF, nc.vector)
-            quantize_grad(g + 1, 0, PASSES)
             weigh(g, HALF, POOL_FROM, nc.vector)
+            quantize_grad(g + 1, 0, PASSES)
+            weigh(g, 0, HALF, nc.vector)
             x_banks(ROUND_BANKS[g] - 1, on_scalar)
             if g + 2 < GROUPS:
                 part_on_scalar(g + 2)
@@ -414,18 +411,22 @@ def tile_router_weight_gradient_s12_kernel(
         x_banks(2 * len(PAIRS) - len(made), on_scalar)
         quantize_l(LAST - 1)
         weigh(LAST, 0, E, nc.vector)
-        quantize_x(5)
+        quantize_x(6)
         quantize_l(LAST)
-        for n in (1, 3, 6, 7):
+        for n in (1, 3, 5, 7):
             quantize_x(n)
         banks = [next_bank() for j in range(EARLY)]
         for j in range(EARLY):
             final_passes(banks[j], j, 0, E, range(LAST))
-        for j in range(TILES - 1):
-            if j >= EARLY:
-                banks.append(next_bank())
-            final_passes(banks[j], j, 0, E, [LAST] if j < EARLY else range(GROUPS))
-            store(banks[j], j, 0, E, on_vector if j == 5 else on_scalar)
+        for j in range(EARLY):
+            final_passes(banks[j], j, 0, E, [LAST])
+            store(banks[j], j, 0, E, on_scalar)
+        banks = [next_bank() for j in range(EARLY, TILES - 1)]
+        for j in range(LATE):
+            final_passes(banks[j], EARLY + j, 0, E, range(2))
+        for j in range(TILES - 1 - EARLY):
+            final_passes(banks[j], EARLY + j, 0, E, range(2 if j < LATE else 0, GROUPS))
+            store(banks[j], EARLY + j, 0, E, on_vector if j % 2 == 0 else on_scalar)
         for lo, hi, copy in ((0, HALF, on_vector), (HALF, HALF + P, on_scalar), (HALF + P, E, on_vector)):
             bank = next_bank()
             final_passes(bank, TILES - 1, lo, hi, range(GROUPS))

@@ -31,7 +31,9 @@ HEAD_BANKS = 8
 ROUND_BANKS = (6, 6, 6)
 PIECE = 4
 PAIRS = [(g, n) for g in range(GROUPS) for n in range(TILES // 2)]
-POOL_FROM = 384
+POOL_FROM = (384, 384, 352)
+SCALAR_STRETCHES = (0, 3, 3, 3)
+VECTOR_BANKS = (1, 1, 0)
 EARLY = 4
 LATE = 2
 WARM_N = 512
@@ -201,12 +203,14 @@ def tile_router_weight_gradient_s12_kernel(
         def parted(pair):
             return g_parted[pair][:].rearrange("p (u w) -> p u w", u=2)
 
-        def part_passes(g, pair, count, copy):
-            part(parted(pair)[:, :, 0 : P * count], grad_words(g, 2 * pair, 2 * pair + 2)[:, 0 : 2 * P * count], copy)
+        def part_passes(g, pair, lo, hi, copy):
+            src = grad_words(g, 2 * pair, 2 * pair + 2)[:, 2 * P * lo : 2 * P * hi]
+            part(parted(pair)[:, :, P * lo : P * hi], src, copy)
 
         def part_on_scalar(g):
-            part_passes(g, 0, 4, on_scalar)
-            part_passes(g, 1, 3 if g == 1 else 4, on_scalar)
+            part_passes(g, 0, 0, 4, on_scalar)
+            if SCALAR_STRETCHES[g] > 0:
+                part_passes(g, 1, 0, SCALAR_STRETCHES[g], on_scalar)
 
         def part_on_gpsimd():
             part(pool_row, grad_words(1, PACK - 1, PACK)[:, 2 * P :], on_gpsimd)
@@ -321,24 +325,25 @@ def tile_router_weight_gradient_s12_kernel(
                     stop=(n == count - 1),
                 )
 
-        nc.vector.memset(a_staged[0][:], 0)
         nc.vector.memset(w_plane[:].bitcast(I32), 0)
         nc.vector.memset(v_wide[0][:].bitcast(I32), 0)
+        nc.vector.memset(a_staged[0][:], 0)
         quantize(warm_codes[:], warm_plane[:], v_wide[0][:])
         nc.vector.memset(ident[:], 0.0)
         make_identity(nc, ident[:], nomemset=True)
 
         nc.vector.memset(a_staged[1][:], 0)
 
-        load_balance()
         load_grad(0, 0)
-        load_a_scales(0, QUADRANTS[:2])
         load_w_scales(QUADRANTS[:2])
+        load_a_scales(0, QUADRANTS[:2])
         load_grad(0, 1)
         load_a(0)
-        load_a_scales(0, QUADRANTS[2:])
-        load_w_scales(QUADRANTS[2:])
+        load_a_scales(0, QUADRANTS[2:3])
+        load_balance()
+        load_a_scales(0, QUADRANTS[3:])
         load_w(0)
+        load_w_scales(QUADRANTS[2:])
         load_values(0)
         load_w(1)
         load_values(1)
@@ -352,7 +357,7 @@ def tile_router_weight_gradient_s12_kernel(
 
         for pair in range(2):
             warm_up(WARM_PASSES[pair])
-            part_passes(0, pair, 4, on_vector)
+            part_passes(0, pair, 0, 4, on_vector)
             for h in range(PASSES):
                 turn(0, h, pair)
         spread_balance()
@@ -360,7 +365,6 @@ def tile_router_weight_gradient_s12_kernel(
         order_scales(0, on_vector)
         load_a(2)
         load_prob(0)
-        load_a_scales(1, QUADRANTS)
         x_banks(HEAD_BANKS, on_scalar)
         quantize_grad(0, 0, 1)
         interleave_values(0)
@@ -378,7 +382,7 @@ def tile_router_weight_gradient_s12_kernel(
             if g == 0:
                 part_on_gpsimd()
             else:
-                weigh(g - 1, POOL_FROM, E, nc.gpsimd)
+                weigh(g - 1, POOL_FROM[g - 1], E, nc.gpsimd)
             if g == 1:
                 order_scales(1, on_gpsimd)
             else:
@@ -386,6 +390,7 @@ def tile_router_weight_gradient_s12_kernel(
             if g == 0:
                 load_grad(2, 0)
                 load_grad(2, 1)
+                load_a_scales(1, QUADRANTS)
             load_prob(g + 1)
             if g == 0:
                 load_a(3)
@@ -396,18 +401,20 @@ def tile_router_weight_gradient_s12_kernel(
                     turn(g + 1, h, pair)
             if g > 0:
                 quantize_l(g - 1)
-            weigh(g, HALF, POOL_FROM, nc.vector)
+            weigh(g, HALF, POOL_FROM[g], nc.vector)
             quantize_grad(g + 1, 0, PASSES)
+            if g + 2 < GROUPS and SCALAR_STRETCHES[g + 2] < 4:
+                part_passes(g + 2, 1, SCALAR_STRETCHES[g + 2], 4, on_vector)
             weigh(g, 0, HALF, nc.vector)
             x_banks(ROUND_BANKS[g] - 1, on_scalar)
             if g + 2 < GROUPS:
                 part_on_scalar(g + 2)
             if g != 1:
                 quantize_x(2 + g)
-            x_banks(1, on_vector)
+            x_banks(1, on_vector if VECTOR_BANKS[g] else on_scalar)
 
         utilities(LAST)
-        weigh(LAST - 1, POOL_FROM, E, nc.gpsimd)
+        weigh(LAST - 1, POOL_FROM[LAST - 1], E, nc.gpsimd)
         x_banks(2 * len(PAIRS) - len(made), on_scalar)
         quantize_l(LAST - 1)
         weigh(LAST, 0, E, nc.vector)

@@ -307,10 +307,10 @@ def tile_router_weight_gradient_s12_kernel(
                     stop=(g == LAST),
                 )
 
-        def store(bank, j, lo, hi, copy):
+        def store(bank, j, lo, hi, copy, queue=nc.sync):
             staged = staged_out[j][:, lo:hi]
             copy(out=staged, in_=bank[:, 0 : hi - lo])
-            nc.sync.dma_start(out=out.rearrange("(j p) e -> p j e", p=P)[:, j, lo:hi], in_=staged)
+            queue.dma_start(out=out.rearrange("(j p) e -> p j e", p=P)[:, j, lo:hi], in_=staged)
 
         def warm_up(count):
             bank = next_bank()
@@ -433,8 +433,9 @@ def tile_router_weight_gradient_s12_kernel(
             final_passes(banks[j], EARLY + j, 0, E, range(2))
         for j in range(TILES - 1 - EARLY):
             final_passes(banks[j], EARLY + j, 0, E, range(2 if j < LATE else 0, GROUPS))
-            store(banks[j], EARLY + j, 0, E, on_vector if j % 2 == 0 else on_scalar)
-        for lo, hi, copy in ((0, HALF, on_vector), (HALF, HALF + P, on_scalar), (HALF + P, E, on_vector)):
+            store(banks[j], EARLY + j, 0, E, on_vector if j == 1 else on_scalar)
+        pieces = ((0, HALF, on_vector, nc.sync), (HALF, HALF + P, on_vector, nc.sync), (HALF + P, E, on_scalar, nc.scalar))
+        for lo, hi, copy, queue in pieces:
             bank = next_bank()
             final_passes(bank, TILES - 1, lo, hi, range(GROUPS))
-            store(bank, TILES - 1, lo, hi, copy)
+            store(bank, TILES - 1, lo, hi, copy, queue)

@@ -94,7 +94,7 @@ def tile_router_weight_gradient_s12_kernel(
         x_wide = [room[:, BANK:] for room in x_room]
         x_codes = [keep("x_codes%d" % n, [P, PIECE * P], U32) for n in range(len(PAIRS) // 2)]
         x_planes = [keep("x_plane%d" % n, [P, PIECE * P], U8) for n in range(len(PAIRS) // 2)]
-        staged_out = [keep("staged_out%d" % n, [P, E], F32) for n in range(TILES)]
+        staged_out = keep("staged_out", [P, TILES * E], F32)
 
         pool_row = x_wide[0].bitcast(F32)[:, 0 : 2 * P].rearrange("p (u w) -> p u w", u=2)
         l_upper = [
@@ -307,10 +307,12 @@ def tile_router_weight_gradient_s12_kernel(
                     stop=(g == LAST),
                 )
 
-        def store(bank, j, lo, hi, copy, queue=nc.sync):
-            staged = staged_out[j][:, lo:hi]
-            copy(out=staged, in_=bank[:, 0 : hi - lo])
-            queue.dma_start(out=out.rearrange("(j p) e -> p j e", p=P)[:, j, lo:hi], in_=staged)
+        def empty(bank, j, lo, hi, copy):
+            copy(out=staged_out[:, E * j + lo : E * j + hi], in_=bank[:, 0 : hi - lo])
+
+        def store(first, last, lo, hi, queue):
+            src = staged_out[:].rearrange("p (j e) -> p j e", e=E)[:, first : last + 1, lo:hi]
+            queue.dma_start(out=out.rearrange("(j p) e -> p j e", p=P)[:, first : last + 1, lo:hi], in_=src)
 
         def warm_up(count):
             bank = next_bank()
@@ -427,15 +429,19 @@ def tile_router_weight_gradient_s12_kernel(
             final_passes(banks[j], j, 0, E, range(LAST))
         for j in range(EARLY):
             final_passes(banks[j], j, 0, E, [LAST])
-            store(banks[j], j, 0, E, on_scalar)
+            empty(banks[j], j, 0, E, on_scalar)
+            if j % 2 == 1:
+                store(j - 1, j, 0, E, nc.sync)
         banks = [next_bank() for j in range(EARLY, TILES - 1)]
         for j in range(LATE):
             final_passes(banks[j], EARLY + j, 0, E, range(2))
         for j in range(TILES - 1 - EARLY):
             final_passes(banks[j], EARLY + j, 0, E, range(2 if j < LATE else 0, GROUPS))
-            store(banks[j], EARLY + j, 0, E, on_vector if j == 1 else on_scalar)
+            empty(banks[j], EARLY + j, 0, E, on_vector if j == 1 else on_scalar)
+            store(EARLY + j, EARLY + j, 0, E, nc.sync)
         pieces = ((0, HALF, on_vector, nc.sync), (HALF, HALF + P, on_vector, nc.sync), (HALF + P, E, on_scalar, nc.scalar))
         for lo, hi, copy, queue in pieces:
             bank = next_bank()
             final_passes(bank, TILES - 1, lo, hi, range(GROUPS))
-            store(bank, TILES - 1, lo, hi, copy, queue)
+            empty(bank, TILES - 1, lo, hi, copy)
+            store(TILES - 1, TILES - 1, lo, hi, queue)

@@ -25,20 +25,22 @@ BANK = 512
 BANKS = 8
 HALF = E // 2
 ALIGN = 64
+QUAD = 32
 TILES = D // P
 QUADRANTS = (0, 2, 1, 3)
-HEAD_BANKS = 8
-ROUND_BANKS = (6, 6, 6)
 PIECE = 4
-PAIRS = [(g, n) for g in range(GROUPS) for n in range(TILES // 2)]
-POOL_FROM = (384, 384, 352)
-SCALAR_STRETCHES = (0, 3, 3, 3)
-VECTOR_BANKS = (1, 1, 0)
-EARLY = 4
-LATE = 2
 WARM_N = 512
-WARM_PASSES = (3, 2)
-
+WARM = 4
+OUT_ON_VECTOR = (5,)
+GATE = (1, 2, 4)
+QX = ((), (), (), (6,), (3, 5, 7))
+POOL_STRETCH = (1, 1, 3)
+POOL_FROM = (352, 352, 352)
+VB = (0, 0, 0)
+SS = (2, 1, 1)
+H0, H1 = 8, 3
+R = (5, 5, 5)
+AHEAD = 3
 
 def tile_router_weight_gradient_s12_kernel(
     tc, a_words, a_scales, w_words, w_scales, grad, values, prob, balance, base, out
@@ -69,12 +71,13 @@ def tile_router_weight_gradient_s12_kernel(
 
         a_raw = [keep("a_raw%d" % g, [P, PASSES, 256], I32) for g in range(2)] * 2
         a_codes = [keep("a_codes%d" % g, [P, PACK, PASSES, 2 * P], U8) for g in range(GROUPS)]
-        a_staged = [keep("a_staged%d" % n, [P, PASSES, 256], I32) for n in range(2)]
-        a_planes = [keep("a_plane%d" % n, [P, PACK, PASSES, 2, P], U8) for n in range(2)]
+        spans = ((0, 2), (2, GROUPS))
+        a_staged = [keep("a_staged%d" % lo, [P, PASSES, P * (hi - lo)], I32) for lo, hi in spans]
+        a_planes = [keep("a_plane%d" % lo, [P, PACK, PASSES, hi - lo, P], U8) for lo, hi in spans]
         w_codes = [keep("w_codes%d" % n, [P, PASSES, D], U8) for n in range(2)]
         w_plane = keep("w_plane", [P, PASSES, D], U8)
 
-        g_raw = [keep("g_raw%d" % g, [P, PACK, D], BF16) for g in range(LAST)]
+        g_raw = [keep("g_raw%d" % g, [P, PACK * D], BF16) for g in range(LAST)]
         g_raw = g_raw[:2] + [g_raw[0], g_raw[2]]
         g_parted = [keep("g_parted%d" % n, [P, PASSES * 4 * P], F32) for n in range(2)]
         g_wide = [keep("g_wide%d" % g, [P, PASSES * GROUP * PACK], BF16) for g in range(2)] * 2
@@ -85,24 +88,18 @@ def tile_router_weight_gradient_s12_kernel(
         v_codes = [keep("v_codes%d" % h, [P, E], U32) for h in range(PASSES)]
         v_planes = [keep("v_plane%d" % h, [P, E], U8) for h in range(PASSES)]
         p_sb = [keep("p_sb%d" % g, [P, PACK, E], BF16) for g in range(GROUPS)]
-        shifted_room = [keep("shifted%d" % n, [P, HALF * n + E * PACK], F32) for n in range(2)]
-        shifted = [room[:, HALF * n :] for n, room in enumerate(shifted_room)]
-        l_wide = [keep("l_wide%d" % g, [P, E * PACK], BF16) for g in range(2)] * 2
+        shifted = [keep("shifted%d" % n, [P, E * PACK], F32) for n in range(2)] * 2
         l_codes = [keep("l_codes%d" % g, [P, E], U32) for g in range(GROUPS)]
         l_planes = [keep("l_plane%d" % g, [P, E], U8) for g in range(GROUPS)]
-        x_room = [keep("x_wide%d" % n, [P, (PIECE + 1) * BANK], BF16) for n in range(len(PAIRS) // 2)]
-        x_wide = [room[:, BANK:] for room in x_room]
-        x_codes = [keep("x_codes%d" % n, [P, PIECE * P], U32) for n in range(len(PAIRS) // 2)]
-        x_planes = [keep("x_plane%d" % n, [P, PIECE * P], U8) for n in range(len(PAIRS) // 2)]
+        x_wide = [keep("x_wide%d" % n, [P, PIECE * BANK], BF16) for n in range(2 * GROUPS)]
+        x_codes = [keep("x_codes%d" % n, [P, PIECE * P], U32) for n in range(2 * GROUPS)]
+        x_planes = [keep("x_plane%d" % n, [P, PIECE * P], U8) for n in range(2 * GROUPS)]
         staged_out = keep("staged_out", [P, TILES * E], F32)
+        l_low = [keep("l_low%d" % n, [P, E * PACK], BF16) for n in range(1)]
+        l_lower = [l_low[0][:, 0 : 2 * BANK], l_low[0][:, 2 * BANK :], l_low[0][:, 0 : 2 * BANK], g_wide[0][:, 0 : PACK * BANK]]
+        l_upper = [x_wide[n][:, 0 : 2 * BANK] for n in GATE] + [g_wide[0][:, 2 * BANK : PACK * BANK]]
+        pool_stretch = g_raw[1][:].bitcast(F32)[:, D : D + 2 * P].rearrange("p (u w) -> p u w", u=2)
 
-        pool_row = x_wide[0].bitcast(F32)[:, 0 : 2 * P].rearrange("p (u w) -> p u w", u=2)
-        l_upper = [
-            x_room[2][:, 0 : 2 * BANK],
-            shifted_room[1][:, 0:BANK].bitcast(BF16),
-            x_room[4][:, 0 : 2 * BANK],
-            l_wide[LAST][:, 2 * BANK :],
-        ]
 
         def load_a(g):
             src = a_words.rearrange("h p n -> p h n")[:, :, 2 * GROUP * g : 2 * GROUP * (g + 1)]
@@ -111,10 +108,10 @@ def tile_router_weight_gradient_s12_kernel(
         def load_scale_rows(dst, scales, lo, hi, quadrants):
             for q in quadrants:
                 src = scales.rearrange("h r n -> r h n")[4 * q : 4 * q + 4, :, lo:hi]
-                nc.sync.dma_start(out=dst[32 * q : 32 * q + 4], in_=src.bitcast(I32))
+                nc.sync.dma_start(out=dst[QUAD * q : QUAD * q + 4], in_=src.bitcast(I32))
 
         def load_a_scales(n, quadrants):
-            load_scale_rows(a_staged[n], a_scales, 2 * GROUP * n, 2 * GROUP * (n + 1), quadrants)
+            load_scale_rows(a_staged[n], a_scales, GROUP * spans[n][0], GROUP * spans[n][1], quadrants)
 
         def load_w_scales(quadrants):
             load_scale_rows(w_plane[:].bitcast(I32), w_scales, 0, D, quadrants)
@@ -124,16 +121,17 @@ def tile_router_weight_gradient_s12_kernel(
             nc.sync.dma_start(out=w_codes[n][:].bitcast(I32), in_=src.bitcast(I32))
 
         def load_grad(g, pair):
-            rows = grad[GROUP * g : GROUP * (g + 1), :].rearrange("(m s) d -> m s d", s=PACK)
-            nc.sync.dma_start(out=g_raw[g][:, 2 * pair : 2 * pair + 2, :], in_=rows[:, 2 * pair : 2 * pair + 2, :])
+            rows = grad[GROUP * g : GROUP * (g + 1), :].rearrange("(m s) d -> m (s d)", s=PACK)
+            cols = slice(2 * D * pair, 2 * D * (pair + 1))
+            nc.sync.dma_start(out=g_raw[g][:, cols], in_=rows[:, cols])
 
         def load_values(h):
             rows = values[GROUP * h : GROUP * (h + 1), :].rearrange("(p t) e -> p t e", t=PACK)
             nc.sync.dma_start(out=v_raw[h][:], in_=rows)
 
-        def load_prob(g):
+        def load_prob(g, rows_s=range(PACK)):
             rows = prob[GROUP * g : GROUP * (g + 1), :].rearrange("(c t s) e -> s c t e", t=PACK, s=PACK)
-            for s in range(PACK):
+            for s in rows_s:
                 nc.sync.dma_start(out=p_sb[g][s:P:PACK, :, :], in_=rows[s])
 
         def load_base(s):
@@ -149,10 +147,10 @@ def tile_router_weight_gradient_s12_kernel(
                 in_=a_raw[g][:].rearrange("p h (b i t w) -> p (h b) t i w", i=2, t=PACK, w=2),
             )
 
-        def order_scales(n, copy):
+        def order_scales(n, copy, word):
             copy(
-                out=a_planes[n][:].bitcast(I32).rearrange("p t h g (b i) -> p (h g b) t i", i=4),
-                in_=a_staged[n][:].rearrange("p h (x i t) -> p (h x) t i", i=4, t=PACK),
+                out=a_planes[n][:].bitcast(word).rearrange("p t h g (b i) -> p (h g b) t i", i=4),
+                in_=a_staged[n][:].bitcast(word).rearrange("p h (x i t) -> p (h x) t i", i=4, t=PACK),
             )
 
         def quantize(dst, plane, src):
@@ -168,69 +166,61 @@ def tile_router_weight_gradient_s12_kernel(
                 in_=bank[:, 0 : 2 * P].rearrange("p (u n) -> p n u", u=2),
             )
 
-        def x_passes(dst, g, t, j, width):
-            n, jj = divmod(j, TILES // 2)
-            for h in range(PASSES):
-                nc.tensor.matmul_mx(
-                    out=dst,
-                    lhsT=a_codes[g][:, t, h, :].bitcast(FP4X4),
-                    lhsT_scale=a_planes[g // 2][:, t, h, g % 2, :],
-                    rhs=w_codes[n][:, h, 2 * P * jj : 2 * (P * jj + width)].bitcast(FP4X4),
-                    rhs_scale=w_plane[:, h, P * j : P * j + width],
-                    start=(h == 0),
-                    stop=(h == PASSES - 1),
-                )
-
         made = []
 
-        def x_banks(count, copy):
+        def x_tiles(count, copy):
             for b in range(len(made), len(made) + count):
                 made.append(b)
-                k, u = divmod(b, 2)
-                g, n = PAIRS[k]
-                words = x_wide[k // 2][:, 2 * BANK * (k % 2) : 2 * BANK * (k % 2 + 1)].rearrange("p (d t) -> p d t", t=PACK)
+                g, j = divmod(b, TILES)
+                n, jj = divmod(j, PIECE)
+                plane = a_planes[g // 2][:, :, :, g % 2, :]
                 bank = next_bank()
                 for t in range(PACK):
-                    x_passes(bank[:, P * t : P * (t + 1)], g, t, 2 * n + u, P)
-                copy(out=words[:, P * u : P * (u + 1)], in_=bank[:].rearrange("p (t d) -> p d t", t=PACK))
+                    for h in range(PASSES):
+                        nc.tensor.matmul_mx(
+                            out=bank[:, P * t : P * (t + 1)],
+                            lhsT=a_codes[g][:, t, h, :].bitcast(FP4X4),
+                            lhsT_scale=plane[:, t, h, :],
+                            rhs=w_codes[n][:, h, 2 * P * jj : 2 * P * (jj + 1)].bitcast(FP4X4),
+                            rhs_scale=w_plane[:, h, P * j : P * (j + 1)],
+                            start=(h == 0),
+                            stop=(h == PASSES - 1),
+                        )
+                words = x_wide[2 * g + n][:, BANK * jj : BANK * (jj + 1)].rearrange("p (d t) -> p d t", t=PACK)
+                copy(out=words, in_=bank[:].rearrange("p (t d) -> p d t", t=PACK))
 
         def part(dst, src, copy):
             copy(out=dst.rearrange("p u (x i) -> p x u i", i=4), in_=src.rearrange("p (x i u) -> p x u i", i=4, u=2))
 
-        def grad_words(g, lo, hi):
-            return g_raw[g][:, lo:hi].rearrange("p s d -> p (s d)").bitcast(F32)
+        def part_pair(g, pair, lo, hi, copy):
+            if lo == hi:
+                return
+            src = g_raw[g][:].bitcast(F32)[:, D * pair + 2 * P * lo : D * pair + 2 * P * hi]
+            part(g_parted[pair][:].rearrange("p (u w) -> p u w", u=2)[:, :, P * lo : P * hi], src, copy)
 
-        def parted(pair):
-            return g_parted[pair][:].rearrange("p (u w) -> p u w", u=2)
-
-        def part_passes(g, pair, lo, hi, copy):
-            src = grad_words(g, 2 * pair, 2 * pair + 2)[:, 2 * P * lo : 2 * P * hi]
-            part(parted(pair)[:, :, P * lo : P * hi], src, copy)
-
-        def part_on_scalar(g):
-            part_passes(g, 0, 0, 4, on_scalar)
-            if SCALAR_STRETCHES[g] > 0:
-                part_passes(g, 1, 0, SCALAR_STRETCHES[g], on_scalar)
+        def parted_stretch(g, pair, n):
+            if (g, pair, n) == POOL_STRETCH:
+                return pool_stretch
+            return g_parted[pair][:].rearrange("p (u w) -> p u w", u=2)[:, :, P * n : P * (n + 1)]
 
         def part_on_gpsimd():
-            part(pool_row, grad_words(1, PACK - 1, PACK)[:, 2 * P :], on_gpsimd)
+            g, pair, n = POOL_STRETCH
+            first = D * pair + 2 * P * n
+            part(pool_stretch, g_raw[g][:].bitcast(F32)[:, first : first + 2 * P], on_gpsimd)
 
-        def words_to_turn(g, h, s, u):
-            if (g, h, s) == (1, PASSES - 1, PACK - 1):
-                return pool_row[:, u]
-            first = P * (PASSES * (s % 2) + h)
-            return parted(s // 2)[:, u, first : first + P]
-
-        def turn(g, h, pair):
-            bank = next_bank()
-            for q in range(4):
-                words = words_to_turn(g, h, 2 * pair + q // 2, q % 2)
-                nc.tensor.transpose(bank[:, P * q : P * (q + 1)], words, ident[:])
+        def turn_group(g, steps):
+            banks = {}
+            for h, pair in steps:
+                banks[h, pair] = next_bank()
+                for q in range(4):
+                    couples = parted_stretch(g, pair, PASSES * (q // 2) + h)[:, q % 2]
+                    nc.tensor.transpose(banks[h, pair][:, P * q : P * (q + 1)], couples, ident[:])
             dst = g_wide[g][:].bitcast(F32).rearrange("p (h t c w) -> p h t c w", h=PASSES, t=PACK, w=8)
-            nc.scalar.copy(
-                out=dst[:, h, :, :, 4 * pair : 4 * pair + 4],
-                in_=bank[:].rearrange("p (q c t) -> p t c q", q=4, t=PACK),
-            )
+            for h, pair in sorted(steps):
+                nc.scalar.copy(
+                    out=dst[:, h, :, :, 4 * pair : 4 * pair + 4],
+                    in_=banks[h, pair][:].rearrange("p (q c t) -> p t c q", q=4, t=PACK),
+                )
 
         def interleave_values(h):
             nc.vector.tensor_copy(
@@ -239,10 +229,10 @@ def tile_router_weight_gradient_s12_kernel(
             )
 
         def utilities(g):
-            dst = shifted[g % 2].rearrange("p (c t i) -> p c t i", t=PACK, i=4)
+            dst = shifted[g][:].rearrange("p (c t i) -> p c t i", t=PACK, i=4)
             banks = [next_bank() for t in range(PACK)]
             steps = [(t, h) for t in range(PACK) for h in range(PASSES)]
-            for t, h in sorted(steps, key=lambda step: step[1]) if g == 0 else steps:
+            for t, h in sorted(steps, key=lambda step: (step[0] // (PACK if g == 0 else 2), step[1])):
                 tokens = slice(GROUP * h + P * t, GROUP * h + P * (t + 1))
                 nc.tensor.matmul_mx(
                     out=banks[t][:],
@@ -265,10 +255,10 @@ def tile_router_weight_gradient_s12_kernel(
 
         def weigh(g, lo, hi, engine):
             cs = slice(lo // 4, hi // 4)
-            dst = l_wide[g][:, PACK * lo : PACK * hi] if lo < HALF else l_upper[g][:, PACK * (lo - HALF) : PACK * (hi - HALF)]
+            dst = l_lower[g][:, PACK * lo : PACK * hi] if lo < HALF else l_upper[g][:, PACK * (lo - HALF) : PACK * (hi - HALF)]
             engine.tensor_tensor(
                 out=dst.rearrange("p (c i t) -> p c t i", i=4, t=PACK),
-                in0=shifted[g % 2].rearrange("p (c t i) -> p c t i", t=PACK, i=4)[:, cs],
+                in0=shifted[g][:].rearrange("p (c t i) -> p c t i", t=PACK, i=4)[:, cs],
                 in1=p_sb[g][:].rearrange("p t (c i) -> p c t i", i=4)[:, cs],
                 op=ALU.mult,
             )
@@ -283,24 +273,20 @@ def tile_router_weight_gradient_s12_kernel(
                 g_wide[g][:, GROUP * PACK * lo : GROUP * PACK * hi],
             )
 
-        def quantize_l(g):
-            if g == LAST:
-                quantize(l_codes[g][:], l_planes[g][:], l_wide[g][:])
-            else:
-                quantize(l_codes[g][:, 0:HALF], l_planes[g][:, 0:HALF], l_wide[g][:, 0 : 2 * BANK])
-                quantize(l_codes[g][:, HALF:], l_planes[g][:, HALF:], l_upper[g])
+        def quantize_l(g, lo, hi, src):
+            quantize(l_codes[g][:, lo:hi], l_planes[g][:, lo:hi], src)
 
         def quantize_x(n):
-            quantize(x_codes[n][:], x_planes[n][:], x_wide[n])
+            quantize(x_codes[n][:], x_planes[n][:], x_wide[n][:])
 
         def final_passes(bank, j, lo, hi, groups):
             for g in groups:
-                n, k = divmod(PAIRS.index((g, j // 2)), 2)
-                cols = slice(P * (2 * k + j % 2), P * (2 * k + j % 2 + 1))
+                n, jj = divmod(j, PIECE)
+                cols = slice(P * jj, P * (jj + 1))
                 nc.tensor.matmul_mx(
                     out=bank[:, 0 : hi - lo],
-                    lhsT=x_codes[n][:, cols].bitcast(FP8X4),
-                    lhsT_scale=x_planes[n][:, cols],
+                    lhsT=x_codes[2 * g + n][:, cols].bitcast(FP8X4),
+                    lhsT_scale=x_planes[2 * g + n][:, cols],
                     rhs=l_codes[g][:, lo:hi].bitcast(FP8X4),
                     rhs_scale=l_planes[g][:, lo:hi],
                     start=(g == 0),
@@ -327,121 +313,118 @@ def tile_router_weight_gradient_s12_kernel(
                     stop=(n == count - 1),
                 )
 
-        nc.vector.memset(w_plane[:].bitcast(I32), 0)
-        nc.vector.memset(v_wide[0][:].bitcast(I32), 0)
+        def finals():
+            banks = [next_bank() for j in range(PIECE)]
+            for g in range(AHEAD):
+                for j in range(PIECE):
+                    final_passes(banks[j], j, 0, E, [g])
+            for j in range(TILES - 1):
+                if j >= PIECE:
+                    banks.append(next_bank())
+                final_passes(banks[j], j, 0, E, range(AHEAD if j < PIECE else 0, GROUPS))
+                empty(banks[j], j, 0, E, on_vector if j in OUT_ON_VECTOR else on_scalar)
+                if j >= PIECE or j % 2 == 1:
+                    store(j if j >= PIECE else j - 1, j, 0, E, nc.sync)
+            pieces = ((0, HALF, on_vector, nc.sync), (HALF, HALF + P, on_vector, nc.sync), (HALF + P, E, on_scalar, nc.scalar))
+            for lo, hi, copy, queue in pieces:
+                bank = next_bank()
+                final_passes(bank, TILES - 1, lo, hi, range(GROUPS))
+                empty(bank, TILES - 1, lo, hi, copy)
+                store(TILES - 1, TILES - 1, lo, hi, queue)
+
+        by_pair = [(h, pair) for pair in range(2) for h in range(PASSES)]
         nc.vector.memset(a_staged[0][:], 0)
-        quantize(warm_codes[:], warm_plane[:], v_wide[0][:])
+        nc.vector.memset(w_plane[:].bitcast(I32), 0)
+        nc.vector.memset(v_wide[1][:].bitcast(I32), 0)
         nc.vector.memset(ident[:], 0.0)
+        quantize(warm_codes[:], warm_plane[:], v_wide[1][:])
         make_identity(nc, ident[:], nomemset=True)
-
-        nc.vector.memset(a_staged[1][:], 0)
-
-        load_grad(0, 0)
-        load_w_scales(QUADRANTS[:2])
-        load_a_scales(0, QUADRANTS[:2])
-        load_grad(0, 1)
         load_a(0)
-        load_a_scales(0, QUADRANTS[2:3])
-        load_balance()
-        load_a_scales(0, QUADRANTS[3:])
+        load_a_scales(0, QUADRANTS[:2])
         load_w(0)
-        load_w_scales(QUADRANTS[2:])
+        load_a_scales(0, QUADRANTS[2:])
+        load_w_scales(QUADRANTS)
         load_values(0)
         load_w(1)
-        load_values(1)
-        load_base(0)
+        load_balance()
+        load_grad(0, 0)
+        load_grad(0, 1)
         load_a(1)
+        load_base(0)
+        load_values(1)
         load_base(1)
         load_grad(1, 0)
         load_base(2)
         load_base(3)
         load_grad(1, 1)
-
-        for pair in range(2):
-            warm_up(WARM_PASSES[pair])
-            part_passes(0, pair, 0, 4, on_vector)
-            for h in range(PASSES):
-                turn(0, h, pair)
-        spread_balance()
+        warm_up(WARM)
         order_codes(0, on_vector)
-        order_scales(0, on_vector)
+        order_scales(0, on_vector, I32)
+        nc.vector.memset(a_staged[1][:], 0)
         load_a(2)
+        load_a_scales(1, QUADRANTS)
         load_prob(0)
-        x_banks(HEAD_BANKS, on_scalar)
-        quantize_grad(0, 0, 1)
+        x_tiles(H0, on_scalar)
         interleave_values(0)
-        quantize_grad(0, 1, 2)
         quantize_values(0)
-        interleave_values(1)
-        quantize_values(1)
+        part_pair(0, 0, 0, 4, on_vector)
+        part_pair(0, 1, 0, 4, on_vector)
+        turn_group(0, by_pair)
+        spread_balance()
         order_codes(1, on_vector)
+        load_a(3)
         quantize_x(0)
-
-        for g in range(LAST):
+        interleave_values(1)
+        x_tiles(H1, on_scalar)
+        quantize_grad(0, 0, 1)
+        quantize_values(1)
+        quantize_grad(0, 1, 2)
+        part_pair(1, 0, 0, 4, on_vector)
+        part_pair(1, 1, 0, 1, on_vector)
+        part_pair(1, 1, 1, 3, on_scalar)
+        part_on_gpsimd()
+        order_codes(2, on_gpsimd)
+        order_scales(1, on_scalar, U32)
+        for g in range(GROUPS):
             utilities(g)
-            if g == 0:
-                part_on_scalar(1)
-            if g == 0:
-                part_on_gpsimd()
-            else:
-                weigh(g - 1, POOL_FROM[g - 1], E, nc.gpsimd)
-            if g == 1:
-                order_scales(1, on_gpsimd)
-            else:
-                order_codes(2 + g // 2, on_gpsimd)
             if g == 0:
                 load_grad(2, 0)
                 load_grad(2, 1)
-                load_a_scales(1, QUADRANTS)
-            load_prob(g + 1)
-            if g == 0:
-                load_a(3)
+                load_prob(1)
                 load_grad(3, 0)
                 load_grad(3, 1)
-            for pair in range(2):
-                for h in range(PASSES):
-                    turn(g + 1, h, pair)
+                load_prob(2)
+                load_prob(3)
+            else:
+                weigh(g - 1, POOL_FROM[g - 1], E, nc.gpsimd)
             if g > 0:
-                quantize_l(g - 1)
-            weigh(g, HALF, POOL_FROM[g], nc.vector)
-            quantize_grad(g + 1, 0, PASSES)
-            if g + 2 < GROUPS and SCALAR_STRETCHES[g + 2] < 4:
-                part_passes(g + 2, 1, SCALAR_STRETCHES[g + 2], 4, on_vector)
-            weigh(g, 0, HALF, nc.vector)
-            x_banks(ROUND_BANKS[g] - 1, on_scalar)
+                weigh(g - 1, HALF, POOL_FROM[g - 1], nc.vector)
+                quantize_l(g - 1, 0, HALF, l_lower[g - 1])
+                quantize_l(g - 1, HALF, E, l_upper[g - 1])
+            if g == LAST:
+                break
+            turn_group(g + 1, by_pair)
+            if g == 0:
+                order_codes(LAST, on_vector)
+                weigh(g, 0, P, nc.vector)
+            quantize_grad(g + 1, 0, 1)
+            weigh(g, P if g == 0 else 0, HALF if g == 0 else P, nc.vector)
+            quantize_grad(g + 1, 1, 2)
+            if g > 0:
+                weigh(g, P, HALF, nc.vector)
+            x_tiles(R[g] - 1, on_scalar)
             if g + 2 < GROUPS:
-                part_on_scalar(g + 2)
-            if g != 1:
-                quantize_x(2 + g)
-            x_banks(1, on_vector if VECTOR_BANKS[g] else on_scalar)
-
-        utilities(LAST)
-        weigh(LAST - 1, POOL_FROM[LAST - 1], E, nc.gpsimd)
-        x_banks(2 * len(PAIRS) - len(made), on_scalar)
-        quantize_l(LAST - 1)
+                part_pair(g + 2, 0, 0, 4, on_scalar)
+                part_pair(g + 2, 1, SS[g + 1], 4, on_vector)
+            quantize_x(GATE[g])
+            if g + 2 < GROUPS:
+                part_pair(g + 2, 1, 0, SS[g + 1], on_scalar)
+            x_tiles(1, on_vector if VB[g] else on_scalar)
+        x_tiles(GROUPS * TILES - len(made), on_scalar)
         weigh(LAST, 0, E, nc.vector)
-        quantize_x(6)
-        quantize_l(LAST)
-        for n in (1, 3, 5, 7):
+        for n in QX[LAST]:
             quantize_x(n)
-        banks = [next_bank() for j in range(EARLY)]
-        for j in range(EARLY):
-            final_passes(banks[j], j, 0, E, range(LAST))
-        for j in range(EARLY):
-            final_passes(banks[j], j, 0, E, [LAST])
-            empty(banks[j], j, 0, E, on_scalar)
-            if j % 2 == 1:
-                store(j - 1, j, 0, E, nc.sync)
-        banks = [next_bank() for j in range(EARLY, TILES - 1)]
-        for j in range(LATE):
-            final_passes(banks[j], EARLY + j, 0, E, range(2))
-        for j in range(TILES - 1 - EARLY):
-            final_passes(banks[j], EARLY + j, 0, E, range(2 if j < LATE else 0, GROUPS))
-            empty(banks[j], EARLY + j, 0, E, on_vector if j == 1 else on_scalar)
-            store(EARLY + j, EARLY + j, 0, E, nc.sync)
-        pieces = ((0, HALF, on_vector, nc.sync), (HALF, HALF + P, on_vector, nc.sync), (HALF + P, E, on_scalar, nc.scalar))
-        for lo, hi, copy, queue in pieces:
-            bank = next_bank()
-            final_passes(bank, TILES - 1, lo, hi, range(GROUPS))
-            empty(bank, TILES - 1, lo, hi, copy)
-            store(TILES - 1, TILES - 1, lo, hi, queue)
+        quantize_l(LAST, 0, E, l_lower[LAST])
+        for n in QX[GROUPS]:
+            quantize_x(n)
+        finals()

@@ -30,17 +30,19 @@ TILES = D // P
 QUADRANTS = (0, 2, 1, 3)
 PIECE = 4
 WARM_N = 512
-WARM = 4
+WARM = 3
 OUT_ON_VECTOR = (5,)
-GATE = (1, 2, 4)
-QX = ((), (), (), (6,), (3, 5, 7))
 POOL_STRETCH = (1, 1, 3)
-POOL_FROM = (352, 352, 352)
+PIECES = (0, 1, 2, 4, 6, 3, 5, 7)
+GATE = (2, 4, 6)
 VB = (0, 0, 0)
-SS = (2, 1, 1)
 H0, H1 = 8, 3
+POOL_WALK = "p c i t"
+SS = (2, 1, 1)
+POOL_FROM = (288, 288, 288)
 R = (5, 5, 5)
-AHEAD = 3
+AHEAD = (3, 2)
+OPEN = (4, 2)
 
 def tile_router_weight_gradient_s12_kernel(
     tc, a_words, a_scales, w_words, w_scales, grad, values, prob, balance, base, out
@@ -79,7 +81,8 @@ def tile_router_weight_gradient_s12_kernel(
 
         g_raw = [keep("g_raw%d" % g, [P, PACK * D], BF16) for g in range(LAST)]
         g_raw = g_raw[:2] + [g_raw[0], g_raw[2]]
-        g_parted = [keep("g_parted%d" % n, [P, PASSES * 4 * P], F32) for n in range(2)]
+        g_parted = [keep("g_parted%d" % n, [P, PASSES * 4 * P], F32) for n in range(3)]
+        g_parted = [[g_parted[0], g_parted[1 + g % 2]] for g in range(GROUPS)]
         g_wide = [keep("g_wide%d" % g, [P, PASSES * GROUP * PACK], BF16) for g in range(2)] * 2
         g_codes = [keep("g_codes%d" % g, [P, PASSES * GROUP], U32) for g in range(2)] * 2
         g_planes = [keep("g_plane%d" % g, [P, PASSES * GROUP], U8) for g in range(2)] * 2
@@ -91,13 +94,13 @@ def tile_router_weight_gradient_s12_kernel(
         shifted = [keep("shifted%d" % n, [P, E * PACK], F32) for n in range(2)] * 2
         l_codes = [keep("l_codes%d" % g, [P, E], U32) for g in range(GROUPS)]
         l_planes = [keep("l_plane%d" % g, [P, E], U8) for g in range(GROUPS)]
-        x_wide = [keep("x_wide%d" % n, [P, PIECE * BANK], BF16) for n in range(2 * GROUPS)]
+        front = {n: PACK * POOL_FROM[g] for g, n in enumerate(GATE)}
+        x_room = [keep("x_wide%d" % n, [P, front.get(n, 0) + PIECE * BANK], BF16) for n in range(2 * GROUPS)]
+        x_wide = [room[:, front.get(n, 0) :] for n, room in enumerate(x_room)]
         x_codes = [keep("x_codes%d" % n, [P, PIECE * P], U32) for n in range(2 * GROUPS)]
         x_planes = [keep("x_plane%d" % n, [P, PIECE * P], U8) for n in range(2 * GROUPS)]
         staged_out = keep("staged_out", [P, TILES * E], F32)
-        l_low = [keep("l_low%d" % n, [P, E * PACK], BF16) for n in range(1)]
-        l_lower = [l_low[0][:, 0 : 2 * BANK], l_low[0][:, 2 * BANK :], l_low[0][:, 0 : 2 * BANK], g_wide[0][:, 0 : PACK * BANK]]
-        l_upper = [x_wide[n][:, 0 : 2 * BANK] for n in GATE] + [g_wide[0][:, 2 * BANK : PACK * BANK]]
+        l_wide = [x_room[n][:, 0 : PACK * E] for n in GATE] + [g_wide[0][:, 0 : PACK * E]]
         pool_stretch = g_raw[1][:].bitcast(F32)[:, D : D + 2 * P].rearrange("p (u w) -> p u w", u=2)
 
 
@@ -171,8 +174,9 @@ def tile_router_weight_gradient_s12_kernel(
         def x_tiles(count, copy):
             for b in range(len(made), len(made) + count):
                 made.append(b)
-                g, j = divmod(b, TILES)
-                n, jj = divmod(j, PIECE)
+                g, n = divmod(PIECES[b // PIECE], 2)
+                jj = b % PIECE
+                j = PIECE * n + jj
                 plane = a_planes[g // 2][:, :, :, g % 2, :]
                 bank = next_bank()
                 for t in range(PACK):
@@ -196,12 +200,12 @@ def tile_router_weight_gradient_s12_kernel(
             if lo == hi:
                 return
             src = g_raw[g][:].bitcast(F32)[:, D * pair + 2 * P * lo : D * pair + 2 * P * hi]
-            part(g_parted[pair][:].rearrange("p (u w) -> p u w", u=2)[:, :, P * lo : P * hi], src, copy)
+            part(g_parted[g][pair][:].rearrange("p (u w) -> p u w", u=2)[:, :, P * lo : P * hi], src, copy)
 
         def parted_stretch(g, pair, n):
             if (g, pair, n) == POOL_STRETCH:
                 return pool_stretch
-            return g_parted[pair][:].rearrange("p (u w) -> p u w", u=2)[:, :, P * n : P * (n + 1)]
+            return g_parted[g][pair][:].rearrange("p (u w) -> p u w", u=2)[:, :, P * n : P * (n + 1)]
 
         def part_on_gpsimd():
             g, pair, n = POOL_STRETCH
@@ -254,12 +258,11 @@ def tile_router_weight_gradient_s12_kernel(
                 )
 
         def weigh(g, lo, hi, engine):
-            cs = slice(lo // 4, hi // 4)
-            dst = l_lower[g][:, PACK * lo : PACK * hi] if lo < HALF else l_upper[g][:, PACK * (lo - HALF) : PACK * (hi - HALF)]
+            walk = "p c t i" if engine is nc.vector else POOL_WALK
             engine.tensor_tensor(
-                out=dst.rearrange("p (c i t) -> p c t i", i=4, t=PACK),
-                in0=shifted[g][:].rearrange("p (c t i) -> p c t i", t=PACK, i=4)[:, cs],
-                in1=p_sb[g][:].rearrange("p t (c i) -> p c t i", i=4)[:, cs],
+                out=l_wide[g][:, PACK * lo : PACK * hi].rearrange("p (c i t) -> " + walk, i=4, t=PACK),
+                in0=shifted[g][:, PACK * lo : PACK * hi].rearrange("p (c t i) -> " + walk, t=PACK, i=4),
+                in1=p_sb[g][:, :, lo:hi].rearrange("p t (c i) -> " + walk, i=4),
                 op=ALU.mult,
             )
 
@@ -273,11 +276,11 @@ def tile_router_weight_gradient_s12_kernel(
                 g_wide[g][:, GROUP * PACK * lo : GROUP * PACK * hi],
             )
 
-        def quantize_l(g, lo, hi, src):
-            quantize(l_codes[g][:, lo:hi], l_planes[g][:, lo:hi], src)
+        def quantize_l(g):
+            quantize(l_codes[g][:], l_planes[g][:], l_wide[g])
 
         def quantize_x(n):
-            quantize(x_codes[n][:], x_planes[n][:], x_wide[n][:])
+            quantize(x_codes[n][:], x_planes[n][:], x_wide[n])
 
         def final_passes(bank, j, lo, hi, groups):
             for g in groups:
@@ -314,14 +317,17 @@ def tile_router_weight_gradient_s12_kernel(
                 )
 
         def finals():
-            banks = [next_bank() for j in range(PIECE)]
-            for g in range(AHEAD):
-                for j in range(PIECE):
-                    final_passes(banks[j], j, 0, E, [g])
+            banks = []
             for j in range(TILES - 1):
-                if j >= PIECE:
+                if j % PIECE == 0:
+                    opened = range(j, j + OPEN[j // PIECE])
+                    banks.extend(next_bank() for k in opened)
+                    for g in range(AHEAD[j // PIECE]):
+                        for k in opened:
+                            final_passes(banks[k], k, 0, E, [g])
+                if j not in opened:
                     banks.append(next_bank())
-                final_passes(banks[j], j, 0, E, range(AHEAD if j < PIECE else 0, GROUPS))
+                final_passes(banks[j], j, 0, E, range(AHEAD[j // PIECE] if j in opened else 0, GROUPS))
                 empty(banks[j], j, 0, E, on_vector if j in OUT_ON_VECTOR else on_scalar)
                 if j >= PIECE or j % 2 == 1:
                     store(j if j >= PIECE else j - 1, j, 0, E, nc.sync)
@@ -395,26 +401,26 @@ def tile_router_weight_gradient_s12_kernel(
                 load_grad(3, 1)
                 load_prob(2)
                 load_prob(3)
+                order_codes(LAST, on_vector)
             else:
                 weigh(g - 1, POOL_FROM[g - 1], E, nc.gpsimd)
-            if g > 0:
-                weigh(g - 1, HALF, POOL_FROM[g - 1], nc.vector)
-                quantize_l(g - 1, 0, HALF, l_lower[g - 1])
-                quantize_l(g - 1, HALF, E, l_upper[g - 1])
+            if g == 1:
+                part_pair(g + 2, 1, SS[g + 1], 4, on_vector)
             if g == LAST:
                 break
+            if g > 0:
+                quantize_l(g - 1)
             turn_group(g + 1, by_pair)
             if g == 0:
-                order_codes(LAST, on_vector)
-                weigh(g, 0, P, nc.vector)
-            quantize_grad(g + 1, 0, 1)
-            weigh(g, P if g == 0 else 0, HALF if g == 0 else P, nc.vector)
-            quantize_grad(g + 1, 1, 2)
+                weigh(g, 0, POOL_FROM[g], nc.vector)
+            for h in range(PASSES):
+                quantize_grad(g + 1, h, h + 1)
             if g > 0:
-                weigh(g, P, HALF, nc.vector)
+                weigh(g, 0, POOL_FROM[g], nc.vector)
             x_tiles(R[g] - 1, on_scalar)
             if g + 2 < GROUPS:
                 part_pair(g + 2, 0, 0, 4, on_scalar)
+            if g == 0:
                 part_pair(g + 2, 1, SS[g + 1], 4, on_vector)
             quantize_x(GATE[g])
             if g + 2 < GROUPS:
@@ -422,9 +428,8 @@ def tile_router_weight_gradient_s12_kernel(
             x_tiles(1, on_vector if VB[g] else on_scalar)
         x_tiles(GROUPS * TILES - len(made), on_scalar)
         weigh(LAST, 0, E, nc.vector)
-        for n in QX[LAST]:
-            quantize_x(n)
-        quantize_l(LAST, 0, E, l_lower[LAST])
-        for n in QX[GROUPS]:
+        quantize_l(LAST - 1)
+        quantize_l(LAST)
+        for n in (1, 3, 5, 7):
             quantize_x(n)
         finals()

@@ -37,9 +37,9 @@ PIECES = (0, 1, 2, 4, 6, 3, 5, 7)
 GATE = (2, 4, 6)
 VB = (0, 0, 0)
 H0, H1 = 8, 3
-POOL_WALK = "p c i t"
+POOL_WALK = "p c t i"
 SS = (2, 1, 1)
-POOL_FROM = (288, 288, 288)
+POOL_FROM = (416, 416, 416)
 R = (5, 5, 5)
 AHEAD = (3, 2)
 OPEN = (4, 2)

@@ -36,13 +36,16 @@ POOL_STRETCH = (1, 1, 3)
 PIECES = (0, 1, 2, 4, 6, 3, 5, 7)
 GATE = (2, 4, 6)
 VB = (0, 0, 0)
-H0, H1 = 8, 3
+H0 = 8
+H1 = 3
 POOL_WALK = "p c t i"
-SS = (2, 1, 1)
-POOL_FROM = (416, 416, 416)
+SS = (2, 2, 2)
+POOL_FROM = (320, 320, 320)
 R = (5, 5, 5)
 AHEAD = (3, 2)
 OPEN = (4, 2)
+SX = (4, 4, 4)
+
 
 def tile_router_weight_gradient_s12_kernel(
     tc, a_words, a_scales, w_words, w_scales, grad, values, prob, balance, base, out
@@ -346,9 +349,8 @@ def tile_router_weight_gradient_s12_kernel(
         quantize(warm_codes[:], warm_plane[:], v_wide[1][:])
         make_identity(nc, ident[:], nomemset=True)
         load_a(0)
-        load_a_scales(0, QUADRANTS[:2])
+        load_a_scales(0, QUADRANTS)
         load_w(0)
-        load_a_scales(0, QUADRANTS[2:])
         load_w_scales(QUADRANTS)
         load_values(0)
         load_w(1)
@@ -394,11 +396,11 @@ def tile_router_weight_gradient_s12_kernel(
         for g in range(GROUPS):
             utilities(g)
             if g == 0:
-                load_grad(2, 0)
                 load_grad(2, 1)
+                load_grad(2, 0)
                 load_prob(1)
-                load_grad(3, 0)
                 load_grad(3, 1)
+                load_grad(3, 0)
                 load_prob(2)
                 load_prob(3)
                 order_codes(LAST, on_vector)
@@ -406,29 +408,25 @@ def tile_router_weight_gradient_s12_kernel(
                 weigh(g - 1, POOL_FROM[g - 1], E, nc.gpsimd)
             if g == 1:
                 part_pair(g + 2, 1, SS[g + 1], 4, on_vector)
-            if g == LAST:
-                break
             if g > 0:
                 quantize_l(g - 1)
+            if g == LAST:
+                break
             turn_group(g + 1, by_pair)
-            if g == 0:
-                weigh(g, 0, POOL_FROM[g], nc.vector)
-            for h in range(PASSES):
-                quantize_grad(g + 1, h, h + 1)
-            if g > 0:
-                weigh(g, 0, POOL_FROM[g], nc.vector)
-            x_tiles(R[g] - 1, on_scalar)
-            if g + 2 < GROUPS:
-                part_pair(g + 2, 0, 0, 4, on_scalar)
+            quantize_grad(g + 1, 0, 1)
             if g == 0:
                 part_pair(g + 2, 1, SS[g + 1], 4, on_vector)
+            quantize_grad(g + 1, 1, 2)
+            weigh(g, 0, POOL_FROM[g], nc.vector)
+            x_tiles(SX[g], on_scalar)
+            if g + 2 < GROUPS:
+                part_pair(g + 2, 0, 0, 4, on_scalar)
             quantize_x(GATE[g])
             if g + 2 < GROUPS:
                 part_pair(g + 2, 1, 0, SS[g + 1], on_scalar)
-            x_tiles(1, on_vector if VB[g] else on_scalar)
+            x_tiles(R[g] - SX[g], on_scalar)
         x_tiles(GROUPS * TILES - len(made), on_scalar)
         weigh(LAST, 0, E, nc.vector)
-        quantize_l(LAST - 1)
         quantize_l(LAST)
         for n in (1, 3, 5, 7):
             quantize_x(n)

@@ -40,7 +40,7 @@ H0 = 8
 H1 = 3
 POOL_WALK = "p c t i"
 SS = (2, 2, 2)
-POOL_FROM = (320, 320, 320)
+POOL_FROM = (336, 336, 336)
 R = (5, 5, 5)
 AHEAD = (3, 2)
 OPEN = (4, 2)
@@ -408,12 +408,12 @@ def tile_router_weight_gradient_s12_kernel(
                 weigh(g - 1, POOL_FROM[g - 1], E, nc.gpsimd)
             if g == 1:
                 part_pair(g + 2, 1, SS[g + 1], 4, on_vector)
-            if g > 0:
-                quantize_l(g - 1)
             if g == LAST:
                 break
             turn_group(g + 1, by_pair)
             quantize_grad(g + 1, 0, 1)
+            if g > 0:
+                quantize_l(g - 1)
             if g == 0:
                 part_pair(g + 2, 1, SS[g + 1], 4, on_vector)
             quantize_grad(g + 1, 1, 2)
@@ -426,8 +426,11 @@ def tile_router_weight_gradient_s12_kernel(
                 part_pair(g + 2, 1, 0, SS[g + 1], on_scalar)
             x_tiles(R[g] - SX[g], on_scalar)
         x_tiles(GROUPS * TILES - len(made), on_scalar)
-        weigh(LAST, 0, E, nc.vector)
-        quantize_l(LAST)
+        weigh(LAST, 0, HALF, nc.vector)
+        quantize_l(LAST - 1)
+        weigh(LAST, HALF, E, nc.vector)
+        quantize(l_codes[LAST][:, 0:HALF], l_planes[LAST][:, 0:HALF], l_wide[LAST][:, 0 : PACK * HALF])
+        quantize(l_codes[LAST][:, HALF:], l_planes[LAST][:, HALF:], l_wide[LAST][:, PACK * HALF :])
         for n in (1, 3, 5, 7):
             quantize_x(n)
         finals()

@@ -27,7 +27,7 @@ HALF = E // 2
 ALIGN = 64
 QUAD = 32
 TILES = D // P
-QUADRANTS = (0, 2, 1, 3)
+QUADRANTS = (0, 1, 2, 3)
 PIECE = 4
 WARM_N = 512
 WARM = 3
@@ -113,8 +113,8 @@ def tile_router_weight_gradient_s12_kernel(
 
         def load_scale_rows(dst, scales, lo, hi, quadrants):
             for q in quadrants:
-                src = scales.rearrange("h r n -> r h n")[4 * q : 4 * q + 4, :, lo:hi]
-                nc.sync.dma_start(out=dst[QUAD * q : QUAD * q + 4], in_=src.bitcast(I32))
+                src = scales.rearrange("h (q r) n -> r q h n", r=4)[q][:, :, lo:hi]
+                nc.sync.dma_start(out=dst[q:P:QUAD], in_=src.bitcast(I32))
 
         def load_a_scales(n, quadrants):
             load_scale_rows(a_staged[n], a_scales, GROUP * spans[n][0], GROUP * spans[n][1], quadrants)

@@ -35,12 +35,12 @@ OUT_ON_VECTOR = (5,)
 POOL_STRETCH = (1, 1, 3)
 PIECES = (0, 1, 2, 4, 6, 3, 5, 7)
 GATE = (2, 4, 6)
-VB = (0, 0, 0)
+VB = (1, 1, 0)
 H0 = 8
 H1 = 3
 POOL_WALK = "p c t i"
 SS = (2, 2, 2)
-POOL_FROM = (336, 336, 336)
+POOL_FROM = (272, 272, 320)
 R = (5, 5, 5)
 AHEAD = (3, 2)
 OPEN = (4, 2)
@@ -358,20 +358,19 @@ def tile_router_weight_gradient_s12_kernel(
         load_grad(0, 0)
         load_grad(0, 1)
         load_a(1)
-        load_base(0)
         load_values(1)
-        load_base(1)
         load_grad(1, 0)
+        load_base(0)
+        load_base(1)
+        load_grad(1, 1)
         load_base(2)
         load_base(3)
-        load_grad(1, 1)
         warm_up(WARM)
         order_codes(0, on_vector)
         order_scales(0, on_vector, I32)
         nc.vector.memset(a_staged[1][:], 0)
         load_a(2)
         load_a_scales(1, QUADRANTS)
-        load_prob(0)
         x_tiles(H0, on_scalar)
         interleave_values(0)
         quantize_values(0)
@@ -381,6 +380,9 @@ def tile_router_weight_gradient_s12_kernel(
         spread_balance()
         order_codes(1, on_vector)
         load_a(3)
+        load_grad(2, 1)
+        load_prob(0)
+        load_grad(2, 0)
         quantize_x(0)
         interleave_values(1)
         x_tiles(H1, on_scalar)
@@ -396,11 +398,10 @@ def tile_router_weight_gradient_s12_kernel(
         for g in range(GROUPS):
             utilities(g)
             if g == 0:
-                load_grad(2, 1)
-                load_grad(2, 0)
-                load_prob(1)
                 load_grad(3, 1)
+                load_prob(1, range(2))
                 load_grad(3, 0)
+                load_prob(1, range(2, PACK))
                 load_prob(2)
                 load_prob(3)
                 order_codes(LAST, on_vector)
@@ -424,7 +425,7 @@ def tile_router_weight_gradient_s12_kernel(
             quantize_x(GATE[g])
             if g + 2 < GROUPS:
                 part_pair(g + 2, 1, 0, SS[g + 1], on_scalar)
-            x_tiles(R[g] - SX[g], on_scalar)
+            x_tiles(R[g] - SX[g], on_vector if VB[g] else on_scalar)
         x_tiles(GROUPS * TILES - len(made), on_scalar)
         weigh(LAST, 0, HALF, nc.vector)
         quantize_l(LAST - 1)

@@ -30,7 +30,7 @@ TILES = D // P
 QUADRANTS = (0, 1, 2, 3)
 PIECE = 4
 WARM_N = 512
-WARM = 3
+WARM = 5
 OUT_ON_VECTOR = (5,)
 POOL_STRETCH = (1, 1, 3)
 PIECES = (0, 1, 2, 4, 6, 3, 5, 7)

from contextlib import ExitStack

import concourse.mybir as mybir
from concourse.masks import make_identity

T, F, D, E = 2048, 1024, 1024, 512
FLOPS = 2 * (T * F * D + T * D * E + T * D * E)

F32 = mybir.dt.float32
BF16 = mybir.dt.bfloat16
I32 = mybir.dt.int32
U32 = mybir.dt.uint32
U8 = mybir.dt.uint8
FP8X4 = mybir.dt.float8_e4m3fn_x4
FP4X4 = mybir.dt.float4_e2m1fn_x4
ALU = mybir.AluOpType

P = 128
PACK = 4
GROUP = P * PACK
GROUPS = T // GROUP
LAST = GROUPS - 1
PASSES = 2
BANK = 512
BANKS = 8
HALF = E // 2
ALIGN = 64
QUAD = 32
TILES = D // P
QUADRANTS = (0, 1, 2, 3)
PIECE = 4
WARM_N = 512
WARM = 5
OUT_ON_VECTOR = (5,)
POOL_STRETCH = (1, 1, 3)
PIECES = (0, 1, 2, 4, 6, 3, 5, 7)
GATE = (2, 4, 6)
VB = (1, 1, 0)
H0 = 8
H1 = 3
POOL_WALK = "p c t i"
SS = (2, 2, 2)
POOL_FROM = (272, 272, 320)
R = (5, 5, 5)
AHEAD = (3, 2)
OPEN = (4, 2)
SX = (4, 4, 4)


def tile_router_weight_gradient_s12_kernel(
    tc, a_words, a_scales, w_words, w_scales, grad, values, prob, balance, base, out
):
    nc = tc.nc
    with ExitStack() as ctx:
        sb = ctx.enter_context(tc.tile_pool(name="sb", bufs=1))
        psum = ctx.enter_context(tc.psum_pool(name="psum", bufs=1))
        ctx.enter_context(tc.manual_schedule())
        on_vector, on_scalar, on_gpsimd = nc.vector.tensor_copy, nc.scalar.copy, nc.gpsimd.tensor_copy

        def keep(name, shape, dtype):
            return sb.tile(shape, dtype, name=name, align_bytes=ALIGN)

        taken = []

        def next_bank():
            n = len(taken)
            taken.append(psum.tile([P, BANK], F32, name="bank%d" % n, tag="bank%d" % (n % BANKS)))
            return taken[n]

        ident = keep("ident", [P, P], F32)
        bal_col = keep("bal_col", [P, PACK], BF16)
        bal_row = keep("bal_row", [P, E], BF16)
        warm_codes = keep("warm_codes", [P, WARM_N], U32)
        warm_plane = keep("warm_plane", [P, WARM_N], U8)
        base_sb = keep("base_sb", [P, GROUPS, 16], BF16)

        a_raw = [keep("a_raw%d" % g, [P, PASSES, 256], I32) for g in range(2)] * 2
        a_codes = [keep("a_codes%d" % g, [P, PACK, PASSES, 2 * P], U8) for g in range(GROUPS)]
        spans = ((0, 2), (2, GROUPS))
        a_staged = [keep("a_staged%d" % lo, [P, PASSES, P * (hi - lo)], I32) for lo, hi in spans]
        a_planes = [keep("a_plane%d" % lo, [P, PACK, PASSES, hi - lo, P], U8) for lo, hi in spans]
        w_codes = [keep("w_codes%d" % n, [P, PASSES, D], U8) for n in range(2)]
        w_plane = keep("w_plane", [P, PASSES, D], U8)

        g_raw = [keep("g_raw%d" % g, [P, PACK * D], BF16) for g in range(LAST)]
        g_raw = g_raw[:2] + [g_raw[0], g_raw[2]]
        g_parted = [keep("g_parted%d" % n, [P, PASSES * 4 * P], F32) for n in range(3)]
        g_parted = [[g_parted[0], g_parted[1 + g % 2]] for g in range(GROUPS)]
        g_wide = [keep("g_wide%d" % g, [P, PASSES * GROUP * PACK], BF16) for g in range(2)] * 2
        g_codes = [keep("g_codes%d" % g, [P, PASSES * GROUP], U32) for g in range(2)] * 2
        g_planes = [keep("g_plane%d" % g, [P, PASSES * GROUP], U8) for g in range(2)] * 2
        v_raw = [keep("v_raw%d" % h, [P, PACK, E], BF16) for h in range(PASSES)]
        v_wide = [keep("v_wide%d" % h, [P, E * PACK], BF16) for h in range(PASSES)]
        v_codes = [keep("v_codes%d" % h, [P, E], U32) for h in range(PASSES)]
        v_planes = [keep("v_plane%d" % h, [P, E], U8) for h in range(PASSES)]
        p_sb = [keep("p_sb%d" % g, [P, PACK, E], BF16) for g in range(GROUPS)]
        shifted = [keep("shifted%d" % n, [P, E * PACK], F32) for n in range(2)] * 2
        l_codes = [keep("l_codes%d" % g, [P, E], U32) for g in range(GROUPS)]
        l_planes = [keep("l_plane%d" % g, [P, E], U8) for g in range(GROUPS)]
        front = {n: PACK * POOL_FROM[g] for g, n in enumerate(GATE)}
        x_room = [keep("x_wide%d" % n, [P, front.get(n, 0) + PIECE * BANK], BF16) for n in range(2 * GROUPS)]
        x_wide = [room[:, front.get(n, 0) :] for n, room in enumerate(x_room)]
        x_codes = [keep("x_codes%d" % n, [P, PIECE * P], U32) for n in range(2 * GROUPS)]
        x_planes = [keep("x_plane%d" % n, [P, PIECE * P], U8) for n in range(2 * GROUPS)]
        staged_out = keep("staged_out", [P, TILES * E], F32)
        l_wide = [x_room[n][:, 0 : PACK * E] for n in GATE] + [g_wide[0][:, 0 : PACK * E]]
        pool_stretch = g_raw[1][:].bitcast(F32)[:, D : D + 2 * P].rearrange("p (u w) -> p u w", u=2)


        def load_a(g):
            src = a_words.rearrange("h p n -> p h n")[:, :, 2 * GROUP * g : 2 * GROUP * (g + 1)]
            nc.sync.dma_start(out=a_raw[g][:], in_=src.bitcast(I32))

        def load_scale_rows(dst, scales, lo, hi, quadrants):
            for q in quadrants:
                src = scales.rearrange("h (q r) n -> r q h n", r=4)[q][:, :, lo:hi]
                nc.sync.dma_start(out=dst[q:P:QUAD], in_=src.bitcast(I32))

        def load_a_scales(n, quadrants):
            load_scale_rows(a_staged[n], a_scales, GROUP * spans[n][0], GROUP * spans[n][1], quadrants)

        def load_w_scales(quadrants):
            load_scale_rows(w_plane[:].bitcast(I32), w_scales, 0, D, quadrants)

        def load_w(n):
            src = w_words.rearrange("h p n -> p h n")[:, :, D * n : D * (n + 1)]
            nc.sync.dma_start(out=w_codes[n][:].bitcast(I32), in_=src.bitcast(I32))

        def load_grad(g, pair):
            rows = grad[GROUP * g : GROUP * (g + 1), :].rearrange("(m s) d -> m (s d)", s=PACK)
            cols = slice(2 * D * pair, 2 * D * (pair + 1))
            nc.sync.dma_start(out=g_raw[g][:, cols], in_=rows[:, cols])

        def load_values(h):
            rows = values[GROUP * h : GROUP * (h + 1), :].rearrange("(p t) e -> p t e", t=PACK)
            nc.sync.dma_start(out=v_raw[h][:], in_=rows)

        def load_prob(g, rows_s=range(PACK)):
            rows = prob[GROUP * g : GROUP * (g + 1), :].rearrange("(c t s) e -> s c t e", t=PACK, s=PACK)
            for s in rows_s:
                nc.sync.dma_start(out=p_sb[g][s:P:PACK, :, :], in_=rows[s])

        def load_base(s):
            rows = base.rearrange("(g c w) -> c g w", g=GROUPS, w=16)
            nc.sync.dma_start(out=base_sb[s:P:PACK, :, 0:13], in_=rows[:, :, s : s + 13])

        def load_balance():
            nc.sync.dma_start(out=bal_col[:], in_=balance.rearrange("(p j) -> p j", j=PACK))

        def order_codes(g, copy):
            copy(
                out=a_codes[g][:].bitcast(I32).rearrange("p t h (b i w) -> p (h b) t i w", i=2, w=2),
                in_=a_raw[g][:].rearrange("p h (b i t w) -> p (h b) t i w", i=2, t=PACK, w=2),
            )

        def order_scales(n, copy, word):
            copy(
                out=a_planes[n][:].bitcast(word).rearrange("p t h g (b i) -> p (h g b) t i", i=4),
                in_=a_staged[n][:].bitcast(word).rearrange("p h (x i t) -> p (h x) t i", i=4, t=PACK),
            )

        def quantize(dst, plane, src):
            nc.vector.quantize_mx(out=dst.bitcast(FP8X4), scales=plane, in_=src)

        def spread_balance():
            bank = next_bank()
            words = bal_col[:].bitcast(F32)
            for u in range(2):
                nc.tensor.transpose(bank[:, P * u : P * (u + 1)], words[:, u : u + 1].to_broadcast([P, P]), ident[:])
            nc.scalar.copy(
                out=bal_row[:].bitcast(F32).rearrange("p (n u) -> p n u", u=2),
                in_=bank[:, 0 : 2 * P].rearrange("p (u n) -> p n u", u=2),
            )

        made = []

        def x_tiles(count, copy):
            for b in range(len(made), len(made) + count):
                made.append(b)
                g, n = divmod(PIECES[b // PIECE], 2)
                jj = b % PIECE
                j = PIECE * n + jj
                plane = a_planes[g // 2][:, :, :, g % 2, :]
                bank = next_bank()
                for t in range(PACK):
                    for h in range(PASSES):
                        nc.tensor.matmul_mx(
                            out=bank[:, P * t : P * (t + 1)],
                            lhsT=a_codes[g][:, t, h, :].bitcast(FP4X4),
                            lhsT_scale=plane[:, t, h, :],
                            rhs=w_codes[n][:, h, 2 * P * jj : 2 * P * (jj + 1)].bitcast(FP4X4),
                            rhs_scale=w_plane[:, h, P * j : P * (j + 1)],
                            start=(h == 0),
                            stop=(h == PASSES - 1),
                        )
                words = x_wide[2 * g + n][:, BANK * jj : BANK * (jj + 1)].rearrange("p (d t) -> p d t", t=PACK)
                copy(out=words, in_=bank[:].rearrange("p (t d) -> p d t", t=PACK))

        def part(dst, src, copy):
            copy(out=dst.rearrange("p u (x i) -> p x u i", i=4), in_=src.rearrange("p (x i u) -> p x u i", i=4, u=2))

        def part_pair(g, pair, lo, hi, copy):
            if lo == hi:
                return
            src = g_raw[g][:].bitcast(F32)[:, D * pair + 2 * P * lo : D * pair + 2 * P * hi]
            part(g_parted[g][pair][:].rearrange("p (u w) -> p u w", u=2)[:, :, P * lo : P * hi], src, copy)

        def parted_stretch(g, pair, n):
            if (g, pair, n) == POOL_STRETCH:
                return pool_stretch
            return g_parted[g][pair][:].rearrange("p (u w) -> p u w", u=2)[:, :, P * n : P * (n + 1)]

        def part_on_gpsimd():
            g, pair, n = POOL_STRETCH
            first = D * pair + 2 * P * n
            part(pool_stretch, g_raw[g][:].bitcast(F32)[:, first : first + 2 * P], on_gpsimd)

        def turn_group(g, steps):
            banks = {}
            for h, pair in steps:
                banks[h, pair] = next_bank()
                for q in range(4):
                    couples = parted_stretch(g, pair, PASSES * (q // 2) + h)[:, q % 2]
                    nc.tensor.transpose(banks[h, pair][:, P * q : P * (q + 1)], couples, ident[:])
            dst = g_wide[g][:].bitcast(F32).rearrange("p (h t c w) -> p h t c w", h=PASSES, t=PACK, w=8)
            for h, pair in sorted(steps):
                nc.scalar.copy(
                    out=dst[:, h, :, :, 4 * pair : 4 * pair + 4],
                    in_=banks[h, pair][:].rearrange("p (q c t) -> p t c q", q=4, t=PACK),
                )

        def interleave_values(h):
            nc.vector.tensor_copy(
                out=v_wide[h][:].rearrange("p (c i t) -> p c t i", i=4, t=PACK),
                in_=v_raw[h][:].rearrange("p t (c i) -> p c t i", i=4),
            )

        def utilities(g):
            dst = shifted[g][:].rearrange("p (c t i) -> p c t i", t=PACK, i=4)
            banks = [next_bank() for t in range(PACK)]
            steps = [(t, h) for t in range(PACK) for h in range(PASSES)]
            for t, h in sorted(steps, key=lambda step: (step[0] // (PACK if g == 0 else 2), step[1])):
                tokens = slice(GROUP * h + P * t, GROUP * h + P * (t + 1))
                nc.tensor.matmul_mx(
                    out=banks[t][:],
                    lhsT=g_codes[g][:, tokens].bitcast(FP8X4),
                    lhsT_scale=g_planes[g][:, tokens],
                    rhs=v_codes[h][:].bitcast(FP8X4),
                    rhs_scale=v_planes[h][:],
                    start=(h == 0),
                    stop=(h == PASSES - 1),
                )
            for t in range(PACK):
                nc.vector.scalar_tensor_tensor(
                    out=dst[:, :, t, :],
                    in0=banks[t][:].rearrange("p (c i) -> p c i", i=4),
                    scalar=base_sb[:, g, 4 * t : 4 * t + 1],
                    in1=bal_row[:].rearrange("p (c i) -> p c i", i=4),
                    op0=ALU.subtract,
                    op1=ALU.add,
                )

        def weigh(g, lo, hi, engine):
            walk = "p c t i" if engine is nc.vector else POOL_WALK
            engine.tensor_tensor(
                out=l_wide[g][:, PACK * lo : PACK * hi].rearrange("p (c i t) -> " + walk, i=4, t=PACK),
                in0=shifted[g][:, PACK * lo : PACK * hi].rearrange("p (c t i) -> " + walk, t=PACK, i=4),
                in1=p_sb[g][:, :, lo:hi].rearrange("p t (c i) -> " + walk, i=4),
                op=ALU.mult,
            )

        def quantize_values(h):
            quantize(v_codes[h][:], v_planes[h][:], v_wide[h][:])

        def quantize_grad(g, lo, hi):
            quantize(
                g_codes[g][:, GROUP * lo : GROUP * hi],
                g_planes[g][:, GROUP * lo : GROUP * hi],
                g_wide[g][:, GROUP * PACK * lo : GROUP * PACK * hi],
            )

        def quantize_l(g):
            quantize(l_codes[g][:], l_planes[g][:], l_wide[g])

        def quantize_x(n):
            quantize(x_codes[n][:], x_planes[n][:], x_wide[n])

        def final_passes(bank, j, lo, hi, groups):
            for g in groups:
                n, jj = divmod(j, PIECE)
                cols = slice(P * jj, P * (jj + 1))
                nc.tensor.matmul_mx(
                    out=bank[:, 0 : hi - lo],
                    lhsT=x_codes[2 * g + n][:, cols].bitcast(FP8X4),
                    lhsT_scale=x_planes[2 * g + n][:, cols],
                    rhs=l_codes[g][:, lo:hi].bitcast(FP8X4),
                    rhs_scale=l_planes[g][:, lo:hi],
                    start=(g == 0),
                    stop=(g == LAST),
                )

        def empty(bank, j, lo, hi, copy):
            copy(out=staged_out[:, E * j + lo : E * j + hi], in_=bank[:, 0 : hi - lo])

        def store(first, last, lo, hi, queue):
            src = staged_out[:].rearrange("p (j e) -> p j e", e=E)[:, first : last + 1, lo:hi]
            queue.dma_start(out=out.rearrange("(j p) e -> p j e", p=P)[:, first : last + 1, lo:hi], in_=src)

        def warm_up(count):
            bank = next_bank()
            for n in range(count):
                nc.tensor.matmul_mx(
                    out=bank[:, 0:WARM_N],
                    lhsT=warm_codes[:, 0:P].bitcast(FP8X4),
                    lhsT_scale=warm_plane[:, 0:P],
                    rhs=warm_codes[:].bitcast(FP8X4),
                    rhs_scale=warm_plane[:],
                    start=(n == 0),
                    stop=(n == count - 1),
                )

        def finals():
            banks = []
            for j in range(TILES - 1):
                if j % PIECE == 0:
                    opened = range(j, j + OPEN[j // PIECE])
                    banks.extend(next_bank() for k in opened)
                    for g in range(AHEAD[j // PIECE]):
                        for k in opened:
                            final_passes(banks[k], k, 0, E, [g])
                if j not in opened:
                    banks.append(next_bank())
                final_passes(banks[j], j, 0, E, range(AHEAD[j // PIECE] if j in opened else 0, GROUPS))
                empty(banks[j], j, 0, E, on_vector if j in OUT_ON_VECTOR else on_scalar)
                if j >= PIECE or j % 2 == 1:
                    store(j if j >= PIECE else j - 1, j, 0, E, nc.sync)
            pieces = ((0, HALF, on_vector, nc.sync), (HALF, HALF + P, on_vector, nc.sync), (HALF + P, E, on_scalar, nc.scalar))
            for lo, hi, copy, queue in pieces:
                bank = next_bank()
                final_passes(bank, TILES - 1, lo, hi, range(GROUPS))
                empty(bank, TILES - 1, lo, hi, copy)
                store(TILES - 1, TILES - 1, lo, hi, queue)

        by_pair = [(h, pair) for pair in range(2) for h in range(PASSES)]
        nc.vector.memset(a_staged[0][:], 0)
        nc.vector.memset(w_plane[:].bitcast(I32), 0)
        nc.vector.memset(v_wide[1][:].bitcast(I32), 0)
        nc.vector.memset(ident[:], 0.0)
        quantize(warm_codes[:], warm_plane[:], v_wide[1][:])
        make_identity(nc, ident[:], nomemset=True)
        load_a(0)
        load_a_scales(0, QUADRANTS)
        load_w(0)
        load_w_scales(QUADRANTS)
        load_values(0)
        load_w(1)
        load_balance()
        load_grad(0, 0)
        load_grad(0, 1)
        load_a(1)
        load_values(1)
        load_grad(1, 0)
        load_base(0)
        load_base(1)
        load_grad(1, 1)
        load_base(2)
        load_base(3)
        warm_up(WARM)
        order_codes(0, on_vector)
        order_scales(0, on_vector, I32)
        nc.vector.memset(a_staged[1][:], 0)
        load_a(2)
        load_a_scales(1, QUADRANTS)
        x_tiles(H0, on_scalar)
        interleave_values(0)
        quantize_values(0)
        part_pair(0, 0, 0, 4, on_vector)
        part_pair(0, 1, 0, 4, on_vector)
        turn_group(0, by_pair)
        spread_balance()
        order_codes(1, on_vector)
        load_a(3)
        load_grad(2, 1)
        load_prob(0)
        load_grad(2, 0)
        quantize_x(0)
        interleave_values(1)
        x_tiles(H1, on_scalar)
        quantize_grad(0, 0, 1)
        quantize_values(1)
        quantize_grad(0, 1, 2)
        part_pair(1, 0, 0, 4, on_vector)
        part_pair(1, 1, 0, 1, on_vector)
        part_pair(1, 1, 1, 3, on_scalar)
        part_on_gpsimd()
        order_codes(2, on_gpsimd)
        order_scales(1, on_scalar, U32)
        for g in range(GROUPS):
            utilities(g)
            if g == 0:
                load_grad(3, 1)
                load_prob(1, range(2))
                load_grad(3, 0)
                load_prob(1, range(2, PACK))
                load_prob(2)
                load_prob(3)
                order_codes(LAST, on_vector)
            else:
                weigh(g - 1, POOL_FROM[g - 1], E, nc.gpsimd)
            if g == 1:
                part_pair(g + 2, 1, SS[g + 1], 4, on_vector)
            if g == LAST:
                break
            turn_group(g + 1, by_pair)
            quantize_grad(g + 1, 0, 1)
            if g > 0:
                quantize_l(g - 1)
            if g == 0:
                part_pair(g + 2, 1, SS[g + 1], 4, on_vector)
            quantize_grad(g + 1, 1, 2)
            weigh(g, 0, POOL_FROM[g], nc.vector)
            x_tiles(SX[g], on_scalar)
            if g + 2 < GROUPS:
                part_pair(g + 2, 0, 0, 4, on_scalar)
            quantize_x(GATE[g])
            if g + 2 < GROUPS:
                part_pair(g + 2, 1, 0, SS[g + 1], on_scalar)
            x_tiles(R[g] - SX[g], on_vector if VB[g] else on_scalar)
        x_tiles(GROUPS * TILES - len(made), on_scalar)
        weigh(LAST, 0, HALF, nc.vector)
        quantize_l(LAST - 1)
        weigh(LAST, HALF, E, nc.vector)
        quantize(l_codes[LAST][:, 0:HALF], l_planes[LAST][:, 0:HALF], l_wide[LAST][:, 0 : PACK * HALF])
        quantize(l_codes[LAST][:, HALF:], l_planes[LAST][:, HALF:], l_wide[LAST][:, PACK * HALF :])
        for n in (1, 3, 5, 7):
            quantize_x(n)
        finals()
